import numpy as np, ml_dtypes
CORES = [16,17,18,19,32,33,34,35]
N = 8
BF = ml_dtypes.bfloat16
def gentries(a):
    return np.ascontiguousarray(a.reshape(8, 16, -1).transpose(0, 2, 1)).reshape(8, -1)
def gtable(e):
    e = np.asarray(e); return np.ascontiguousarray(e.reshape(8, -1, 16).transpose(0, 2, 1)).reshape(128, -1).astype(np.int32)
B, L, S, T, TH = 2560, 128, 64, 8, 1235
W = B + 2 * S * T
def pack(kb, ch, q, hv):
    return {"kb": np.ascontiguousarray(kb.reshape(N, 128, B)).astype(np.float32).astype(BF), "ch": np.ascontiguousarray(ch.reshape(N, 128, B)).astype(np.int32),
            "qs": np.ascontiguousarray(q.reshape(N, 128, L)).astype(np.float32).astype(BF), "hv": np.stack([gtable(a.reshape(8, -1)) for a in hv])}
def nodes(rng, pop, n):
    often = np.take_along_axis(pop, rng.integers(0, pop.shape[2], (N, 8, n)), 2)
    return np.where(rng.random((N, 8, n)) < 0.5, often, rng.integers(1, B, (N, 8, n)))
def abroad(h):
    return np.stack([np.roll(h[:, :, t], -t, axis=0) for t in range(T)], axis=2)
def setup_inputs(rng):
    pop = rng.integers(1, B, (N, 8, B // 4)); kb = rng.integers(0, 256, (N, 8, 16, B))
    ch = nodes(rng, pop, 16 * B).reshape(N, 8, 16, B)
    none = rng.choice(np.array([0.03, 0.1, 0.2, 0.3]), (N, 8, 1, 1)); none = np.where(rng.random((N, 8, 1, B)) < 0.02, 1.0, none)
    ch = np.where(rng.random(ch.shape) < none, 0, ch)
    q = rng.integers(0, 256, (N, 8, 16, L)); edge = rng.integers(0, 41, q.shape); edge = np.where(rng.random(q.shape) < 0.5, edge, 255 - edge)
    q = np.where(rng.random((N, 8, 1, L)) < 0.125, edge, q)
    return pack(kb, ch, q, abroad(nodes(rng, pop, T * L).reshape(N, 8, T, L)))
def setup_inputs_spread(rng):
    kb = (np.exp2(8 * rng.random((N, 8, 1, B))) * rng.random((N, 8, 16, B))).astype(np.int64)
    q = (np.exp2(8 * rng.random((N, 8, 1, L))) * rng.random((N, 8, 16, L))).astype(np.int64)
    ch = 1 + ((B - 1) * rng.random((N, 8, 16, B)) ** 2).astype(np.int64)
    ch = np.where(rng.random(ch.shape) < rng.random((N, 8, 1, B)) ** 2, 0, ch)
    hv = 1 + ((B - 1) * rng.random((N, 8, T, L)) ** 2).astype(np.int64)
    return pack(np.minimum(kb, 255), np.minimum(ch, B - 1), np.minimum(q, 255), np.minimum(hv, B - 1))
def setup_inputs_ends(rng):
    d = rng.choice(np.array([0.08, 0.15, 0.5, 0.9]), (N, 8, 1, B), p=np.array([0.4, 0.3, 0.1, 0.2])); kb = 255 * (rng.random((N, 8, 16, B)) < d).astype(np.int64)
    d = rng.choice(np.array([0.08, 0.2, 0.5, 0.9]), (N, 8, 1, L), p=np.array([0.4, 0.3, 0.15, 0.15])); q = 255 * (rng.random((N, 8, 16, L)) < d).astype(np.int64)
    u = rng.random((N, 8, 16, B)); ch = np.where(u < 0.42, 0, np.where(u < 0.64, B - 1, rng.integers(2, B - 1, u.shape)))
    end = rng.random((N, 8, T, L)) < np.where(np.arange(L) < S, 0.35, 0.95)
    hv = np.where(end, np.where(rng.random(end.shape) < 0.5, 1, B - 1), rng.integers(2, B - 1, end.shape))
    kb[..., 1] = 255; kb[..., B - 1] = 255; kb[..., 2] = 0; kb[..., B - 2] = 0; row = np.arange(16)
    ch[..., 1] = np.where(row == 0, 0, np.where(row % 2 == 1, B - 1, 1)); ch[..., 2] = np.where(row % 2 == 1, B - 2, 2)
    q[..., 0] = 0; q[..., L - 1] = 255; q[..., L - 2] = 0; q[..., L - 3] = 0; q[..., L - 4] = 255
    hv[:, :, 0, 0] = 1; hv[:, :, 0, L - 2:] = 1; hv[:, :, 0, L - 4:L - 2] = 2
    return pack(kb, ch, q, hv)
def setup_inputs_corners(rng):
    kb = rng.integers(0, 61, (N, 8, 16, B)); q = rng.integers(0, 61, (N, 8, 16, L)); ch = np.zeros((N, 8, 16, B), np.int64)
    hv = rng.integers(1, B, (N, 8, T, L)); hv[..., 0] = 1; hv[..., L - 1] = B - 1; v = np.arange(B)
    for r in range(N):
        for g in range(8):
            k = (g + r) % 8; c = ch[r, g]; some = rng.integers(1, B, (16, B))
            if k == 0: c[:] = v
            elif k == 2: c[15] = some[15]
            elif k == 3: c[14] = some[14]
            elif k == 4: c[0] = some[0]
            elif k == 5: c[:] = np.where(some % 2 == 0, 1, B - 1)
            elif k == 6: c[rng.integers(0, 16, B), v] = np.where(v < B - 1, v + 1, 1)
            elif k == 7:
                c[:] = some; kb[r, g] = rng.integers(0, 256, (16, B)); q[r, g] = rng.integers(0, 256, (16, L))
    return pack(kb, ch, q, hv)
def setup_inputs_crowd(rng):
    kb = rng.integers(200, 256, (N, 8, 16, B)); q = rng.integers(0, 61, (N, 8, 16, L)); hv = rng.integers(1, B, (N, 8, T, L))
    ch = np.where(rng.random((N, 8, 16, B)) < 0.5, 0, rng.integers(1, B, (N, 8, 16, B)))
    plan = np.zeros((N, 8, 4 * S + 3), np.int64); cuts = np.zeros(N, np.int64); i = np.arange(S)
    for r in range(N):
        for g in range(8):
            o = rng.permutation(np.arange(1, B))
            for place, node in ((2 * S - 1, B - 1), (3 * S - 2, 1)):
                w = int(np.argmax(o == node)); o[w] = o[place]; o[place] = node
            ring = o[:4 * S]; z, y, w = [int(a) for a in o[4 * S:4 * S + 3]]; far = o[4 * S + 3:]; plan[r, g] = o[:4 * S + 3]
            kg = kb[r, g]; cg = ch[r, g]
            kg[:, ring] = rng.integers(0, 61, (16, 4 * S)); kg[:, y] = 5
            cg[:, ring] = np.where(rng.random((16, 4 * S)) < 0.5, 0, far[rng.integers(0, far.size, (16, 4 * S))])
            row = rng.integers(0, 15, 4 * S); row[S] = 0; row[S + 1] = 14; row[2 * S] = 14; row[2 * S + 1] = 0
            cg[row, ring] = np.roll(ring, -S)
            cg[:, [z, y, w]] = 0; cg[int(rng.integers(0, 16)), z] = y
            m = 0 if r == 0 else (1 if g == 7 else 0) if r == 1 else (g + r) % 8
            chain = i + 0; stage = 0 * i; n = S
            if m == 1: chain[1] = 0; n = S - 2
            elif m == 2: chain = 0 * i + S - 1; n = 0
            elif m == 3: chain = 0 * i; chain[S - 1] = S - 1; n = 0
            elif m == 4: chain = 0 * i; chain[S - 2] = S - 2; chain[S - 1] = S - 1; n = 2
            elif m == 5: chain = i % 4; n = 4
            elif m == 6: chain = i - i % 2; stage = 2 * (i % 2)
            elif m == 7: chain = i - i % 2; stage = 3 * (i % 2); n = 0
            hv[r, g, 0, :S] = ring[stage * S + chain]; hv[r, g, 0, S:] = ring[rng.integers(0, 4 * S, L - S)]
            cuts[r] += n
    for t in range(1, T):
        near = np.take_along_axis(np.roll(plan, -t, axis=0), rng.integers(0, 4 * S, (N, 8, L)), 2)
        hv[:, :, t] = np.where(rng.random((N, 8, L)) < 0.75, near, hv[:, :, t])
    then = np.roll(plan, -1, axis=0)
    for e in range(3):
        hv[:, :, 0, L - 6 + e] = plan[:, :, 4 * S]; hv[:, :, 0, L - 3 + e] = plan[:, :, 4 * S + 2]; hv[:, :, 1, L - 3 + e] = then[:, :, 4 * S]
        for r in range(N):
            for lane, s in ((L - 6 + e, TH + e - 1), (L - 3 + e, TH + (int(cuts[(r + 1) % N]) & 63) + e - 1)):
                q[r, :, :, lane] = 5 + s // 16 + (np.arange(16) < s % 16).astype(np.int64)
    return pack(kb, ch, q, hv)
def check_inputs(d):
    bad = []
    for k, lo, hi in (("kb", 0, 255), ("ch", 0, B - 1), ("qs", 0, 255), ("hv", 1, B - 1)):
        v = np.asarray(d[k]).astype(np.float32)
        if not np.all((v >= lo) & (v <= hi)): bad.append("range of " + k)
        elif np.any(v != np.floor(v)): bad.append("whole numbers in " + k)
    return bad
def reference(kb, ch, qs, hv):
    c = np.zeros((N, 8, 16, W), np.int64); c[..., :B] = ch.reshape(N, 8, 16, B)
    K = np.zeros((N, 8, 16, W), np.int32); K[..., :B] = kb.astype(np.float32).astype(np.int32).reshape(N, 8, 16, B)
    q = qs.astype(np.float32).astype(np.int32).reshape(N, 8, 16, L); p = np.zeros((N, 8, 16, L), np.int32)
    h = np.stack([gentries(a) for a in hv]).astype(np.int64).reshape(N, 8, T, L)
    A = [0] * N; row = np.arange(16)[None, :]; lower = np.tril(np.ones((S, S), bool), -1); twin = np.arange(S) ^ 1
    for t in range(T):
        for x in range(N):
            o = (x - t) % N; C = c[x]; Kx = K[x]; Q = q[o][:, :, None, :]; P = p[o]; v = h[o, :, t]
            never = np.ones((8, L), bool); at = [v]; by = []
            for step in range(3):
                kids = np.take_along_axis(C, v[:, None, :], 2)
                key = np.take_along_axis(Kx, kids.reshape(8, 1, 16 * L), 2).reshape(8, 16, 16, L)
                y = np.abs(P[:, :, None, :] - key)
                s = np.where(kids == 0, 2 ** 20, np.add.reduce(np.abs(y - Q), axis=1))
                k = np.argmin(s, axis=1)
                go = np.take_along_axis(s, k[:, None, :], 1)[:, 0] <= TH + A[x]
                v = np.where(go, np.take_along_axis(kids, k[:, None, :], 1)[:, 0], v)
                P = np.where(go[:, None, :], np.take_along_axis(y, k[:, None, None, :], 2)[:, :, 0], P)
                never = never & go; at.append(v); by.append(k)
            p[o] = P
            a, b, j, k = at[1][:, :S], at[2][:, :S], by[1][:, :S], by[2][:, :S]
            can = never[:, :S] & (a != b) & (j < 15)
            two = np.stack([a, b], axis=-1)
            meet = np.any(two[:, :, None, :, None] == two[:, None, :, None, :], axis=(3, 4))
            stand = can & ~np.any(meet & lower & can[:, None, :], axis=2)
            g, i = np.nonzero(stand & stand[:, twin])
            a, b, j, k = a[g, i], b[g, i], j[g, i], k[g, i]; every = np.arange(len(g))
            m = B + 2 * S * t + 2 * i; n = m + 1; other = B + 2 * S * t + 2 * (i ^ 1)
            ra = C[g, :, a]; rb = C[g, :, b]
            ua = row > j[:, None]; ub = row > k[:, None]
            rm = np.where(ua, ra, 0); rm[every, j] = n
            na = np.where(ua, 0, ra); na[every, j + 1] = other
            C[g, :, a] = na; C[g, :, b] = np.where(ub, 0, rb); C[g, :, m] = rm; C[g, :, n] = np.where(ub, rb, 0)
            if t < T - 1:
                Kx[g, :, m] = Kx[g, :, a]; Kx[g, :, n] = Kx[g, :, b]
            A[x] = len(g) & 63
    return {"yc": c.reshape(N, 128, W).astype(np.float32), "yp": p.reshape(N, 128, L).astype(np.float32).astype(BF)}

@@ -1,0 +1,448 @@
+from concourse.mybir import dt, AluOpType, AxisListType, ActivationFunctionType
+
+OP = AluOpType
+AF = ActivationFunctionType
+N, NB, NV = 8, 2560, 8
+NW = NB + 128 * NV
+FAR, BIG, TH = 1024.0, 2048.0, 1235.5
+SIZES = (512, 512)
+LOADS = 4
+F, H, I, U = "float32", "bfloat16", "int32", "uint16"
+SCRATCH = {}
+for _t, _n, _names in (
+        (I, NB, "chi"), (F, NW + 128, "C"), (H, NW, "Ks Kp"), (H, 1024, "QS PO exn alt emat kga kgb"), (U, 512, "HS"), (H, 1152, "PS"),
+        (I, 64, "hv32 repi"), (H, 128, "eye bo okh bad seg4 pta pca ptb pcb"), (H, 8, "bo2 bo1"), (H, 408, "wq"),
+        (H, 136, "jc uj nea neb"), (F, 136, "m0 pj j4k gi17 d0t fa w2a fb w2b"), (F, 512, "di mt nn"), (H, 512, "dib wt wtf"),
+        (H, 64, "n64k n64 oneh okl dda ddb"), (F, 64, "ones pow4 quart zero lo jr kr ua oj oj1 ub au an"), (I, 12, "pi"),
+        (F, 128, "gi thi cm nbr val mn"), (F, 32, "pos8 dg dp cols fl ds dsj dla dlb"), (I, 16, "coli"), (U, 64, "rep cta ctb"),
+        (F, NW, "iot"), (F, 8, "dump0 dump8 nm nms nmo nmc ofb8 tl"), (F, 4, "ljf ca cb cc m4"), (U, 4, "ju ku"), (U, 8, "tlu"),
+        (F, 1, "cnt tc"), (I, 2, "zi"), (F, 192, "cfa cfb"), (H, 4096, "yqa yqb"), (H, 2048, "zoa zob"), (U, 12, "la lb")):
+    for _b in _names.split(): SCRATCH[_b] = ("sbuf", [128, _n], _t)
+for _b in "pd0a pd1a sca mia pd0b pd1b scb mib".split(): SCRATCH[_b] = ("psum", [128, 512], F)
+PSUM = {k for k, v in SCRATCH.items() if v[0] == "psum"}
+DMAS = ["ld%d" % i for i in range(LOADS)] + "ldk ldp ldq ldh st0 st1 st2 st3 stp".split()
+SEMAPHORES = ("v s pe gp snd".split() + DMAS + ["a%s%d" % (k, t) for k in "qh" for t in range(1, 8)]
+              + ["a%s%d" % (h, t) for h in "ab" for t in range(1, 9)])
+CY, PCY, LAT = 0.00083, 0.00042, 0.11
+
+
+def ap(name, c0, c1, step=1, p=128, ind=None):
+    return (name, c0, c1, step, p, ind)
+
+
+def toks(a):
+    return [(a[0], a[1], a[2])] + (toks(a[5]) if a[5] else [])
+
+
+def res(T, a):
+    v = T[a[0]][0:a[4], a[1]:a[2]] if a[3] == 1 else T[a[0]][0:a[4], a[1]:a[2]:a[3]]
+    return v.indirect(res(T, a[5])) if a[5] else v
+
+
+def ln(a):
+    return 16 * (a[5][2] - a[5][1]) if a[5] else -(-(a[2] - a[1]) // a[3])
+
+
+def two(*aps):
+    return all(SCRATCH[a[0]][2] in (H, U) for a in aps)
+
+
+def build():
+    ops = []; PT = {}
+
+    def add(eng, emit, rd, wr, cost, n=1, done=None, after=(), lag=0.0):
+        o = {"eng": eng, "emit": emit, "rd": [t for a in rd for t in toks(a)], "wr": [toks(a)[0] for a in wr], "cost": cost,
+             "n": n, "done": done, "after": list(after), "lag": lag, "i": len(ops)}
+        for a in wr: o["rd"] += toks(a)[1:]
+        ops.append(o)
+        return o["i"]
+
+    def vc(out, ins, per=1.0):
+        n = ln(out)
+        if out[5]: return 0.06 + n * 3.8 * CY
+        if any(a[5] for a in ins): return 0.06 + n * 1.5 * CY
+        return 0.02 + max(64, n * per) * CY
+
+    def tt(out, a, b, op):
+        per = 1 if a[0] in PSUM or b[0] in PSUM else 2
+        return add("V", lambda g, T: g.vector.tensor_tensor(res(T, out), res(T, a), res(T, b), op), (a, b), (out,), vc(out, (a,), per))
+
+    def ts(out, a, s1, s2, o1, o2=None):
+        sc = lambda T, s: res(T, s) if isinstance(s, tuple) else s
+        def emit(g, T):
+            if o2 is None: return g.vector.tensor_scalar(res(T, out), res(T, a), sc(T, s1), None, o1)
+            return g.vector.tensor_scalar(res(T, out), res(T, a), sc(T, s1), sc(T, s2), o1, o2)
+        return add("V", emit, [a] + [s for s in (s1, s2) if isinstance(s, tuple)], (out,), vc(out, (), 0.5 if two(out, a) else 1))
+
+    def cp(out, a):
+        return add("V", lambda g, T: g.vector.tensor_copy(res(T, out), res(T, a)), (a,), (out,), vc(out, (a,)))
+
+    def scan(out, d0, d1, o1, o2, init=0.0):
+        return add("V", lambda g, T: g.vector.tensor_tensor_scan(res(T, out), res(T, d0), res(T, d1), init, o1, o2), (d0, d1), (out,), vc(out, (), 0.5 if two(out, d0, d1) else 1))
+
+    def ms(out, x):
+        return add("V", lambda g, T: g.vector.memset(res(T, out), x), (), (out,), vc(out, ()))
+
+    def act(out, a, func, scale=1.0, after=()):
+        return add("S", lambda g, T: g.scalar.activation(res(T, out), res(T, a), func, scale=scale), (a,), (out,),
+                   0.08 + ln(out) * (1.5 if a[5] else 1.0) * CY, after=after)
+
+    def mm(ml, f32=False, after=()):
+        def emit(g, T):
+            return [g.tensor.matmul(res(T, o), res(T, l), res(T, r), st, sp) for (o, l, r, st, sp) in ml]
+        c = sum(max(min(64, ln(m[1])), ln(m[2])) for m in ml) * (4 if f32 else 1) * PCY + 0.05
+        return add("P", emit, [m[k] for m in ml for k in (1, 2)], [m[0] for m in ml], c, n=len(ml), after=after)
+
+    def iota(out, pat, base, cmul):
+        def emit(g, T):
+            if SCRATCH[out[0]][2] == I: return g.iota(res(T, out), pat, base, cmul)
+            return g.iota(res(T, out), pat, base, cmul, allow_small_or_imprecise_dtypes=True)
+        return add("G", emit, (), (out,), 0.15 + 2 * ln(out) * CY)
+
+    def aff(a, pat, base):
+        return add("G", lambda g, T: g.affine_select(res(T, a), res(T, a), pat, OP.is_equal, 0.0, base, 1), (a,), (a,), 0.2 + 2 * ln(a) * CY)
+
+    def dma(out, a, sem, lag):
+        add("Y", lambda g, T: g.sync.dma_start(res(T, out), res(T, a)), [x for x in (a,) if x[0] in SCRATCH],
+            [x for x in (out,) if x[0] in SCRATCH], 0.1, done=(sem, 16), lag=lag)
+
+    def send(out, a, sem):
+        def emit(g, T, core, topo):
+            dst = T.cores[(T.rank_of(core) + 1) % N]
+            rid, pid, _ = topo.addr(dst)
+            g.remote_dma(res(T, out), res(T, a), T.sem[sem], T.sem["snd"], pid, rid, sum(1 << x for x in topo.engines(core, dst)[:8]))
+        return add("G", emit, (a,), (), 0.8, n=0, done=("snd", 8))
+
+    def recv(out, sem, sender):
+        return add("R", None, (), (out,), 0.0, n=0, done=(sem, 8), after=[sender], lag=2.5)
+
+    W4 = NB // LOADS
+    dma(ap("hv32", 0, 64), ap("hv", 0, 64), "ldh", 2.2)
+    for i in range(LOADS): dma(ap("chi", i * W4, (i + 1) * W4), ap("ch", i * W4, (i + 1) * W4), "ld%d" % i, 3.0 + 0.8 * i)
+    dma(ap("QS", 0, 128), ap("qs", 0, 128), "ldq", 3)
+    dma(ap("Ks", 0, NB), ap("kb", 0, NB), "ldk", 6.5)
+    dma(ap("Kp", 0, NB), ap("kb", 0, NB), "ldp", 7.5)
+    col = lambda k: ap("cols", k, k + 1)
+    ci = lambda k: ap("coli", k, k + 1)
+    a64 = lambda n, c0=0, c1=136, st=1: ap(n, c0, c1, st, 64)
+    X, GC, RH, OFG, OFP, X1 = [col(k) for k in range(6)]
+    iota(ci(0), [[0, 1]], 0, 1)
+    iota(ap("gi", 0, 128), [[1, 8], [0, 16]], 0, 0)
+    ms(ap("eye", 0, 128), 1.0)
+    aff(ap("eye", 0, 128), [[-1, 128]], 0)
+    ms(ap("pj", 0, 136), 1.0)
+    aff(ap("pj", 0, 136), [[-16, 8], [1, 17]], -15)
+    ms(ap("pj", 16, 136, 17), 0.0)
+    ms(a64("exn", 0, 1024), -1.0)
+    aff(a64("exn", 0, 1024), [[-1, 64], [0, 16]], 0)
+    iota(ap("repi", 0, 64), [[1, 64]], 0, 0)
+    cp(ap("rep", 0, 64), ap("repi", 0, 64))
+    iota(ap("gi17", 0, 136), [[1, 8], [0, 17]], 0, 0)
+    ms(a64("di", 0, 512), 1.0)
+    aff(a64("di", 0, 512), [[-16, 4], [0, 8], [-1, 16]], 0)
+    iota(ap("pos8", 0, 32), [[0, 4], [1, 8]], 0, 0)
+    iota(ap("jc", 0, 136), [[0, 8], [-1, 17]], 15, 0)
+    ms(ap("jc", 16, 136, 17), 0.0)
+    ms(ap("ones", 0, 64), 1.0); ms(ap("oneh", 0, 64), 1.0)
+    iota(ap("j4k", 0, 136), [[0, 8], [-4096, 17]], 61440, 0)
+    ms(ap("j4k", 16, 136, 17), 0.0)
+    iota(ap("dump0", 0, 8), [[16, 8]], NW, 0)
+    iota(ap("iot", 0, NW), [[1, NW]], 1, 0)
+    iota(ap("mt", 0, 512), [[128, 8], [4, 32], [-2, 2]], NB + 2, 0)
+    iota(ap("nn", 0, 512), [[128, 8], [2, 64]], NB + 1, 0)
+    ts(ci(1), ci(0), 15, None, OP.bitwise_and)
+    ts(ci(2), ci(0), 4, None, OP.logical_shift_right)
+    ts(ci(3), ci(1), 1, None, OP.logical_shift_right)
+    cp(X, ci(1)); cp(GC, ci(2)); cp(RH, ci(3))
+    ts(ap("bo", 0, 128), ap("gi", 0, 128), GC, None, OP.is_equal)
+    ts(ap("bo1", 0, 8), ap("gi", 0, 128, 16), GC, None, OP.is_equal)
+    ts(ap("bo2", 0, 8), ap("gi", 0, 128, 16), GC, -2.0, OP.is_equal, OP.mult)
+    ts(ap("wq", 0, 136), ap("gi17", 0, 136), GC, None, OP.is_equal)
+    ms(ap("wq", 16, 136, 17), 0.0); ms(ap("wq", 136, 408), 0.0)
+    ts(a64("n64k", 0, 64), a64("eye", 0, 64), -65536.0, None, OP.mult)
+    ts(a64("n64", 0, 64), a64("eye", 0, 64), -64.0, None, OP.mult)
+    ms(a64("m0"), 0.0)
+    ms(a64("m0", 0, 136, 17), 1.0)
+    ms(ap("alt", 0, 1024, 2), BIG)
+    ms(ap("alt", 1, 1024, 2), 0.0)
+    ts(ap("dg", 0, 32), ap("pos8", 0, 32), GC, 1065536.0, OP.is_gt, OP.mult)
+    ts(ap("dg", 0, 32), ap("dg", 0, 32), -1000000.0, None, OP.add)
+    ts(OFG, GC, -65536.0, 458752.0, OP.mult, OP.add)
+    ts(a64("d0t"), a64("m0"), TH, None, OP.mult)
+    ms(ap("PS", 0, 128), 0.0)
+    ms(ap("C", NB, NW + 128), 0.0)
+    cp(a64("dib", 0, 512), a64("di", 0, 512))
+    ts(ap("dp", 0, 32), ap("pos8", 0, 32), RH, 1010.0, OP.is_gt, OP.mult)
+    ts(ap("dp", 0, 32), ap("dp", 0, 32), -1000.0, None, OP.add)
+    ts(OFP, RH, -10.0, 70.0, OP.mult, OP.add)
+    ms(ap("ofb8", 0, 8), 0.0); ts(ap("ofb8", 0, 8), ap("ofb8", 0, 8), OFP, None, OP.add)
+    ms(ap("seg4", 0, 128), 1.0); ms(ap("seg4", 0, 128, 4), 0.0)
+    ts(X1, X, 1.0, None, OP.add)
+    ts(ap("dump8", 0, 8), ap("dump0", 0, 8), X, 2.0 ** -13, OP.add, OP.mult)
+    ms(ap("cm", 0, 128), 0.125)
+    ms(ap("quart", 0, 64), 0.25); ms(ap("zero", 0, 64), 0.0)
+    scan(ap("pow4", 0, 64), ap("quart", 0, 64), ap("zero", 0, 64), OP.mult, OP.add, float(4.0 ** 32))
+    ts(ap("thi", 0, 128, 2), ap("pow4", 0, 64), 2.0, None, OP.mult)
+    ts(ap("thi", 1, 128, 2), ap("pow4", 0, 64), 2.0, None, OP.mult)
+    ts(ap("lo", 0, 64), ap("pow4", 0, 64), 0.6, None, OP.mult)
+    for b in range(4):
+        ts(ci(4), ci(1), b, None, OP.logical_shift_right)
+        ts(ci(5), ci(4), 1, None, OP.bitwise_and)
+        ts(col(8 + b), ci(5), float(4.0 ** -(2 ** b) - 1.0), 1.0, OP.mult, OP.add)
+    tt(col(12), col(8), col(9), OP.mult); tt(col(13), col(10), col(11), OP.mult); tt(col(14), col(12), col(13), OP.mult)
+    for k in range(4): ts(ap("wt", k * 128, k * 128 + 128), ap("bo", 0, 128), col(14), float(4.0 ** (31 - 16 * k)), OP.mult, OP.mult)
+    cp(ap("HS", 0, 64), ap("hv32", 0, 64))
+    for i in range(LOADS): cp(ap("C", i * W4, (i + 1) * W4), ap("chi", i * W4, (i + 1) * W4))
+    ms(ap("C", 0, 1), 0.0)
+    ms(ap("Ks", 0, 1), FAR)
+    ms(ap("Kp", 0, 1), 0.0)
+
+    def lists(h, src, mat, out, f32):
+        mm([(ap("sc" + h, 136 + 8 * k, 144 + 8 * k), a64(mat, 128 * k, 128 * k + 128), a64(src, 15, 136, 17), True, True) for k in range(4)], f32)
+        scan(out, ap("dg", 0, 32), ap("sc" + h, 136, 168), OP.add, OP.max)
+
+    def step(t, s, h, P):
+        hi = "ab".index(h); win = NB + 128 * t; yq = 2048 * (t % 2)
+        b = t * 64 + t * 8 + hi * 4
+        L = ap("l" + h, 4 * s - 4, 4 * s) if s else ap("HS", b, b + 4)
+        cfs = ap("cf" + h, 64 * s, 64 * s + 64); S = a64("sc" + h); CT = a64("mi" + h); J = a64("mi" + h, 136, 272)
+        cp(ap("ct" + h, 0, 64), ap("C", 0, win, ind=L))
+        act(cfs, ap("C", 0, win, ind=L), AF.Copy)
+        both = h == "a" and s == 2
+        rows = h == "a" and s == 1
+        q = [(CT, cfs, ap("pj", 0, 136), not rows, False)]
+        if both: q.append((CT, ap("ones", 0, 64, p=1), ap("j4k", 0, 136, p=1), False, False))
+        if rows: q = [(a64("mi" + h, 0, 272), ap("QS", 0, 64), ap("wq", 136, 408), True, False)] + q
+        q1 = mm(q, True)
+        if rows: mm([(J, ap("oneh", 0, 64, p=1), ap("jc", 0, 136, p=1), False, False)], after=[q1])
+        q1 = mm([(S, ap("QS", t * 128 + hi * 64, t * 128 + hi * 64 + 64), ap("wq", 0, 136), True, False)])
+        for c in range(len(SIZES)):
+            w = SIZES[c]; c0 = sum(SIZES[:c]); y0 = yq + 2 * c0
+            k = ap("kg" + h, c0, c0 + w); d = ap("pd%d" % (c % 2) + h, 0, w)
+            kk = ap("Ks", 0, win, ind=ap("ct" + h, c0 // 16, (c0 + w) // 16))
+            if c == 0: cp(k, kk)
+            else: act(k, kk, AF.Copy, after=[PT[h]])
+            mm([(d, ap("eye", 0, 128), k, True, False)])
+            mm([(d, a64("pt" + h, 0, 128), a64("exn", c0, c0 + w), False, True)])
+            act(ap("yq" + h, y0, y0 + 2 * w, 2), d, AF.Abs)
+            scan(ap("zo" + h, 2 * c0, 2 * c0 + 2 * w), ap("alt", 0, 2 * w), ap("yq" + h, y0, y0 + 2 * w), OP.max, OP.min)
+        o = lambda j: a64("sc" + h, 15 - j, 136, 17)
+        y1 = mm([(o(j), ap("yq" + h, yq + 2 * j, yq + 2048, 32), ap("bo1", 0, 8), False, False) for j in range(16)], after=[q1])
+        mm([(o(j), ap("zo" + h, 2 * j + 1, 2048, 32), ap("bo2", 0, 8), False, j == 15) for j in range(16)], after=[y1])
+        scan(a64("f" + h), a64("d0t"), S, OP.max, OP.min)
+        ne = a64("ne" + h)
+        tt(ne, S, a64("f" + h), OP.not_equal)
+        if rows: mm([(CT, a64("n64k", 0, 64), ne, False, False), (J, a64("n64", 0, 64), ne, False, True)])
+        else: mm([(CT, a64("n64k", 0, 64), ne, False, True)])
+        scan(a64("w2" + h), ne, CT, OP.mult, OP.max)
+        Ln = ap("l" + h, 4 * s, 4 * s + 4); dl = ap("dl" + h, 7, 32, 8)
+        lists(h, "w2" + h, "di", ap("dl" + h, 0, 32), True)
+        if both:
+            ts(ap("pi", 0, 4), dl, OFG, None, OP.subtract)
+            ts(ap("pi", 4, 8), ap("pi", 0, 4), 4095, None, OP.bitwise_and)
+            ts(ap("pi", 8, 12), ap("pi", 0, 4), 12, None, OP.logical_shift_right)
+            cp(Ln, ap("pi", 4, 8)); cp(ap("ku", 0, 4), ap("pi", 8, 12))
+            act(ap("kr", 0, 64), ap("iot", 0, 16, ind=ap("ku", 0, 4)), AF.Copy)
+        else:
+            ts(Ln, dl, OFG, None, OP.subtract)
+        tt(ap("dd" + h, 0, 64), ap("Kp", 0, win, ind=Ln), P, OP.subtract)
+        if s < 2:
+            Pn = ap("pc" + h, 64 * s, 64 * s + 64)
+            mm([(a64("sc" + h, 256, 384), ap("dd" + h, 0, 64), ap("eye", 0, 128), True, True)])
+            PT[h] = act(a64("pt" + h, 0, 128), a64("sc" + h, 256, 384), AF.Abs)
+        else:
+            Pn = ap("PO", t * 128 + hi * 64, t * 128 + hi * 64 + 64)
+        act(Pn, ap("dd" + h, 0, 64), AF.Abs)
+        if h == "a" and s < 2:
+            ts(ap("nm", 4 * s, 4 * s + 4), dl, OFG, 1.0, OP.subtract, OP.add)
+            ts(ap("nms", 4 * s, 4 * s + 4), dl, OFG, 2.0 ** -13, OP.subtract, OP.mult)
+            act(ap("nbr", s, 128, 2), ap("iot", 0, win, ind=Ln), AF.Copy)
+            if t < NV - 1: act(ap("Ks", win + s, win + 128, 2), ap("Kp", 0, win, ind=Ln), AF.Copy)
+        if rows:
+            scan(a64("uj"), ne, J, OP.mult, OP.max)
+            lists(h, "uj", "dib", ap("dsj", 0, 32), False)
+            ts(ap("ju", 0, 4), ap("dsj", 7, 32, 8), OFG, None, OP.subtract)
+            act(ap("jr", 0, 64), ap("iot", 0, 16, ind=ap("ju", 0, 4)), AF.Copy)
+            ts(ap("ljf", 0, 4), ap("dsj", 7, 32, 8), OFG, None, OP.subtract)
+        return Pn
+
+    f64 = lambda n: ap(n, 0, 64)
+    c4 = lambda n, o=0: ap(n, o, o + 4)
+    e8 = lambda n: ap(n, 0, 8)
+
+    def slice_early(t):
+        ra = ap("cfa", 64, 128)
+        tt(c4("ca"), c4("nm"), c4("nm", 4), OP.not_equal)
+        ts(c4("cb"), c4("ljf"), 15.0, None, OP.is_lt)
+        tt(c4("cc"), c4("ca"), c4("cb"), OP.mult)
+        tt(c4("nmc"), c4("nm"), c4("cc"), OP.mult)
+        tt(c4("nmc", 4), c4("nm", 4), c4("cc"), OP.mult)
+        for n in range(8):
+            c = (0, 4, 1, 5, 2, 6, 3, 7)[n]; b = 32 * (c % 4)
+            ts(ap("emat", c * 128 + b, c * 128 + 128), ap("nbr", b, 128), ap("nmc", c, c + 1), None, OP.is_equal)
+        tt(e8("nmo"), e8("nms"), e8("ofb8"), OP.subtract)
+        ts(f64("ua"), f64("jr"), X1, None, OP.is_lt)
+        ts(f64("oj"), f64("jr"), X1, None, OP.is_equal)
+        ts(f64("oj1"), f64("jr"), X, None, OP.is_equal)
+        tt(f64("au"), ra, f64("ua"), OP.mult)
+        tt(f64("an"), ra, f64("au"), OP.subtract)
+        tt(f64("oj1"), f64("oj1"), ap("mt", 64 * t, 64 * t + 64), OP.mult)
+        tt(ap("val", 0, 64), f64("an"), f64("oj1"), OP.add)
+        tt(f64("oj"), f64("oj"), ap("nn", 64 * t, 64 * t + 64), OP.mult)
+        tt(ap("mn", 0, 128, 2), f64("au"), f64("oj"), OP.add)
+        if t < NV - 1: act(ap("Kp", NB + 128 * t, NB + 128 * t + 128), ap("Ks", NB + 128 * t, NB + 128 * t + 128), AF.Copy)
+
+    def slice_late(t):
+        win = NB + 128 * t; last = []
+        ts(c4("m4"), ap("dla", 7, 32, 8), OFG, 0.0, OP.subtract, OP.is_gt)
+        for k in range(4): ts(ap("wtf", k * 128, k * 128 + 128), ap("wt", k * 128, k * 128 + 128), ap("m4", k, k + 1), None, OP.mult)
+        for k in range(4):
+            w = ap("wtf", k * 128, k * 128 + 128)
+            last = [mm([(ap("pd0a", 32 * k, 128), w, ap("emat", c * 128 + 32 * k, c * 128 + 128), c == 0, c == 7) for c in (k, k + 4)], after=last)]
+        tt(ap("okh", 0, 128), ap("pd0a", 0, 128), ap("thi", 0, 128), OP.is_ge)
+        tt(f64("okl"), ap("pd0a", 0, 128, 2), f64("lo"), OP.is_lt)
+        tt(ap("okh", 0, 128, 2), ap("okh", 0, 128, 2), f64("okl"), OP.max)
+        scan(ap("bad", 0, 128), ap("seg4", 0, 128), ap("okh", 0, 128), OP.mult, OP.max)
+        scan(ap("ds", 0, 32), ap("dp", 0, 32), ap("bad", 3, 128, 4), OP.add, OP.max)
+        for w in range(2): tt(c4("tl", 4 * w), ap("ds", 7, 32, 8), c4("nmo", 4 * w), OP.add)
+        tt(e8("tl"), e8("tl"), e8("dump8"), OP.min)
+        ts(e8("tlu"), e8("tl"), 8192.0, None, OP.mult)
+        ts(ap("fl", 0, 32), ap("bad", 3, 128, 4), -1.0, 1.0, OP.mult, OP.add)
+        rb = ap("cfa", 128, 192)
+        ts(f64("ub"), f64("kr"), X1, None, OP.is_lt)
+        tt(ap("mn", 1, 128, 2), rb, f64("ub"), OP.mult)
+        tt(ap("val", 64, 128), rb, ap("mn", 1, 128, 2), OP.subtract)
+        cp(ap("C", 0, NW + 128, ind=e8("tlu")), ap("val", 0, 128))
+        for q in range(4): tt(ap("C", win + q, win + 128, 4), ap("mn", q, 128, 4), ap("fl", 0, 32), OP.mult)
+        if t < NV - 1:
+            add("V", lambda g, T: g.vector.tensor_reduce(T.cnt[:], T.fl[:], AxisListType.X, OP.add), (ap("fl", 0, 32),), (ap("cnt", 0, 1),), 0.09)
+            mm([(ap("pd0a", 128, 129), ap("cm", 0, 128), ap("cnt", 0, 1), True, True)], True)
+            cp(ap("zi", 0, 1), ap("pd0a", 128, 129))
+            ts(ap("zi", 1, 2), ap("zi", 0, 1), 63, None, OP.bitwise_and)
+            ts(ap("tc", 0, 1), ap("zi", 1, 2), TH, None, OP.add)
+            ts(a64("d0t"), a64("m0"), a64("tc", 0, 1), None, OP.mult)
+
+    for t in range(NV):
+        qn = ap("QS", (t + 1) * 128, (t + 2) * 128); hn = ap("HS", (t + 1) * 64, (t + 2) * 64)
+        if t < NV - 1:
+            qsent = send(qn, ap("QS", t * 128, t * 128 + 128), "aq%d" % (t + 1))
+            hsent = send(hn, ap("HS", t * 64, t * 64 + 64), "ah%d" % (t + 1))
+        P = {}; yq = 2048 * (t % 2)
+        for hi in range(2):
+            h = "ab"[hi]; b = t * 128 + hi * 64; P[h] = ap("PS", b, b + 64)
+            act(ap("yq" + h, yq + 1, yq + 2048, 2), ap("QS", b, b + 64, ind=ap("rep", 0, 64)), AF.Copy)
+            mm([(a64("sc" + h, 256, 384), P[h], ap("eye", 0, 128), True, True)])
+            PT[h] = act(a64("pt" + h, 0, 128), a64("sc" + h, 256, 384), AF.Copy)
+        if t < NV - 1:
+            recv(qn, "aq%d" % (t + 1), qsent); recv(hn, "ah%d" % (t + 1), hsent)
+        for s in range(3):
+            for h in "ab": P[h] = step(t, s, h, P[h])
+            if s == 1: slice_early(t)
+        on = [(ap("PS", (t + 1) * 128 + k * 64, (t + 1) * 128 + k * 64 + 64), "a%s%d" % ("ab"[k], t + 1)) for k in range(2)]
+        sent = [send(on[k][0], P["ab"[k]], on[k][1]) for k in range(2)]
+        slice_late(t)
+        for k in range(2): recv(on[k][0], on[k][1], sent[k])
+    cp(ap("C", 0, 1), ap("chi", 0, 1))
+    dma(ap("yp", 0, 128), ap("PS", 1024, 1152), "stp", 2)
+    for i in range(4): dma(ap("yc", i * 896, (i + 1) * 896), ap("C", i * 896, (i + 1) * 896), "st%d" % i, 5)
+    return ops
+
+
+def plan(ops):
+    hist = {}; runs = {}; m = len(ops)
+    for o in ops:
+        dep = {}
+        for (n, lo, hi) in o["rd"]:
+            for (q, w, l2, h2) in hist.get(n, ()):
+                if w and l2 < hi and lo < h2: dep[q] = "raw"
+        for (n, lo, hi) in o["wr"]:
+            for (q, w, l2, h2) in hist.get(n, ()):
+                if l2 < hi and lo < h2:
+                    if w: dep.setdefault(q, "waw")
+                    else: dep.setdefault(q, "war")
+        for q in o["after"]: dep.setdefault(q, "ord")
+        for n in {x[0] for x in o["rd"] + o["wr"]} & PSUM:
+            r = runs.setdefault(n, [])
+            if not r or r[-1][0] != o["eng"]: r.append((o["eng"], []))
+            if len(r) > 1:
+                for q in r[-2][1]: dep.setdefault(q, "bank")
+            r[-1][1].append(o["i"])
+        dep.pop(o["i"], None)
+        o["dep"] = dep
+        for (n, lo, hi) in o["wr"]:
+            old = hist.setdefault(n, [])
+            old[:] = [e for e in old if not (lo <= e[2] and e[3] <= hi)] + [(o["i"], True, lo, hi)]
+        for (n, lo, hi) in o["rd"]: hist.setdefault(n, []).append((o["i"], False, lo, hi))
+    succ = [[] for _ in ops]; left = [len(o["dep"]) for o in ops]; pri = [0.0] * m
+    for o in ops:
+        for q in o["dep"]: succ[q].append(o["i"])
+    for o in reversed(ops): pri[o["i"]] = o["cost"] + o["lag"] + LAT + max([pri[x] for x in succ[o["i"]]] or [0.0])
+    order = {e: [] for e in "VSPGYR"}; free = {e: 0.0 for e in order}
+    ready = {i for i in range(m) if left[i] == 0}; est = [0.0] * m; fin = [0.0] * m
+    while ready:
+        best = None
+        for e in free:
+            cand = [i for i in ready if e == ops[i]["eng"]]
+            if not cand: continue
+            now = [i for i in cand if est[i] <= free[e]]
+            i = max(now, key=lambda x: (pri[x], -x)) if now else min(cand, key=lambda x: (est[x], -pri[x], x))
+            st = max(free[e], est[i])
+            if best is None or (st, -pri[i]) < best[0]: best = ((st, -pri[i]), st, e, i)
+        _, st, e, i = best
+        ready.discard(i); ops[i]["q"] = e; order[e].append(i)
+        free[e] = st + ops[i]["cost"] if e != "R" else 0.0
+        fin[i] = st + ops[i]["cost"] + ops[i]["lag"]
+        for x in succ[i]:
+            est[x] = max(est[x], fin[i] + LAT); left[x] -= 1
+            if left[x] == 0: ready.add(x)
+    cnt = {e: 0 for e in order}
+    for e in order:
+        for i in order[e]:
+            if ops[i]["done"] is None:
+                cnt[e] += ops[i]["n"]; ops[i]["tgt"] = (NAME[e], cnt[e])
+            else: ops[i]["tgt"] = ops[i]["done"]
+    known = {e: {} for e in order}; at = {}; ptr = {e: 0 for e in order}; waits = {}
+    while len(at) < m:
+        for e in order:
+            while ptr[e] < len(order[e]):
+                i = order[e][ptr[e]]; o = ops[i]
+                if any(q not in at for q in o["dep"]): break
+                w = []
+                for q in sorted(o["dep"], key=lambda q: -fin[q]):
+                    kind = o["dep"][q]; p = ops[q]
+                    if e == "R" or p["done"] == ("snd", 8): continue
+                    if p["q"] == e and e != "Y" and (kind in ("bank", "ord") or (e == "P" and kind == "waw")): continue
+                    s, v = p["tgt"]
+                    if known[e].get(s, 0) >= v: continue
+                    w.append((s, v))
+                    for s2, v2 in list(at[q].items()) + [(s, v)]:
+                        if known[e].get(s2, 0) < v2: known[e][s2] = v2
+                waits[i] = [x for x in w if not any(y[0] == x[0] and y[1] > x[1] for y in w)]
+                at[i] = dict(known[e]); ptr[e] += 1
+    return order, waits, cnt, max(fin)
+
+
+NAME = {"V": "v", "S": "s", "P": "pe", "G": "gp"}
+MEMO = {}
+
+
+def rank_program(g, core, T, topo):
+    if T.rank_of(core) is None: return
+    if "p" not in MEMO:
+        MEMO["o"] = build(); MEMO["p"] = plan(MEMO["o"])
+    ops = MEMO["o"]; order, waits, cnt, _ = MEMO["p"]
+    queue = {"V": g.vector, "S": g.scalar, "P": g.tensor, "G": g, "Y": g.sync}
+    sent = 0
+    for e in "YVSPG":
+        for i in order[e]:
+            o = ops[i]
+            for s, v in waits[i]: queue[e].wait_ge(T.sem[s], v)
+            if o["done"] == ("snd", 8):
+                o["emit"](g, T, core, topo); sent += 8
+            elif o["done"]: o["emit"](g, T).then_inc(T.sem[o["done"][0]], 16)
+            else:
+                r = o["emit"](g, T)
+                for x in (r if isinstance(r, list) else [r]): x.then_inc(T.sem[NAME[e]], 1)
+    for e in "VSPG": g.wait_ge(T.sem[NAME[e]], cnt[e])
+    for s in DMAS: g.wait_ge(T.sem[s], 16)
+    g.wait_ge(T.sem["snd"], sent)

@@ -4,42 +4,56 @@ OP = AluOpType
 AF = ActivationFunctionType
 N, NB, NV = 8, 2560, 8
 NW = NB + 128 * NV
-FAR, BIG, TH = 1024.0, 2048.0, 1235.5
-SIZES = (512, 512)
+FAR, OFF, TH = 1024.0, 4096.0, 1235 + 31 / 32
+CHUNKS = ((0, 6), (6, 12), (12, 16))
+KV = 32
+PFIRST = True
 LOADS = 4
+YW = 64 * 17
 F, H, I, U = "float32", "bfloat16", "int32", "uint16"
 SCRATCH = {}
 for _t, _n, _names in (
-        (I, NB, "chi"), (F, NW + 128, "C"), (H, NW, "Ks Kp"), (H, 1024, "QS PO exn alt emat kga kgb"), (U, 512, "HS"), (H, 1152, "PS"),
-        (I, 64, "hv32 repi"), (H, 128, "eye bo okh bad seg4 pta pca ptb pcb"), (H, 8, "bo2 bo1"), (H, 408, "wq"),
-        (H, 136, "jc uj nea neb"), (F, 136, "m0 pj j4k gi17 d0t fa w2a fb w2b"), (F, 512, "di mt nn"), (H, 512, "dib wt wtf"),
-        (H, 64, "n64k n64 oneh okl dda ddb"), (F, 64, "ones pow4 quart zero lo jr kr ua oj oj1 ub au an"), (I, 12, "pi"),
-        (F, 128, "gi thi cm nbr val mn"), (F, 32, "pos8 dg dp cols fl ds dsj dla dlb"), (I, 16, "coli"), (U, 64, "rep cta ctb"),
-        (F, NW, "iot"), (F, 8, "dump0 dump8 nm nms nmo nmc ofb8 tl"), (F, 4, "ljf ca cb cc m4"), (U, 4, "ju ku"), (U, 8, "tlu"),
-        (F, 1, "cnt tc"), (I, 2, "zi"), (F, 192, "cfa cfb"), (H, 4096, "yqa yqb"), (H, 2048, "zoa zob"), (U, 12, "la lb")):
+        (I, NB, "chi"), (F, NW + 64, "C"), (H, NW, "Ks Kp"), (H, 1024, "QP emat"), (U, 576, "HS"), (H, 2048, "PS PO"),
+        (I, 64, "hv32"), (H, 128, "QS PF eye ones boB good seg kqa kqb"), (F, 128, "gd"), (H, 4, "gh"), (H, 144, "Wy Wz"), (H, 256, "pta ptb"),
+        (H, 68, "c4k jrow dj dw nea neb uj uw"), (F, 68, "d0a d0b fa fb"), (F, 204, "wa wb"), (F, 512, "mt nn dm"), (H, 512, "wtf"),
+        (H, 64, "n64"), (H, 32, "dg"), (F, 64, "pow4 quart zero oj oj1 au an"), (F, 48, "tb"),
+        (F, 128, "gi thm pr nbr val mn cf"), (F, 32, "cols"), (I, 16, "coli"), (U, 64, "cta ctb"),
+        (F, NW, "iot"), (F, 8, "nd"), (F, 4, "dump w4 ca wc"), (U, 4, "ju ku gu"), (U, 8, "tlu"),
+        (F, 1, "tc"), (I, 2, "zi"), (H, YW, "exn hold qza qzb ya yb za zb"), (H, 2 * YW, "qra qrb"), (U, 12, "la lb")):
     for _b in _names.split(): SCRATCH[_b] = ("sbuf", [128, _n], _t)
-for _b in "pd0a pd1a sca mia pd0b pd1b scb mib".split(): SCRATCH[_b] = ("psum", [128, 512], F)
+for _h in "ab":
+    SCRATCH["kg" + _h] = ("sbuf", [128, 1024], H)
+    SCRATCH["cx" + _h] = ("sbuf", [128, 4, 32], F)
+    SCRATCH["tx" + _h] = ("sbuf", [128, 4, 34], F)
+    for _b in ("sc", "mi"): SCRATCH[_b + _h] = ("psum", [128, 512], F)
+    for _b in ("pd0", "pd1"): SCRATCH[_b + _h] = ("psum", [128, 30, 17], F)
 PSUM = {k for k, v in SCRATCH.items() if v[0] == "psum"}
-DMAS = ["ld%d" % i for i in range(LOADS)] + "ldk ldp ldq ldh st0 st1 st2 st3 stp".split()
+DMAS = ["ld%d" % i for i in range(LOADS)] + "ldk ldp ldq ldh st0 st1 st2 st3 spa spb".split()
 SEMAPHORES = ("v s pe gp snd".split() + DMAS + ["a%s%d" % (k, t) for k in "qh" for t in range(1, 8)]
               + ["a%s%d" % (h, t) for h in "ab" for t in range(1, 9)])
 CY, PCY, LAT = 0.00083, 0.00042, 0.11
 
 
 def ap(name, c0, c1, step=1, p=128, ind=None):
-    return (name, c0, c1, step, p, ind)
+    return (name, c0, c1, step, p, ind, None, (c0, c1))
+
+
+def a3(name, m0, m1, ms, c0, c1, part=(0, 4)):
+    return (name, c0, c1, 1, 128, None, (m0, m1, ms), part)
 
 
 def toks(a):
-    return [(a[0], a[1], a[2])] + (toks(a[5]) if a[5] else [])
+    return [(a[0],) + a[7]] + (toks(a[5]) if a[5] else [])
 
 
 def res(T, a):
+    if a[6]: return T[a[0]][0:128, a[6][0]:a[6][1]:a[6][2], a[1]:a[2]]
     v = T[a[0]][0:a[4], a[1]:a[2]] if a[3] == 1 else T[a[0]][0:a[4], a[1]:a[2]:a[3]]
     return v.indirect(res(T, a[5])) if a[5] else v
 
 
 def ln(a):
+    if a[6]: return -(-(a[6][1] - a[6][0]) // a[6][2]) * (a[2] - a[1])
     return 16 * (a[5][2] - a[5][1]) if a[5] else -(-(a[2] - a[1]) // a[3])
 
 
@@ -48,7 +62,7 @@ def two(*aps):
 
 
 def build():
-    ops = []; PT = {}
+    ops = []
 
     def add(eng, emit, rd, wr, cost, n=1, done=None, after=(), lag=0.0):
         o = {"eng": eng, "emit": emit, "rd": [t for a in rd for t in toks(a)], "wr": [toks(a)[0] for a in wr], "cost": cost,
@@ -75,17 +89,22 @@ def build():
         return add("V", emit, [a] + [s for s in (s1, s2) if isinstance(s, tuple)], (out,), vc(out, (), 0.5 if two(out, a) else 1))
 
     def cp(out, a):
-        return add("V", lambda g, T: g.vector.tensor_copy(res(T, out), res(T, a)), (a,), (out,), vc(out, (a,)))
+        return add("V", lambda g, T: g.vector.tensor_copy(res(T, out), res(T, a)), (a,), (out,), vc(out, (a,), 0.5 if two(out, a) else 1))
 
     def scan(out, d0, d1, o1, o2, init=0.0):
         return add("V", lambda g, T: g.vector.tensor_tensor_scan(res(T, out), res(T, d0), res(T, d1), init, o1, o2), (d0, d1), (out,), vc(out, (), 0.5 if two(out, d0, d1) else 1))
 
-    def ms(out, x):
-        return add("V", lambda g, T: g.vector.memset(res(T, out), x), (), (out,), vc(out, ()))
+    def turn(out, a):
+        return add("V", lambda g, T: g.vector.transpose(res(T, out), res(T, a)), (a,), (out,), vc(out, ()))
 
-    def act(out, a, func, scale=1.0, after=()):
-        return add("S", lambda g, T: g.scalar.activation(res(T, out), res(T, a), func, scale=scale), (a,), (out,),
-                   0.08 + ln(out) * (1.5 if a[5] else 1.0) * CY, after=after)
+    def ms(out, x):
+        return add("V", lambda g, T: g.vector.memset(res(T, out), x), (), (out,), vc(out, (), 0.5 if two(out) else 1))
+
+    def act(out, a, func, scale=None, after=()):
+        def emit(g, T):
+            if scale: return g.scalar.activation(res(T, out), res(T, a), func, scale=res(T, scale))
+            return g.scalar.activation(res(T, out), res(T, a), func)
+        return add("S", emit, (a, scale) if scale else (a,), (out,), 0.08 + ln(out) * (1.5 if a[5] else 1.0) * CY, after=after)
 
     def mm(ml, f32=False, after=()):
         def emit(g, T):
@@ -118,233 +137,205 @@ def build():
 
     W4 = NB // LOADS
     dma(ap("hv32", 0, 64), ap("hv", 0, 64), "ldh", 2.2)
+    dma(ap("QS", 0, 128), ap("qs", 0, 128), "ldq", 2.3)
     for i in range(LOADS): dma(ap("chi", i * W4, (i + 1) * W4), ap("ch", i * W4, (i + 1) * W4), "ld%d" % i, 3.0 + 0.8 * i)
-    dma(ap("QS", 0, 128), ap("qs", 0, 128), "ldq", 3)
     dma(ap("Ks", 0, NB), ap("kb", 0, NB), "ldk", 6.5)
     dma(ap("Kp", 0, NB), ap("kb", 0, NB), "ldp", 7.5)
     col = lambda k: ap("cols", k, k + 1)
     ci = lambda k: ap("coli", k, k + 1)
-    a64 = lambda n, c0=0, c1=136, st=1: ap(n, c0, c1, st, 64)
-    X, GC, RH, OFG, OFP, X1 = [col(k) for k in range(6)]
+    a64 = lambda n, c0=0, c1=128: ap(n, c0, c1, 1, 64)
+    s68 = lambda n, o=0: ap(n, o, o + 68)
+    end = lambda n, o=0: ap(n, o + 16, o + 68, 17)
+    f64 = lambda n, o=0: ap(n, o, o + 64)
+    c4 = lambda n, o=0: ap(n, o, o + 4)
+    eye = ap("eye", 0, 128)
+    X, GC, RH, EV, OD, WC, X2, X1, WM = [col(k) for k in range(9)]
     iota(ci(0), [[0, 1]], 0, 1)
-    iota(ap("gi", 0, 128), [[1, 8], [0, 16]], 0, 0)
-    ms(ap("eye", 0, 128), 1.0)
-    aff(ap("eye", 0, 128), [[-1, 128]], 0)
-    ms(ap("pj", 0, 136), 1.0)
-    aff(ap("pj", 0, 136), [[-16, 8], [1, 17]], -15)
-    ms(ap("pj", 16, 136, 17), 0.0)
+    iota(ap("iot", 0, 144), [[1, 144]], 0, 0)
+    ms(eye, 1.0)
+    aff(eye, [[-1, 128]], 0)
     ms(a64("exn", 0, 1024), -1.0)
-    aff(a64("exn", 0, 1024), [[-1, 64], [0, 16]], 0)
-    iota(ap("repi", 0, 64), [[1, 64]], 0, 0)
-    cp(ap("rep", 0, 64), ap("repi", 0, 64))
-    iota(ap("gi17", 0, 136), [[1, 8], [0, 17]], 0, 0)
-    ms(a64("di", 0, 512), 1.0)
-    aff(a64("di", 0, 512), [[-16, 4], [0, 8], [-1, 16]], 0)
-    iota(ap("pos8", 0, 32), [[0, 4], [1, 8]], 0, 0)
-    iota(ap("jc", 0, 136), [[0, 8], [-1, 17]], 15, 0)
-    ms(ap("jc", 16, 136, 17), 0.0)
-    ms(ap("ones", 0, 64), 1.0); ms(ap("oneh", 0, 64), 1.0)
-    iota(ap("j4k", 0, 136), [[0, 8], [-4096, 17]], 61440, 0)
-    ms(ap("j4k", 16, 136, 17), 0.0)
-    iota(ap("dump0", 0, 8), [[16, 8]], NW, 0)
-    iota(ap("iot", 0, NW), [[1, NW]], 1, 0)
+    aff(a64("exn", 0, 1024), [[-1, 16], [-16, 4], [0, 16]], 0)
+    iota(s68("jrow"), [[0, 4], [1, 17]], -1, 0)
+    iota(ap("gi", 0, 128), [[1, 8], [0, 16]], 0, 0)
+    iota(ap("iot", 144, NW), [[1, NW - 144]], 144, 0)
+    iota(ap("pr", 0, 128), [[0, 4], [1, 8], [0, 4]], 0, 0)
+    iota(c4("dump"), [[16, 4]], NW, 0)
     iota(ap("mt", 0, 512), [[128, 8], [4, 32], [-2, 2]], NB + 2, 0)
     iota(ap("nn", 0, 512), [[128, 8], [2, 64]], NB + 1, 0)
     ts(ci(1), ci(0), 15, None, OP.bitwise_and)
     ts(ci(2), ci(0), 4, None, OP.logical_shift_right)
     ts(ci(3), ci(1), 1, None, OP.logical_shift_right)
-    cp(X, ci(1)); cp(GC, ci(2)); cp(RH, ci(3))
-    ts(ap("bo", 0, 128), ap("gi", 0, 128), GC, None, OP.is_equal)
-    ts(ap("bo1", 0, 8), ap("gi", 0, 128, 16), GC, None, OP.is_equal)
-    ts(ap("bo2", 0, 8), ap("gi", 0, 128, 16), GC, -2.0, OP.is_equal, OP.mult)
-    ts(ap("wq", 0, 136), ap("gi17", 0, 136), GC, None, OP.is_equal)
-    ms(ap("wq", 16, 136, 17), 0.0); ms(ap("wq", 136, 408), 0.0)
-    ts(a64("n64k", 0, 64), a64("eye", 0, 64), -65536.0, None, OP.mult)
-    ts(a64("n64", 0, 64), a64("eye", 0, 64), -64.0, None, OP.mult)
-    ms(a64("m0"), 0.0)
-    ms(a64("m0", 0, 136, 17), 1.0)
-    ms(ap("alt", 0, 1024, 2), BIG)
-    ms(ap("alt", 1, 1024, 2), 0.0)
-    ts(ap("dg", 0, 32), ap("pos8", 0, 32), GC, 1065536.0, OP.is_gt, OP.mult)
-    ts(ap("dg", 0, 32), ap("dg", 0, 32), -1000000.0, None, OP.add)
-    ts(OFG, GC, -65536.0, 458752.0, OP.mult, OP.add)
-    ts(a64("d0t"), a64("m0"), TH, None, OP.mult)
-    ms(ap("PS", 0, 128), 0.0)
-    ms(ap("C", NB, NW + 128), 0.0)
-    cp(a64("dib", 0, 512), a64("di", 0, 512))
-    ts(ap("dp", 0, 32), ap("pos8", 0, 32), RH, 1010.0, OP.is_gt, OP.mult)
-    ts(ap("dp", 0, 32), ap("dp", 0, 32), -1000.0, None, OP.add)
-    ts(OFP, RH, -10.0, 70.0, OP.mult, OP.add)
-    ms(ap("ofb8", 0, 8), 0.0); ts(ap("ofb8", 0, 8), ap("ofb8", 0, 8), OFP, None, OP.add)
-    ms(ap("seg4", 0, 128), 1.0); ms(ap("seg4", 0, 128, 4), 0.0)
-    ts(X1, X, 1.0, None, OP.add)
-    ts(ap("dump8", 0, 8), ap("dump0", 0, 8), X, 2.0 ** -13, OP.add, OP.mult)
-    ms(ap("cm", 0, 128), 0.125)
-    ms(ap("quart", 0, 64), 0.25); ms(ap("zero", 0, 64), 0.0)
-    scan(ap("pow4", 0, 64), ap("quart", 0, 64), ap("zero", 0, 64), OP.mult, OP.add, float(4.0 ** 32))
-    ts(ap("thi", 0, 128, 2), ap("pow4", 0, 64), 2.0, None, OP.mult)
-    ts(ap("thi", 1, 128, 2), ap("pow4", 0, 64), 2.0, None, OP.mult)
-    ts(ap("lo", 0, 64), ap("pow4", 0, 64), 0.6, None, OP.mult)
+    ts(ci(6), ci(2), 1, None, OP.bitwise_and)
+    cp(X, ci(1)); cp(GC, ci(2)); cp(RH, ci(3)); cp(OD, ci(6))
+    ts(EV, OD, -1.0, 1.0, OP.mult, OP.add)
+    ts(WC, GC, 16.0, 15.0, OP.mult, OP.add)
+    ts(ap("Wy", 0, 144), ap("iot", 0, 144), WC, None, OP.is_equal)
+    ts(ap("Wz", 0, 144), ap("iot", 0, 144), WC, -2.0, OP.is_equal, OP.mult)
+    ts(a64("n64", 0, 64), a64("eye", 0, 64), -1.0, None, OP.mult)
+    for k in range(4): ts(ap("dm", 128 * k, 128 * k + 128), eye, (EV, OD)[k // 2], (1.0, -1.0)[k % 2], OP.mult, OP.mult)
+    ms(ap("ones", 0, 128), 1.0)
+    ms(s68("c4k"), OFF); ms(ap("c4k", 0, 68, 17), 0.0)
+    ts(s68("jrow"), s68("jrow"), 1 / 16, 0.0, OP.mult, OP.max)
+    ms(s68("dj"), -1.0); ms(ap("dj", 0, 68, 17), 0.0); ms(end("dj"), 15.0)
+    ms(ap("hold", 0, YW), 1.0); ms(ap("hold", 0, YW, 17), 0.0)
+    for h in "ab":
+        ms(ap("qz" + h, 0, YW), 0.0); ms(s68("d0" + h), 0.0)
+        for k in "01": ms(a3("pd" + k + h, 0, 30, 1, 0, 1), 0.0)
+        ms(a3("tx" + h, 0, 4, 1, 0, 1), 0.0); ms(a3("tx" + h, 0, 4, 1, 33, 34), 0.0)
+    ms(ap("tc", 0, 1), TH + OFF)
+    ms(ap("PS", 0, 256), 0.0)
+    ms(ap("PO", 0, 2048), 0.0)
+    ms(ap("C", NB, NW + 64), 0.0)
+    ts(ap("boB", 0, 128), ap("gi", 0, 128), GC, 2.0 ** 64, OP.is_equal, OP.mult)
+    ts(X2, X, 2.0, None, OP.mult); ts(X1, X, -1.0, None, OP.add)
+    ts(ap("dg", 0, 32), ap("iot", 0, 32), X2, -3.0, OP.is_equal, OP.mult)
+    ts(ap("tb", 0, 16), ap("iot", 0, 16), X, None, OP.is_ge)
+    ts(ap("tb", 16, 32), ap("iot", 0, 16), X, None, OP.is_equal)
+    ts(ap("tb", 32, 48), ap("iot", 0, 16), X1, None, OP.is_equal)
+    ms(ap("seg", 0, 128), 0.0); ms(ap("seg", 0, 128, 32), 1.0)
+    ts(c4("dump"), c4("dump"), X, None, OP.add)
+    ms(f64("quart"), 0.25); ms(f64("zero"), 0.0)
+    scan(f64("pow4"), f64("quart"), f64("zero"), OP.mult, OP.add, float(4.0 ** 32))
+    ts(ap("thm", 0, 128, 2), f64("pow4"), -1.0, None, OP.mult)
+    ts(ap("thm", 1, 128, 2), f64("pow4"), 2.0, None, OP.mult)
+    ts(ap("pr", 0, 128), ap("pr", 0, 128), RH, 1e29, OP.not_equal, OP.mult)
+    tt(ap("thm", 0, 128), ap("thm", 0, 128), ap("pr", 0, 128), OP.add)
     for b in range(4):
         ts(ci(4), ci(1), b, None, OP.logical_shift_right)
         ts(ci(5), ci(4), 1, None, OP.bitwise_and)
-        ts(col(8 + b), ci(5), float(4.0 ** -(2 ** b) - 1.0), 1.0, OP.mult, OP.add)
-    tt(col(12), col(8), col(9), OP.mult); tt(col(13), col(10), col(11), OP.mult); tt(col(14), col(12), col(13), OP.mult)
-    for k in range(4): ts(ap("wt", k * 128, k * 128 + 128), ap("bo", 0, 128), col(14), float(4.0 ** (31 - 16 * k)), OP.mult, OP.mult)
+        ts(col(12 + b), ci(5), float(4.0 ** -(2 ** b) - 1.0), 1.0, OP.mult, OP.add)
+    tt(col(16), col(12), col(13), OP.mult); tt(col(17), col(14), col(15), OP.mult); tt(WM, col(16), col(17), OP.mult)
+    ts(c4("w4"), ap("pow4", 0, 64, 16), WM, None, OP.mult)
+    ms(s68("dw"), 0.0)
+    ts(ap("dw", 0, 68, 17), c4("w4"), -1.0, None, OP.mult); cp(ap("dw", 15, 68, 17), c4("w4"))
     cp(ap("HS", 0, 64), ap("hv32", 0, 64))
+    for hi in range(2):
+        for c in range(4): cp(ap("QP", 64 * hi + c, 64 * hi + 64, 4), ap("QS", 64 * hi + 16 * c, 64 * hi + 16 * c + 16))
+        o = c4("sc" + "ab"[hi])
+        mm([(o, ap("Wy", 15 - m, 143 - m), c4("QP", 64 * hi + 4 * m), m == 0, m == 15) for m in range(16)])
+        cp(c4("HS", 64 + 4 * hi), o)
     for i in range(LOADS): cp(ap("C", i * W4, (i + 1) * W4), ap("chi", i * W4, (i + 1) * W4))
     ms(ap("C", 0, 1), 0.0)
     ms(ap("Ks", 0, 1), FAR)
     ms(ap("Kp", 0, 1), 0.0)
-
-    def lists(h, src, mat, out, f32):
-        mm([(ap("sc" + h, 136 + 8 * k, 144 + 8 * k), a64(mat, 128 * k, 128 * k + 128), a64(src, 15, 136, 17), True, True) for k in range(4)], f32)
-        scan(out, ap("dg", 0, 32), ap("sc" + h, 136, 168), OP.add, OP.max)
+    PT = {}
 
     def step(t, s, h, P):
-        hi = "ab".index(h); win = NB + 128 * t; yq = 2048 * (t % 2)
-        b = t * 64 + t * 8 + hi * 4
-        L = ap("l" + h, 4 * s - 4, 4 * s) if s else ap("HS", b, b + 4)
-        cfs = ap("cf" + h, 64 * s, 64 * s + 64); S = a64("sc" + h); CT = a64("mi" + h); J = a64("mi" + h, 136, 272)
-        cp(ap("ct" + h, 0, 64), ap("C", 0, win, ind=L))
-        act(cfs, ap("C", 0, win, ind=L), AF.Copy)
-        both = h == "a" and s == 2
-        rows = h == "a" and s == 1
-        q = [(CT, cfs, ap("pj", 0, 136), not rows, False)]
-        if both: q.append((CT, ap("ones", 0, 64, p=1), ap("j4k", 0, 136, p=1), False, False))
-        if rows: q = [(a64("mi" + h, 0, 272), ap("QS", 0, 64), ap("wq", 136, 408), True, False)] + q
-        q1 = mm(q, True)
-        if rows: mm([(J, ap("oneh", 0, 64, p=1), ap("jc", 0, 136, p=1), False, False)], after=[q1])
-        q1 = mm([(S, ap("QS", t * 128 + hi * 64, t * 128 + hi * 64 + 64), ap("wq", 0, 136), True, False)])
-        for c in range(len(SIZES)):
-            w = SIZES[c]; c0 = sum(SIZES[:c]); y0 = yq + 2 * c0
-            k = ap("kg" + h, c0, c0 + w); d = ap("pd%d" % (c % 2) + h, 0, w)
-            kk = ap("Ks", 0, win, ind=ap("ct" + h, c0 // 16, (c0 + w) // 16))
-            if c == 0: cp(k, kk)
-            else: act(k, kk, AF.Copy, after=[PT[h]])
-            mm([(d, ap("eye", 0, 128), k, True, False)])
-            mm([(d, a64("pt" + h, 0, 128), a64("exn", c0, c0 + w), False, True)])
-            act(ap("yq" + h, y0, y0 + 2 * w, 2), d, AF.Abs)
-            scan(ap("zo" + h, 2 * c0, 2 * c0 + 2 * w), ap("alt", 0, 2 * w), ap("yq" + h, y0, y0 + 2 * w), OP.max, OP.min)
-        o = lambda j: a64("sc" + h, 15 - j, 136, 17)
-        y1 = mm([(o(j), ap("yq" + h, yq + 2 * j, yq + 2048, 32), ap("bo1", 0, 8), False, False) for j in range(16)], after=[q1])
-        mm([(o(j), ap("zo" + h, 2 * j + 1, 2048, 32), ap("bo2", 0, 8), False, j == 15) for j in range(16)], after=[y1])
-        scan(a64("f" + h), a64("d0t"), S, OP.max, OP.min)
-        ne = a64("ne" + h)
-        tt(ne, S, a64("f" + h), OP.not_equal)
-        if rows: mm([(CT, a64("n64k", 0, 64), ne, False, False), (J, a64("n64", 0, 64), ne, False, True)])
-        else: mm([(CT, a64("n64k", 0, 64), ne, False, True)])
-        scan(a64("w2" + h), ne, CT, OP.mult, OP.max)
-        Ln = ap("l" + h, 4 * s, 4 * s + 4); dl = ap("dl" + h, 7, 32, 8)
-        lists(h, "w2" + h, "di", ap("dl" + h, 0, 32), True)
-        if both:
-            ts(ap("pi", 0, 4), dl, OFG, None, OP.subtract)
-            ts(ap("pi", 4, 8), ap("pi", 0, 4), 4095, None, OP.bitwise_and)
-            ts(ap("pi", 8, 12), ap("pi", 0, 4), 12, None, OP.logical_shift_right)
-            cp(Ln, ap("pi", 4, 8)); cp(ap("ku", 0, 4), ap("pi", 8, 12))
-            act(ap("kr", 0, 64), ap("iot", 0, 16, ind=ap("ku", 0, 4)), AF.Copy)
+        hi = "ab".index(h); win = NB + 128 * t; qr = YW * (t % 2)
+        L = c4("l" + h, 4 * s - 4) if s else c4("HS", t * 80 + hi * 4)
+        kids = ap("C", 0, win if s else NB, ind=L); S = s68("sc" + h); D = s68("mi" + h); W = 68 * s
+        cp(f64("ct" + h), kids)
+        cp(ap("kg" + h, 0, 16 * KV), ap("Ks", 0, win, ind=ap("ct" + h, 0, KV)))
+        act(ap("kg" + h, 16 * KV, 1024), ap("Ks", 0, win, ind=ap("ct" + h, KV, 64)), AF.Copy, after=[PT[h]] if s and PFIRST else [])
+        ts(a3("cx" + h, 0, 4, 1, 0, 16, (0, 1)), f64("ct" + h), EV, None, OP.mult)
+        ts(a3("cx" + h, 0, 4, 1, 16, 32, (1, 2)), f64("ct" + h), OD, None, OP.mult)
+        if h == "a" and s: act(f64("cf", 64 * s - 64), kids, AF.Copy)
+        turn(a3("tx" + h, 0, 4, 1, 1, 33), a3("cx" + h, 0, 4, 1, 0, 32))
+        mm([(D, ap("dm", 128 * k, 128 * k + 128), a3("tx" + h, 0, 4, 1, o, o + 17), k == 0, k == 3) for k, o in enumerate((0, 1, 16, 17))], True)
+        mm([(S, ap("ones", 0, 128, p=1), ap(r, 0, 68, p=1), r == "c4k", False) for r in ("c4k", "jrow")])
+        for c, (m0, m1) in enumerate(CHUNKS):
+            c0, c1 = 68 * m0, 68 * m1; pd = "pd%d" % (c % 2) + h; n = 4 * (m1 - m0); d = a3(pd, 0, n, 1, 0, 17)
+            dk = a3(pd, 0, n, 1, 1, 17); ex = a64("exn", 64 * m0, 64 * m1)
+            if s: mm([(dk, P, ex, True, False)])
+            mm([(a3(pd, b, n, 4, 1, 17), eye, ap("kg" + h, 256 * b + 16 * m0, 256 * b + 16 * m1), s == 0 and b == 0, s > 0 and b == 3) for b in range(4)])
+            if not s: mm([(dk, P, ex, False, True)])
+            act(ap("y" + h, c0, c1), d, AF.Abs)
+            mm([(S, ap("Wy", 15 - m, 143 - m), s68("y" + h, 68 * m), False, False) for m in range(m0, m1)])
+            scan(ap("z" + h, c0, c1), ap("qr" + h, qr + c0, qr + c1), ap("y" + h, c0, c1), OP.max, OP.min)
+            mm([(S, ap("Wz", 15 - m, 143 - m), s68("z" + h, 68 * m), False, m == 15) for m in range(m0, m1)])
+        ne = s68("ne" + h)
+        scan(s68("f" + h), s68("d0" + h), S, OP.max, OP.min)
+        tt(ne, S, s68("f" + h), OP.not_equal)
+        scan(s68("w" + h, W), ne, D, OP.mult, OP.add)
+        Ln = c4("l" + h, 4 * s)
+        cp(Ln, end("w" + h, W))
+        kq = ap("Ks", win + s, win + 128, 2) if h == "a" and s < 2 else f64("kq" + h)
+        if t == NV - 1 and s == 2:
+            o = ap("mi" + h, 128, 192); Pn = f64("kq" + h, 64)
+            mm([(o, P, a64("n64", 0, 64), True, False)])
+            act(kq, ap("Kp", 0, win, ind=Ln), AF.Copy)
+            mm([(o, eye, kq, False, True)])
         else:
-            ts(Ln, dl, OFG, None, OP.subtract)
-        tt(ap("dd" + h, 0, 64), ap("Kp", 0, win, ind=Ln), P, OP.subtract)
-        if s < 2:
-            Pn = ap("pc" + h, 64 * s, 64 * s + 64)
-            mm([(a64("sc" + h, 256, 384), ap("dd" + h, 0, 64), ap("eye", 0, 128), True, True)])
-            PT[h] = act(a64("pt" + h, 0, 128), a64("sc" + h, 256, 384), AF.Abs)
-        else:
-            Pn = ap("PO", t * 128 + hi * 64, t * 128 + hi * 64 + 64)
-        act(Pn, ap("dd" + h, 0, 64), AF.Abs)
-        if h == "a" and s < 2:
-            ts(ap("nm", 4 * s, 4 * s + 4), dl, OFG, 1.0, OP.subtract, OP.add)
-            ts(ap("nms", 4 * s, 4 * s + 4), dl, OFG, 2.0 ** -13, OP.subtract, OP.mult)
-            act(ap("nbr", s, 128, 2), ap("iot", 0, win, ind=Ln), AF.Copy)
-            if t < NV - 1: act(ap("Ks", win + s, win + 128, 2), ap("Kp", 0, win, ind=Ln), AF.Copy)
-        if rows:
-            scan(a64("uj"), ne, J, OP.mult, OP.max)
-            lists(h, "uj", "dib", ap("dsj", 0, 32), False)
-            ts(ap("ju", 0, 4), ap("dsj", 7, 32, 8), OFG, None, OP.subtract)
-            act(ap("jr", 0, 64), ap("iot", 0, 16, ind=ap("ju", 0, 4)), AF.Copy)
-            ts(ap("ljf", 0, 4), ap("dsj", 7, 32, 8), OFG, None, OP.subtract)
+            o = a64("mi" + h, 128, 256); b = t * 256 + hi * 128
+            Pn = a64("pt" + h, 128 * s, 128 * s + 128) if s < 2 else a64("PO", b, b + 128)
+            mm([(o, a64("n64", 0, 64), P, True, False)])
+            act(kq, ap("Kp", 0, win, ind=Ln), AF.Copy)
+            mm([(o, kq, eye, False, True)])
+        PT[h] = act(Pn, o, AF.Abs)
+        if h == "a" and s < 2: act(ap("nbr", s, 128, 2), ap("iot", 0, win, ind=Ln), AF.Copy)
+        if h == "a" and s:
+            scan(s68("uj"), ne, s68("dj"), OP.mult, OP.add)
+            cp(c4("ju" if s == 1 else "ku"), end("uj"))
+        if h == "a" and s == 1: scan(s68("uw"), ne, s68("dw"), OP.mult, OP.add)
         return Pn
 
-    f64 = lambda n: ap(n, 0, 64)
-    c4 = lambda n, o=0: ap(n, o, o + 4)
-    e8 = lambda n: ap(n, 0, 8)
-
     def slice_early(t):
-        ra = ap("cfa", 64, 128)
-        tt(c4("ca"), c4("nm"), c4("nm", 4), OP.not_equal)
-        ts(c4("cb"), c4("ljf"), 15.0, None, OP.is_lt)
-        tt(c4("cc"), c4("ca"), c4("cb"), OP.mult)
-        tt(c4("nmc"), c4("nm"), c4("cc"), OP.mult)
-        tt(c4("nmc", 4), c4("nm", 4), c4("cc"), OP.mult)
-        for n in range(8):
-            c = (0, 4, 1, 5, 2, 6, 3, 7)[n]; b = 32 * (c % 4)
-            ts(ap("emat", c * 128 + b, c * 128 + 128), ap("nbr", b, 128), ap("nmc", c, c + 1), None, OP.is_equal)
-        tt(e8("nmo"), e8("nms"), e8("ofb8"), OP.subtract)
-        ts(f64("ua"), f64("jr"), X1, None, OP.is_lt)
-        ts(f64("oj"), f64("jr"), X1, None, OP.is_equal)
-        ts(f64("oj1"), f64("jr"), X, None, OP.is_equal)
-        tt(f64("au"), ra, f64("ua"), OP.mult)
-        tt(f64("an"), ra, f64("au"), OP.subtract)
-        tt(f64("oj1"), f64("oj1"), ap("mt", 64 * t, 64 * t + 64), OP.mult)
-        tt(ap("val", 0, 64), f64("an"), f64("oj1"), OP.add)
-        tt(f64("oj"), f64("oj"), ap("nn", 64 * t, 64 * t + 64), OP.mult)
-        tt(ap("mn", 0, 128, 2), f64("au"), f64("oj"), OP.add)
-        if t < NV - 1: act(ap("Kp", NB + 128 * t, NB + 128 * t + 128), ap("Ks", NB + 128 * t, NB + 128 * t + 128), AF.Copy)
+        win = NB + 128 * t; ra = f64("cf")
+        tt(c4("ca"), end("wa"), end("wa", 68), OP.not_equal)
+        tt(c4("wc"), c4("ca"), end("uw"), OP.mult)
+        for c in range(4):
+            for w in range(2):
+                o = 128 * (c + 4 * w); n = 68 * w + 17 * c + 16
+                ts(ap("emat", o + 32 * c, o + 128), ap("nbr", 32 * c, 128), ap("wa", n, n + 1), None, OP.is_equal)
+        for w in range(2): tt(c4("nd", 4 * w), end("wa", 68 * w), c4("dump"), OP.subtract)
+        tt(f64("an"), ap("tb", 0, 16, ind=c4("ju")), ra, OP.mult)
+        tt(f64("oj1"), ap("tb", 32, 48, ind=c4("ju")), f64("mt", 64 * t), OP.mult)
+        tt(f64("val"), f64("an"), f64("oj1"), OP.add)
+        tt(f64("au"), ra, f64("an"), OP.subtract)
+        tt(f64("oj"), ap("tb", 16, 32, ind=c4("ju")), f64("nn", 64 * t), OP.mult)
+        tt(f64("mn"), f64("au"), f64("oj"), OP.add)
+        if t < NV - 1: cp(ap("Kp", win, win + 128), ap("Ks", win, win + 128))
 
     def slice_late(t):
-        win = NB + 128 * t; last = []
-        ts(c4("m4"), ap("dla", 7, 32, 8), OFG, 0.0, OP.subtract, OP.is_gt)
-        for k in range(4): ts(ap("wtf", k * 128, k * 128 + 128), ap("wt", k * 128, k * 128 + 128), ap("m4", k, k + 1), None, OP.mult)
-        for k in range(4):
-            w = ap("wtf", k * 128, k * 128 + 128)
-            last = [mm([(ap("pd0a", 32 * k, 128), w, ap("emat", c * 128 + 32 * k, c * 128 + 128), c == 0, c == 7) for c in (k, k + 4)], after=last)]
-        tt(ap("okh", 0, 128), ap("pd0a", 0, 128), ap("thi", 0, 128), OP.is_ge)
-        tt(f64("okl"), ap("pd0a", 0, 128, 2), f64("lo"), OP.is_lt)
-        tt(ap("okh", 0, 128, 2), ap("okh", 0, 128, 2), f64("okl"), OP.max)
-        scan(ap("bad", 0, 128), ap("seg4", 0, 128), ap("okh", 0, 128), OP.mult, OP.max)
-        scan(ap("ds", 0, 32), ap("dp", 0, 32), ap("bad", 3, 128, 4), OP.add, OP.max)
-        for w in range(2): tt(c4("tl", 4 * w), ap("ds", 7, 32, 8), c4("nmo", 4 * w), OP.add)
-        tt(e8("tl"), e8("tl"), e8("dump8"), OP.min)
-        ts(e8("tlu"), e8("tl"), 8192.0, None, OP.mult)
-        ts(ap("fl", 0, 32), ap("bad", 3, 128, 4), -1.0, 1.0, OP.mult, OP.add)
-        rb = ap("cfa", 128, 192)
-        ts(f64("ub"), f64("kr"), X1, None, OP.is_lt)
-        tt(ap("mn", 1, 128, 2), rb, f64("ub"), OP.mult)
-        tt(ap("val", 64, 128), rb, ap("mn", 1, 128, 2), OP.subtract)
-        cp(ap("C", 0, NW + 128, ind=e8("tlu")), ap("val", 0, 128))
-        for q in range(4): tt(ap("C", win + q, win + 128, 4), ap("mn", q, 128, 4), ap("fl", 0, 32), OP.mult)
+        win = NB + 128 * t; rb = f64("cf", 64)
+        for c in range(4):
+            w = ap("wtf", c * 128, c * 128 + 128); n = 136 + 17 * c + 16; o = ap("sca", 128 + 32 * c, 256)
+            ts(w, ap("boB", 0, 128), ap("wa", n, n + 1), ap("wc", c, c + 1), OP.mult, OP.min)
+            mm([(o, w, ap("emat", 160 * c, 128 * c + 128), c == 0, False), (ap("sca", 128 + 32 * c, 160 + 32 * c), w, ap("dg", 0, 32), False, False),
+                (o, w, ap("emat", 512 + 160 * c, 512 + 128 * c + 128), False, c == 3)])
+        tt(ap("good", 0, 128), ap("sca", 128, 256), ap("thm", 0, 128), OP.is_lt)
+        scan(ap("gd", 0, 128), ap("seg", 0, 128), ap("good", 0, 128), OP.max, OP.min)
+        for c in range(4): ts(ap("tlu", c, 8, 4), ap("nd", c, 8, 4), ap("gd", 32 * c + 31, 32 * c + 32), ap("dump", c, c + 1), OP.mult, OP.add)
+        tt(f64("val", 64), ap("tb", 0, 16, ind=c4("ku")), rb, OP.mult)
+        for w in range(2): cp(ap("C", 0, NW + 64, ind=c4("tlu", 4 * w)), f64("val", 64 * w))
+        tt(f64("mn", 64), rb, f64("val", 64), OP.subtract)
+        cp(c4("gu"), ap("gd", 31, 128, 32))
+        for w in range(2): tt(ap("C", win + w, win + 128, 2), ap("iot", 0, 8, ind=c4("gu")), f64("mn", 64 * w), OP.mult)
         if t < NV - 1:
-            add("V", lambda g, T: g.vector.tensor_reduce(T.cnt[:], T.fl[:], AxisListType.X, OP.add), (ap("fl", 0, 32),), (ap("cnt", 0, 1),), 0.09)
-            mm([(ap("pd0a", 128, 129), ap("cm", 0, 128), ap("cnt", 0, 1), True, True)], True)
-            cp(ap("zi", 0, 1), ap("pd0a", 128, 129))
+            cp(c4("gh"), ap("gd", 31, 128, 32))
+            mm([(ap("sca", 256, 257), ap("ones", 0, 128), ap("gh", c, c + 1), c == 0, c == 3) for c in range(4)])
+            cp(ap("zi", 0, 1), ap("sca", 256, 257))
             ts(ap("zi", 1, 2), ap("zi", 0, 1), 63, None, OP.bitwise_and)
-            ts(ap("tc", 0, 1), ap("zi", 1, 2), TH, None, OP.add)
-            ts(a64("d0t"), a64("m0"), a64("tc", 0, 1), None, OP.mult)
+            ts(ap("tc", 0, 1), ap("zi", 1, 2), TH + OFF, None, OP.add)
 
     for t in range(NV):
-        qn = ap("QS", (t + 1) * 128, (t + 2) * 128); hn = ap("HS", (t + 1) * 64, (t + 2) * 64)
+        qn = ap("QP", (t + 1) * 128, (t + 2) * 128); hn = ap("HS", (t + 1) * 72, (t + 2) * 72)
         if t < NV - 1:
-            qsent = send(qn, ap("QS", t * 128, t * 128 + 128), "aq%d" % (t + 1))
-            hsent = send(hn, ap("HS", t * 64, t * 64 + 64), "ah%d" % (t + 1))
-        P = {}; yq = 2048 * (t % 2)
+            qsent = send(qn, ap("QP", t * 128, t * 128 + 128), "aq%d" % (t + 1))
+            hsent = send(hn, ap("HS", t * 72, t * 72 + 72), "ah%d" % (t + 1))
+        P = {}
         for hi in range(2):
-            h = "ab"[hi]; b = t * 128 + hi * 64; P[h] = ap("PS", b, b + 64)
-            act(ap("yq" + h, yq + 1, yq + 2048, 2), ap("QS", b, b + 64, ind=ap("rep", 0, 64)), AF.Copy)
-            mm([(a64("sc" + h, 256, 384), P[h], ap("eye", 0, 128), True, True)])
-            PT[h] = act(a64("pt" + h, 0, 128), a64("sc" + h, 256, 384), AF.Copy)
+            h = "ab"[hi]; b = t * 256 + hi * 128; P[h] = a64("PS", b, b + 128); qr = YW * (t % 2)
+            cp(ap("qz" + h, 0, YW, 17), f64("QP", t * 128 + hi * 64))
+            scan(ap("qr" + h, qr, qr + YW), ap("hold", 0, YW), ap("qz" + h, 0, YW), OP.mult, OP.max)
+            ts(ap("d0" + h, 1, 68, 17), c4("HS", t * 72 + 64 + hi * 4), -1.0, ap("tc", 0, 1), OP.mult, OP.add)
         if t < NV - 1:
             recv(qn, "aq%d" % (t + 1), qsent); recv(hn, "ah%d" % (t + 1), hsent)
         for s in range(3):
             for h in "ab": P[h] = step(t, s, h, P[h])
             if s == 1: slice_early(t)
-        on = [(ap("PS", (t + 1) * 128 + k * 64, (t + 1) * 128 + k * 64 + 64), "a%s%d" % ("ab"[k], t + 1)) for k in range(2)]
-        sent = [send(on[k][0], P["ab"[k]], on[k][1]) for k in range(2)]
+        on = []
+        for hi in range(2):
+            b = t * 256 + hi * 128; sem = "a%s%d" % ("ab"[hi], t + 1)
+            if t < NV - 1: on.append((ap("PS", b + 256, b + 384), sem, ap("PO", b, b + 128)))
+            else: on.append((f64("PF", 64 * hi), sem, P["ab"[hi]]))
+        sent = [send(o, a, sem) for o, sem, a in on]
         slice_late(t)
         for k in range(2): recv(on[k][0], on[k][1], sent[k])
     cp(ap("C", 0, 1), ap("chi", 0, 1))
-    dma(ap("yp", 0, 128), ap("PS", 1024, 1152), "stp", 2)
     for i in range(4): dma(ap("yc", i * 896, (i + 1) * 896), ap("C", i * 896, (i + 1) * 896), "st%d" % i, 5)
+    for hi in range(2): dma(f64("yp", 64 * hi), f64("PF", 64 * hi), "sp" + "ab"[hi], 2)
     return ops
 
 
@@ -374,6 +365,9 @@ def plan(ops):
             old[:] = [e for e in old if not (lo <= e[2] and e[3] <= hi)] + [(o["i"], True, lo, hi)]
         for (n, lo, hi) in o["rd"]: hist.setdefault(n, []).append((o["i"], False, lo, hi))
     succ = [[] for _ in ops]; left = [len(o["dep"]) for o in ops]; pri = [0.0] * m
+    def free_of_wait(p, o):
+        kind = o["dep"][p["i"]]
+        return p["eng"] == o["eng"] != "Y" and (kind in ("bank", "ord") or (o["eng"] == "P" and kind == "waw"))
     for o in ops:
         for q in o["dep"]: succ[q].append(o["i"])
     for o in reversed(ops): pri[o["i"]] = o["cost"] + o["lag"] + LAT + max([pri[x] for x in succ[o["i"]]] or [0.0])
@@ -389,11 +383,11 @@ def plan(ops):
             st = max(free[e], est[i])
             if best is None or (st, -pri[i]) < best[0]: best = ((st, -pri[i]), st, e, i)
         _, st, e, i = best
-        ready.discard(i); ops[i]["q"] = e; order[e].append(i)
+        ready.discard(i); ops[i]["st"] = st; order[e].append(i)
         free[e] = st + ops[i]["cost"] if e != "R" else 0.0
         fin[i] = st + ops[i]["cost"] + ops[i]["lag"]
         for x in succ[i]:
-            est[x] = max(est[x], fin[i] + LAT); left[x] -= 1
+            est[x] = max(est[x], fin[i] + (0.0 if free_of_wait(ops[i], ops[x]) else LAT)); left[x] -= 1
             if left[x] == 0: ready.add(x)
     cnt = {e: 0 for e in order}
     for e in order:
@@ -409,9 +403,8 @@ def plan(ops):
                 if any(q not in at for q in o["dep"]): break
                 w = []
                 for q in sorted(o["dep"], key=lambda q: -fin[q]):
-                    kind = o["dep"][q]; p = ops[q]
-                    if e == "R" or p["done"] == ("snd", 8): continue
-                    if p["q"] == e and e != "Y" and (kind in ("bank", "ord") or (e == "P" and kind == "waw")): continue
+                    p = ops[q]
+                    if e == "R" or p["done"] == ("snd", 8) or free_of_wait(p, o): continue
                     s, v = p["tgt"]
                     if known[e].get(s, 0) >= v: continue
                     w.append((s, v))

@@ -4,34 +4,38 @@ OP = AluOpType
 AF = ActivationFunctionType
 N, NB, NV = 8, 2560, 8
 NW = NB + 128 * NV
-FAR, OFF, TH = 1024.0, 4096.0, 1235 + 31 / 32
+FAR, OFF, TH = 1024.0, 4096.0, 1235.0
+BIAS = {"a": 0.0, "b": -0.5, None: 0.0}
 CHUNKS = ((0, 6), (6, 12), (12, 16))
-KV = 32
+KV = {"a": (34, 34, 34), "b": (34, 34, 34)}
 PFIRST = True
+NOWAIT = ("bank", "ord")
 LOADS = 4
 YW = 64 * 17
-F, H, I, U = "float32", "bfloat16", "int32", "uint16"
+F, H, Q, I, U = "float32", "bfloat16", "float16", "int32", "uint16"
+MID = 1792.0
 SCRATCH = {}
 for _t, _n, _names in (
         (I, NB, "chi"), (F, NW + 64, "C"), (H, NW, "Ks Kp"), (H, 1024, "QP emat"), (U, 576, "HS"), (H, 2048, "PS PO"),
         (I, 64, "hv32"), (H, 128, "QS PF eye ones boB good seg kqa kqb"), (F, 128, "gd"), (H, 4, "gh"), (H, 144, "Wy Wz"), (H, 256, "pta ptb"),
-        (H, 68, "c4k jrow dj dw nea neb uj uw"), (F, 68, "d0a d0b fa fb"), (F, 204, "wa wb"), (F, 512, "mt nn dm"), (H, 512, "wtf"),
+        (H, 68, "c4k jrow dj dw nea neb uj uw"), (F, 68, "fa fb"), (F, 204, "wa wb"), (F, 512, "mt nn"), (Q, 512, "dm"), (Q, 128, "onq"), (Q, 68, "mrow"), (H, 512, "wtf"),
         (H, 64, "n64"), (H, 32, "dg"), (F, 64, "pow4 quart zero oj oj1 au an"), (F, 48, "tb"),
         (F, 128, "gi thm pr nbr val mn cf"), (F, 32, "cols"), (I, 16, "coli"), (U, 64, "cta ctb"),
         (F, NW, "iot"), (F, 8, "nd"), (F, 4, "dump w4 ca wc"), (U, 4, "ju ku gu"), (U, 8, "tlu"),
-        (F, 1, "tc"), (I, 2, "zi"), (H, YW, "exn hold qza qzb ya yb za zb"), (H, 2 * YW, "qra qrb"), (U, 12, "la lb")):
+        (F, 16, "tc"), (U, 2, "zu"), (F, 576, "bnd"), (F, 272, "d0"), (H, YW, "exn ya yb za zb"), (H, 4 * YW, "qr"), (U, 12, "la lb")):
     for _b in _names.split(): SCRATCH[_b] = ("sbuf", [128, _n], _t)
 for _h in "ab":
     SCRATCH["kg" + _h] = ("sbuf", [128, 1024], H)
-    SCRATCH["cx" + _h] = ("sbuf", [128, 4, 32], F)
-    SCRATCH["tx" + _h] = ("sbuf", [128, 4, 34], F)
+    SCRATCH["cx" + _h] = ("sbuf", [128, 4, 32], Q)
+    SCRATCH["tx" + _h] = ("sbuf", [128, 4, 34], Q)
     for _b in ("sc", "mi"): SCRATCH[_b + _h] = ("psum", [128, 512], F)
     for _b in ("pd0", "pd1"): SCRATCH[_b + _h] = ("psum", [128, 30, 17], F)
 PSUM = {k for k, v in SCRATCH.items() if v[0] == "psum"}
 DMAS = ["ld%d" % i for i in range(LOADS)] + "ldk ldp ldq ldh st0 st1 st2 st3 spa spb".split()
-SEMAPHORES = ("v s pe gp snd".split() + DMAS + ["a%s%d" % (k, t) for k in "qh" for t in range(1, 8)]
-              + ["a%s%d" % (h, t) for h in "ab" for t in range(1, 9)])
-CY, PCY, LAT = 0.00083, 0.00042, 0.11
+ARRIVE = ["a%s%d" % (k, t) for k in "qh" for t in range(1, 8)] + ["a%s%d" % (h, t) for h in "ab" for t in range(1, 9)]
+SEMAPHORES = "v s pe gp snd".split() + DMAS + ARRIVE
+CY, PCY, LAT, SC = 0.00083, 0.00042, 0.18, 1.2
+AHEAD, URGENT, ROUNDS, FLY = 0.7, 3.0, 2, 3.0
 
 
 def ap(name, c0, c1, step=1, p=128, ind=None):
@@ -43,7 +47,11 @@ def a3(name, m0, m1, ms, c0, c1, part=(0, 4)):
 
 
 def toks(a):
-    return [(a[0],) + a[7]] + (toks(a[5]) if a[5] else [])
+    return [(a[0],) + a[7] + (a[3],)] + (toks(a[5]) if a[5] else [])
+
+
+def meet(a, b):
+    return a[0] < b[1] and b[0] < a[1] and (a[2] != b[2] or (a[0] - b[0]) % a[2] == 0)
 
 
 def res(T, a):
@@ -58,15 +66,15 @@ def ln(a):
 
 
 def two(*aps):
-    return all(SCRATCH[a[0]][2] in (H, U) for a in aps)
+    return all(SCRATCH[a[0]][2] in (H, Q, U) for a in aps)
 
 
 def build():
-    ops = []
+    ops = []; tag = [None]
 
     def add(eng, emit, rd, wr, cost, n=1, done=None, after=(), lag=0.0):
-        o = {"eng": eng, "emit": emit, "rd": [t for a in rd for t in toks(a)], "wr": [toks(a)[0] for a in wr], "cost": cost,
-             "n": n, "done": done, "after": list(after), "lag": lag, "i": len(ops)}
+        o = {"eng": eng, "emit": emit, "rd": [t for a in rd for t in toks(a)], "wr": [toks(a)[0] for a in wr], "cost": cost * (SC if n else 1),
+             "n": n, "done": done, "after": list(after), "lag": lag, "i": len(ops), "tag": tag[0]}
         for a in wr: o["rd"] += toks(a)[1:]
         ops.append(o)
         return o["i"]
@@ -95,7 +103,7 @@ def build():
         return add("V", lambda g, T: g.vector.tensor_tensor_scan(res(T, out), res(T, d0), res(T, d1), init, o1, o2), (d0, d1), (out,), vc(out, (), 0.5 if two(out, d0, d1) else 1))
 
     def turn(out, a):
-        return add("V", lambda g, T: g.vector.transpose(res(T, out), res(T, a)), (a,), (out,), vc(out, ()))
+        return add("V", lambda g, T: g.vector.transpose(res(T, out), res(T, a)), (a,), (out,), vc(out, (), 0.5 if two(out, a) else 1))
 
     def ms(out, x):
         return add("V", lambda g, T: g.vector.memset(res(T, out), x), (), (out,), vc(out, (), 0.5 if two(out) else 1))
@@ -109,7 +117,7 @@ def build():
     def mm(ml, f32=False, after=()):
         def emit(g, T):
             return [g.tensor.matmul(res(T, o), res(T, l), res(T, r), st, sp) for (o, l, r, st, sp) in ml]
-        c = sum(max(min(64, ln(m[1])), ln(m[2])) for m in ml) * (4 if f32 else 1) * PCY + 0.05
+        c = sum(max(min(64, ln(m[1])), ln(m[2])) for m in ml) * (4 if f32 else 1) * PCY + 0.01
         return add("P", emit, [m[k] for m in ml for k in (1, 2)], [m[0] for m in ml], c, n=len(ml), after=after)
 
     def iota(out, pat, base, cmul):
@@ -121,19 +129,22 @@ def build():
     def aff(a, pat, base):
         return add("G", lambda g, T: g.affine_select(res(T, a), res(T, a), pat, OP.is_equal, 0.0, base, 1), (a,), (a,), 0.2 + 2 * ln(a) * CY)
 
+    def gcp(out, a):
+        return add("G", lambda g, T: g.affine_select(res(T, out), res(T, a), [[0, ln(a)]], OP.is_equal, 0.0, 0, 0), (a,), (out,), 0.17 + 2 * ln(a) * CY)
+
     def dma(out, a, sem, lag):
         add("Y", lambda g, T: g.sync.dma_start(res(T, out), res(T, a)), [x for x in (a,) if x[0] in SCRATCH],
             [x for x in (out,) if x[0] in SCRATCH], 0.1, done=(sem, 16), lag=lag)
 
-    def send(out, a, sem):
+    def send(out, a, sem, after=()):
         def emit(g, T, core, topo):
             dst = T.cores[(T.rank_of(core) + 1) % N]
             rid, pid, _ = topo.addr(dst)
-            g.remote_dma(res(T, out), res(T, a), T.sem[sem], T.sem["snd"], pid, rid, sum(1 << x for x in topo.engines(core, dst)[:8]))
-        return add("G", emit, (a,), (), 0.8, n=0, done=("snd", 8))
+            g.remote_dma(res(T, out), res(T, a), T.sem[sem], T.sem["snd"], pid, rid, topo.mask(core, dst))
+        return add("G", emit, (a,), (), 0.8, n=0, done=("snd", 8), after=after)
 
     def recv(out, sem, sender):
-        return add("R", None, (), (out,), 0.0, n=0, done=(sem, 8), after=[sender], lag=2.5)
+        return add("R", None, (), (out,), 0.0, n=0, done=(sem, 8), after=[sender], lag=FLY)
 
     W4 = NB // LOADS
     dma(ap("hv32", 0, 64), ap("hv", 0, 64), "ldh", 2.2)
@@ -149,7 +160,7 @@ def build():
     f64 = lambda n, o=0: ap(n, o, o + 64)
     c4 = lambda n, o=0: ap(n, o, o + 4)
     eye = ap("eye", 0, 128)
-    X, GC, RH, EV, OD, WC, X2, X1, WM = [col(k) for k in range(9)]
+    X, GC, RH, EV, OD, WC, X2, X1, WM, C0 = [col(k) for k in range(10)]
     iota(ci(0), [[0, 1]], 0, 1)
     iota(ap("iot", 0, 144), [[1, 144]], 0, 0)
     ms(eye, 1.0)
@@ -161,6 +172,7 @@ def build():
     iota(ap("iot", 144, NW), [[1, NW - 144]], 144, 0)
     iota(ap("pr", 0, 128), [[0, 4], [1, 8], [0, 4]], 0, 0)
     iota(c4("dump"), [[16, 4]], NW, 0)
+    iota(ap("bnd", 0, 576), [[0, 9], [1, 64]], int(TH + OFF), 0)
     iota(ap("mt", 0, 512), [[128, 8], [4, 32], [-2, 2]], NB + 2, 0)
     iota(ap("nn", 0, 512), [[128, 8], [2, 64]], NB + 1, 0)
     ts(ci(1), ci(0), 15, None, OP.bitwise_and)
@@ -174,19 +186,19 @@ def build():
     ts(ap("Wz", 0, 144), ap("iot", 0, 144), WC, -2.0, OP.is_equal, OP.mult)
     ts(a64("n64", 0, 64), a64("eye", 0, 64), -1.0, None, OP.mult)
     for k in range(4): ts(ap("dm", 128 * k, 128 * k + 128), eye, (EV, OD)[k // 2], (1.0, -1.0)[k % 2], OP.mult, OP.mult)
-    ms(ap("ones", 0, 128), 1.0)
-    ms(s68("c4k"), OFF); ms(ap("c4k", 0, 68, 17), 0.0)
-    ts(s68("jrow"), s68("jrow"), 1 / 16, 0.0, OP.mult, OP.max)
+    ms(ap("ones", 0, 128), 1.0); ms(f64("zero"), 0.0)
+    cp(ap("onq", 0, 128), ap("ones", 0, 128))
+    ms(s68("c4k"), 0.0); ms(ap("c4k", 0, 68, 17), -MID); ms(end("c4k"), MID); cp(s68("mrow"), s68("c4k"))
+    ts(s68("jrow"), s68("jrow"), 1 / 16, -31 / 32, OP.mult, OP.add)
+    ms(ap("jrow", 0, 68, p=1), OFF); ms(ap("jrow", 0, 68, 17), 0.0)
     ms(s68("dj"), -1.0); ms(ap("dj", 0, 68, 17), 0.0); ms(end("dj"), 15.0)
-    ms(ap("hold", 0, YW), 1.0); ms(ap("hold", 0, YW, 17), 0.0)
+    ms(ap("d0", 0, 272), 0.0)
     for h in "ab":
-        ms(ap("qz" + h, 0, YW), 0.0); ms(s68("d0" + h), 0.0)
         for k in "01": ms(a3("pd" + k + h, 0, 30, 1, 0, 1), 0.0)
-        ms(a3("tx" + h, 0, 4, 1, 0, 1), 0.0); ms(a3("tx" + h, 0, 4, 1, 33, 34), 0.0)
+        for k in (0, 33): cp(a3("tx" + h, 0, 4, 1, k, k + 1), c4("zero"))
+        ms(ap("mi" + h, 128, 256), 0.0)
     ms(ap("tc", 0, 1), TH + OFF)
     ms(ap("PS", 0, 256), 0.0)
-    ms(ap("PO", 0, 2048), 0.0)
-    ms(ap("C", NB, NW + 64), 0.0)
     ts(ap("boB", 0, 128), ap("gi", 0, 128), GC, 2.0 ** 64, OP.is_equal, OP.mult)
     ts(X2, X, 2.0, None, OP.mult); ts(X1, X, -1.0, None, OP.add)
     ts(ap("dg", 0, 32), ap("iot", 0, 32), X2, -3.0, OP.is_equal, OP.mult)
@@ -195,7 +207,7 @@ def build():
     ts(ap("tb", 32, 48), ap("iot", 0, 16), X1, None, OP.is_equal)
     ms(ap("seg", 0, 128), 0.0); ms(ap("seg", 0, 128, 32), 1.0)
     ts(c4("dump"), c4("dump"), X, None, OP.add)
-    ms(f64("quart"), 0.25); ms(f64("zero"), 0.0)
+    ms(f64("quart"), 0.25)
     scan(f64("pow4"), f64("quart"), f64("zero"), OP.mult, OP.add, float(4.0 ** 32))
     ts(ap("thm", 0, 128, 2), f64("pow4"), -1.0, None, OP.mult)
     ts(ap("thm", 1, 128, 2), f64("pow4"), 2.0, None, OP.mult)
@@ -215,25 +227,28 @@ def build():
         o = c4("sc" + "ab"[hi])
         mm([(o, ap("Wy", 15 - m, 143 - m), c4("QP", 64 * hi + 4 * m), m == 0, m == 15) for m in range(16)])
         cp(c4("HS", 64 + 4 * hi), o)
-    for i in range(LOADS): cp(ap("C", i * W4, (i + 1) * W4), ap("chi", i * W4, (i + 1) * W4))
-    ms(ap("C", 0, 1), 0.0)
+    cp(C0, ap("chi", 0, 1)); ms(ap("chi", 0, 1), 0)
     ms(ap("Ks", 0, 1), FAR)
     ms(ap("Kp", 0, 1), 0.0)
     PT = {}
 
     def step(t, s, h, P):
-        hi = "ab".index(h); win = NB + 128 * t; qr = YW * (t % 2)
+        hi = "ab".index(h); win = NB + 128 * t; qr = YW * (2 * (t % 2) + hi)
         L = c4("l" + h, 4 * s - 4) if s else c4("HS", t * 80 + hi * 4)
-        kids = ap("C", 0, win if s else NB, ind=L); S = s68("sc" + h); D = s68("mi" + h); W = 68 * s
+        kids = ap("C" if t else "chi", 0, win if s else NB, ind=L); S = s68("sc" + h); D = s68("mi" + h); W = 68 * s
         cp(f64("ct" + h), kids)
-        cp(ap("kg" + h, 0, 16 * KV), ap("Ks", 0, win, ind=ap("ct" + h, 0, KV)))
-        act(ap("kg" + h, 16 * KV, 1024), ap("Ks", 0, win, ind=ap("ct" + h, KV, 64)), AF.Copy, after=[PT[h]] if s and PFIRST else [])
-        ts(a3("cx" + h, 0, 4, 1, 0, 16, (0, 1)), f64("ct" + h), EV, None, OP.mult)
-        ts(a3("cx" + h, 0, 4, 1, 16, 32, (1, 2)), f64("ct" + h), OD, None, OP.mult)
-        if h == "a" and s: act(f64("cf", 64 * s - 64), kids, AF.Copy)
+        kv = KV[h][s]
+        cp(ap("kg" + h, 0, 16 * kv), ap("Ks", 0, win, ind=ap("ct" + h, 0, kv)))
+        act(ap("kg" + h, 16 * kv, 1024), ap("Ks", 0, win, ind=ap("ct" + h, kv, 64)), AF.Copy, after=[PT[h]] if s and PFIRST else [])
+        ts(a3("cx" + h, 0, 4, 1, 0, 16, (0, 1)), f64("ct" + h), MID, EV, OP.subtract, OP.mult)
+        ts(a3("cx" + h, 0, 4, 1, 16, 32, (1, 2)), f64("ct" + h), MID, OD, OP.subtract, OP.mult)
+        if h == "a" and s:
+            if t: act(f64("cf", 64 * s - 64), kids, AF.Copy)
+            else: cp(f64("cf", 64 * s - 64), f64("ct" + h))
         turn(a3("tx" + h, 0, 4, 1, 1, 33), a3("cx" + h, 0, 4, 1, 0, 32))
-        mm([(D, ap("dm", 128 * k, 128 * k + 128), a3("tx" + h, 0, 4, 1, o, o + 17), k == 0, k == 3) for k, o in enumerate((0, 1, 16, 17))], True)
-        mm([(S, ap("ones", 0, 128, p=1), ap(r, 0, 68, p=1), r == "c4k", False) for r in ("c4k", "jrow")])
+        mm([(D, ap("onq", 0, 128, p=1), ap("mrow", 0, 68, p=1), True, False)]
+           + [(D, ap("dm", 128 * k, 128 * k + 128), a3("tx" + h, 0, 4, 1, o, o + 17), False, k == 3) for k, o in enumerate((0, 1, 16, 17))])
+        mm([(S, ap("ones", 0, 128, p=2), ap("jrow", 0, 68, p=2), True, False)])
         for c, (m0, m1) in enumerate(CHUNKS):
             c0, c1 = 68 * m0, 68 * m1; pd = "pd%d" % (c % 2) + h; n = 4 * (m1 - m0); d = a3(pd, 0, n, 1, 0, 17)
             dk = a3(pd, 0, n, 1, 1, 17); ex = a64("exn", 64 * m0, 64 * m1)
@@ -242,10 +257,10 @@ def build():
             if not s: mm([(dk, P, ex, False, True)])
             act(ap("y" + h, c0, c1), d, AF.Abs)
             mm([(S, ap("Wy", 15 - m, 143 - m), s68("y" + h, 68 * m), False, False) for m in range(m0, m1)])
-            scan(ap("z" + h, c0, c1), ap("qr" + h, qr + c0, qr + c1), ap("y" + h, c0, c1), OP.max, OP.min)
+            scan(ap("z" + h, c0, c1), ap("qr", qr + c0, qr + c1), ap("y" + h, c0, c1), OP.max, OP.min)
             mm([(S, ap("Wz", 15 - m, 143 - m), s68("z" + h, 68 * m), False, m == 15) for m in range(m0, m1)])
         ne = s68("ne" + h)
-        scan(s68("f" + h), s68("d0" + h), S, OP.max, OP.min)
+        scan(s68("f" + h), s68("d0", 136 * (t % 2) + 68 * hi), S, OP.max, OP.min)
         tt(ne, S, s68("f" + h), OP.not_equal)
         scan(s68("w" + h, W), ne, D, OP.mult, OP.add)
         Ln = c4("l" + h, 4 * s)
@@ -262,7 +277,8 @@ def build():
             mm([(o, a64("n64", 0, 64), P, True, False)])
             act(kq, ap("Kp", 0, win, ind=Ln), AF.Copy)
             mm([(o, kq, eye, False, True)])
-        PT[h] = act(Pn, o, AF.Abs)
+        if Pn[0] == "PO": act(ap(*Pn[:3]), ap(*o[:3]), AF.Abs)
+        else: PT[h] = act(Pn, o, AF.Abs)
         if h == "a" and s < 2: act(ap("nbr", s, 128, 2), ap("iot", 0, win, ind=Ln), AF.Copy)
         if h == "a" and s:
             scan(s68("uj"), ne, s68("dj"), OP.mult, OP.add)
@@ -285,7 +301,7 @@ def build():
         tt(f64("au"), ra, f64("an"), OP.subtract)
         tt(f64("oj"), ap("tb", 16, 32, ind=c4("ju")), f64("nn", 64 * t), OP.mult)
         tt(f64("mn"), f64("au"), f64("oj"), OP.add)
-        if t < NV - 1: cp(ap("Kp", win, win + 128), ap("Ks", win, win + 128))
+        if t < NV - 1: gcp(ap("Kp", win, win + 128), ap("Ks", win, win + 128))
 
     def slice_late(t):
         win = NB + 128 * t; rb = f64("cf", 64)
@@ -303,28 +319,35 @@ def build():
         cp(c4("gu"), ap("gd", 31, 128, 32))
         for w in range(2): tt(ap("C", win + w, win + 128, 2), ap("iot", 0, 8, ind=c4("gu")), f64("mn", 64 * w), OP.mult)
         if t < NV - 1:
-            cp(c4("gh"), ap("gd", 31, 128, 32))
+            act(c4("gh"), ap("gd", 31, 128, 32), AF.Copy)
             mm([(ap("sca", 256, 257), ap("ones", 0, 128), ap("gh", c, c + 1), c == 0, c == 3) for c in range(4)])
-            cp(ap("zi", 0, 1), ap("sca", 256, 257))
-            ts(ap("zi", 1, 2), ap("zi", 0, 1), 63, None, OP.bitwise_and)
-            ts(ap("tc", 0, 1), ap("zi", 1, 2), TH + OFF, None, OP.add)
+            cp(ap("zu", 0, 1), ap("sca", 256, 257))
+            act(ap("tc", 0, 16), ap("bnd", 0, 576, ind=ap("zu", 0, 1)), AF.Copy)
 
+    sent = []
     for t in range(NV):
         qn = ap("QP", (t + 1) * 128, (t + 2) * 128); hn = ap("HS", (t + 1) * 72, (t + 2) * 72)
         if t < NV - 1:
-            qsent = send(qn, ap("QP", t * 128, t * 128 + 128), "aq%d" % (t + 1))
-            hsent = send(hn, ap("HS", t * 72, t * 72 + 72), "ah%d" % (t + 1))
+            qsent = send(qn, ap("QP", t * 128, t * 128 + 128), "aq%d" % (t + 1), sent)
+            hsent = send(hn, ap("HS", t * 72, t * 72 + 72), "ah%d" % (t + 1), sent)
         P = {}
+        qr = 2 * YW * (t % 2)
         for hi in range(2):
-            h = "ab"[hi]; b = t * 256 + hi * 128; P[h] = a64("PS", b, b + 128); qr = YW * (t % 2)
-            cp(ap("qz" + h, 0, YW, 17), f64("QP", t * 128 + hi * 64))
-            scan(ap("qr" + h, qr, qr + YW), ap("hold", 0, YW), ap("qz" + h, 0, YW), OP.mult, OP.max)
-            ts(ap("d0" + h, 1, 68, 17), c4("HS", t * 72 + 64 + hi * 4), -1.0, ap("tc", 0, 1), OP.mult, OP.add)
+            b = t * 256 + hi * 128; P["ab"[hi]] = a64("PS", b, b + 128)
+            if t == 0:
+                for j in range(17): cp(ap("qr", hi * YW + j, hi * YW + YW, 17), f64("QP", hi * 64))
+        if t:
+            for j in range(1 if t > 1 else 0, 17): gcp(ap("qr", qr + j, qr + 2 * YW, 17), ap("QP", t * 128, t * 128 + 128))
+        d0 = 136 * (t % 2)
+        ts(ap("d0", d0 + 1, d0 + 136, 17), ap("HS", t * 72 + 64, t * 72 + 72), -1.0, ap("tc", 0, 1), OP.mult, OP.add)
         if t < NV - 1:
             recv(qn, "aq%d" % (t + 1), qsent); recv(hn, "ah%d" % (t + 1), hsent)
         for s in range(3):
-            for h in "ab": P[h] = step(t, s, h, P[h])
+            for h in "ab":
+                tag[0] = h; P[h] = step(t, s, h, P[h]); tag[0] = None
             if s == 1: slice_early(t)
+        if t == 0:
+            for i in range(8): cp(ap("C", i * 320, (i + 1) * 320), ap("chi", i * 320, (i + 1) * 320))
         on = []
         for hi in range(2):
             b = t * 256 + hi * 128; sem = "a%s%d" % ("ab"[hi], t + 1)
@@ -333,7 +356,7 @@ def build():
         sent = [send(o, a, sem) for o, sem, a in on]
         slice_late(t)
         for k in range(2): recv(on[k][0], on[k][1], sent[k])
-    cp(ap("C", 0, 1), ap("chi", 0, 1))
+    cp(ap("C", 0, 1), C0)
     for i in range(4): dma(ap("yc", i * 896, (i + 1) * 896), ap("C", i * 896, (i + 1) * 896), "st%d" % i, 5)
     for hi in range(2): dma(f64("yp", 64 * hi), f64("PF", 64 * hi), "sp" + "ab"[hi], 2)
     return ops
@@ -343,14 +366,12 @@ def plan(ops):
     hist = {}; runs = {}; m = len(ops)
     for o in ops:
         dep = {}
-        for (n, lo, hi) in o["rd"]:
-            for (q, w, l2, h2) in hist.get(n, ()):
-                if w and l2 < hi and lo < h2: dep[q] = "raw"
-        for (n, lo, hi) in o["wr"]:
-            for (q, w, l2, h2) in hist.get(n, ()):
-                if l2 < hi and lo < h2:
-                    if w: dep.setdefault(q, "waw")
-                    else: dep.setdefault(q, "war")
+        for x in o["rd"]:
+            for (q, w, y) in hist.get(x[0], ()):
+                if w and meet(x[1:], y): dep[q] = "raw"
+        for x in o["wr"]:
+            for (q, w, y) in hist.get(x[0], ()):
+                if meet(x[1:], y): dep.setdefault(q, "waw" if w else "war")
         for q in o["after"]: dep.setdefault(q, "ord")
         for n in {x[0] for x in o["rd"] + o["wr"]} & PSUM:
             r = runs.setdefault(n, [])
@@ -360,17 +381,18 @@ def plan(ops):
             r[-1][1].append(o["i"])
         dep.pop(o["i"], None)
         o["dep"] = dep
-        for (n, lo, hi) in o["wr"]:
+        for (n, lo, hi, st) in o["wr"]:
             old = hist.setdefault(n, [])
-            old[:] = [e for e in old if not (lo <= e[2] and e[3] <= hi)] + [(o["i"], True, lo, hi)]
-        for (n, lo, hi) in o["rd"]: hist.setdefault(n, []).append((o["i"], False, lo, hi))
+            old[:] = [e for e in old if not (lo <= e[2][0] and e[2][1] <= hi and (st == 1 or e[2] == (lo, hi, st)))] + [(o["i"], True, (lo, hi, st))]
+        for x in o["rd"]: hist.setdefault(x[0], []).append((o["i"], False, x[1:]))
     succ = [[] for _ in ops]; left = [len(o["dep"]) for o in ops]; pri = [0.0] * m
     def free_of_wait(p, o):
         kind = o["dep"][p["i"]]
-        return p["eng"] == o["eng"] != "Y" and (kind in ("bank", "ord") or (o["eng"] == "P" and kind == "waw"))
+        return p["eng"] == o["eng"] != "Y" and (kind in NOWAIT or (o["eng"] == "P" and kind == "waw"))
     for o in ops:
         for q in o["dep"]: succ[q].append(o["i"])
     for o in reversed(ops): pri[o["i"]] = o["cost"] + o["lag"] + LAT + max([pri[x] for x in succ[o["i"]]] or [0.0])
+    for o in ops: pri[o["i"]] += BIAS[o["tag"]]
     order = {e: [] for e in "VSPGYR"}; free = {e: 0.0 for e in order}
     ready = {i for i in range(m) if left[i] == 0}; est = [0.0] * m; fin = [0.0] * m
     while ready:
@@ -380,6 +402,9 @@ def plan(ops):
             if not cand: continue
             now = [i for i in cand if est[i] <= free[e]]
             i = max(now, key=lambda x: (pri[x], -x)) if now else min(cand, key=lambda x: (est[x], -pri[x], x))
+            t0 = max(free[e], est[i])
+            soon = [x for x in cand if t0 < est[x] < t0 + AHEAD * ops[i]["cost"] and pri[x] - pri[i] > URGENT * (est[x] - t0 + ops[x]["cost"])]
+            if soon: i = max(soon, key=lambda x: (pri[x], -x))
             st = max(free[e], est[i])
             if best is None or (st, -pri[i]) < best[0]: best = ((st, -pri[i]), st, e, i)
         _, st, e, i = best
@@ -389,6 +414,27 @@ def plan(ops):
         for x in succ[i]:
             est[x] = max(est[x], fin[i] + (0.0 if free_of_wait(ops[i], ops[x]) else LAT)); left[x] -= 1
             if left[x] == 0: ready.add(x)
+    gap = lambda q, x: ops[q]["lag"] + (0.0 if free_of_wait(ops[q], ops[x]) else LAT)
+    back = [[(x, gap(o["i"], x)) for x in succ[o["i"]]] for o in ops]; fore = [[(q, gap(q, o["i"])) for q in o["dep"]] for o in ops]
+    def pack(seq, before, head):
+        end = [0.0] * m; busy = {e: [] for e in order}
+        for i in seq:
+            c = ops[i]["cost"]; t = max([end[q] + d for q, d in before[i]] + [head[i]]); b = busy[ops[i]["eng"]]
+            if c:
+                k = len(b)
+                while k and b[k - 1][1] > t: k -= 1
+                while k < len(b) and b[k][0] < t + c: t = max(t, b[k][1]); k += 1
+                b.insert(k, (t, t + c))
+            end[i] = t + c
+        return end
+    span = lambda end: max(end[i] + ops[i]["lag"] for i in range(m))
+    end = [fin[i] - ops[i]["lag"] for i in range(m)]; top = end
+    for _ in range(ROUNDS):
+        r = pack(sorted(range(m), key=lambda i: (-end[i] - ops[i]["lag"], -i)), back, [o["lag"] for o in ops])
+        end = pack(sorted(range(m), key=lambda i: (-r[i], i)), fore, [0.0] * m)
+        if span(end) < span(top): top = end
+    for o in ops: o["st"] = top[o["i"]] - o["cost"]; fin[o["i"]] = top[o["i"]] + o["lag"]
+    for e in order: order[e].sort(key=lambda i: (ops[i]["st"], i))
     cnt = {e: 0 for e in order}
     for e in order:
         for i in order[e]:
@@ -425,13 +471,14 @@ def rank_program(g, core, T, topo):
         MEMO["o"] = build(); MEMO["p"] = plan(MEMO["o"])
     ops = MEMO["o"]; order, waits, cnt, _ = MEMO["p"]
     queue = {"V": g.vector, "S": g.scalar, "P": g.tensor, "G": g, "Y": g.sync}
-    sent = 0
+    sent = 0; r = T.rank_of(core)
+    into = len(topo.engines(T.cores[(r - 1) % N], core)); out = len(topo.engines(core, T.cores[(r + 1) % N]))
     for e in "YVSPG":
         for i in order[e]:
             o = ops[i]
-            for s, v in waits[i]: queue[e].wait_ge(T.sem[s], v)
+            for s, v in waits[i]: queue[e].wait_ge(T.sem[s], into if s in ARRIVE else v)
             if o["done"] == ("snd", 8):
-                o["emit"](g, T, core, topo); sent += 8
+                o["emit"](g, T, core, topo); sent += out
             elif o["done"]: o["emit"](g, T).then_inc(T.sem[o["done"][0]], 16)
             else:
                 r = o["emit"](g, T)

@@ -1,3 +1,4 @@
+from concourse.bass import DstId, RemoteDMATransfer
 from concourse.mybir import dt, AluOpType, AxisListType, ActivationFunctionType
 
 OP = AluOpType
@@ -5,10 +6,14 @@ AF = ActivationFunctionType
 N, NB, NV = 8, 2560, 8
 NW = NB + 128 * NV
 FAR, OFF, TH = 1024.0, 4096.0, 1235.0
-BIAS = {"a": 0.0, "b": -0.5, None: 0.0}
-CHUNKS = ((0, 6), (6, 12), (12, 16))
-KV = {"a": (34, 34, 34), "b": (34, 34, 34)}
-PFIRST = True
+BIAS = {("Y", "QS", None): 10.0, ("Y", "hv32", None): 9.0, ("V", "QP", None): 4.0, ("S", "qr", None): 3.0}
+CHUNKS = ((0, 5), (5, 11), (11, 16))
+KV = {"a": (32, 34, 32), "b": (32, 34, 32)}
+CF, EACH, VABS = "V", 0.0, ()
+TURNS = (("a", 0), ("b", 0), ("a", 1), ("b", 1), ("a", 2), ("b", 2))
+K32 = False
+PFIRST, KS, KQ, PMM, KW = True, 12, "SSS", 0, 10
+ALT = {"a": (3, 1, 1), "b": (1, 1, 3)}
 NOWAIT = ("bank", "ord")
 LOADS = 4
 YW = 64 * 17
@@ -16,34 +21,34 @@ F, H, Q, I, U = "float32", "bfloat16", "float16", "int32", "uint16"
 MID = 1792.0
 SCRATCH = {}
 for _t, _n, _names in (
-        (I, NB, "chi"), (F, NW + 64, "C"), (H, NW, "Ks Kp"), (H, 1024, "QP emat"), (U, 576, "HS"), (H, 2048, "PS PO"),
-        (I, 64, "hv32"), (H, 128, "QS PF eye ones boB good seg kqa kqb"), (F, 128, "gd"), (H, 4, "gh"), (H, 144, "Wy Wz"), (H, 256, "pta ptb"),
-        (H, 68, "c4k jrow dj dw nea neb uj uw"), (F, 68, "fa fb"), (F, 204, "wa wb"), (F, 512, "mt nn"), (Q, 512, "dm"), (Q, 128, "onq"), (Q, 68, "mrow"), (H, 512, "wtf"),
-        (H, 64, "n64"), (H, 32, "dg"), (F, 64, "pow4 quart zero oj oj1 au an"), (F, 48, "tb"),
-        (F, 128, "gi thm pr nbr val mn cf"), (F, 32, "cols"), (I, 16, "coli"), (U, 64, "cta ctb"),
-        (F, NW, "iot"), (F, 8, "nd"), (F, 4, "dump w4 ca wc"), (U, 4, "ju ku gu"), (U, 8, "tlu"),
-        (F, 16, "tc"), (U, 2, "zu"), (F, 576, "bnd"), (F, 272, "d0"), (H, YW, "exn ya yb za zb"), (H, 4 * YW, "qr"), (U, 12, "la lb")):
+        (I, NB, "chi"), (F, NW + 64, "C"), (H, NW, "Ks Kp"), (H, 1024, "QP emat"), (U, 1024, "HS"), (H, 2048, "PS PO"),
+        (I, 64, "hv32"), (H, 128, "QS PF eye ones half boB good seg kqa kqb"), (F, 128, "gd"), (H, 4, "gh"), (H, 144, "Wy Wz"), (H, 256, "pta ptb"),
+        (H, 68, "c4k jrow dj dw nea neb uw"), (F, 68, "fa fb"), (F, 340, "wa wb"), (F, 512, "mt"), (Q, 512, "dm"), (Q, 128, "onq"), (Q, 68, "mrow"), (H, 512, "wtf"),
+        (H, 64, "n64"), (H, 32, "dg"), (F, 64, "pow4 quart zero oj oj1 au an"), (F, 32, "tb"),
+        (F, 128, "gi thm pr nbr val cf"), (F, 32, "cols"), (I, 16, "coli"), (U, 64, "cta ctb"),
+        (F, NW, "iot"), (F, 16, "nd dback"), (F, 4, "dump w4 ca wc"), (U, 4, "ju ku"), (U, 16, "tlu"), (F, 160, "tz"),
+        (F, 16, "tc"), (U, 2, "zu"), (F, 288, "bnd"), (F, 272, "d0"), (H, YW, "exn ya yb za zb"), (H, 4 * YW, "qr"), (U, 12, "la lb")):
     for _b in _names.split(): SCRATCH[_b] = ("sbuf", [128, _n], _t)
 for _h in "ab":
     SCRATCH["kg" + _h] = ("sbuf", [128, 1024], H)
     SCRATCH["cx" + _h] = ("sbuf", [128, 4, 32], Q)
     SCRATCH["tx" + _h] = ("sbuf", [128, 4, 34], Q)
-    for _b in ("sc", "mi"): SCRATCH[_b + _h] = ("psum", [128, 512], F)
-    for _b in ("pd0", "pd1"): SCRATCH[_b + _h] = ("psum", [128, 30, 17], F)
+    SCRATCH["sc" + _h] = ("psum", [128, 512], F)
+    for _b in ("pd0", "pd1", "pd2"): SCRATCH[_b + _h] = ("psum", [128, 30, 17], F)
 PSUM = {k for k, v in SCRATCH.items() if v[0] == "psum"}
 DMAS = ["ld%d" % i for i in range(LOADS)] + "ldk ldp ldq ldh st0 st1 st2 st3 spa spb".split()
-ARRIVE = ["a%s%d" % (k, t) for k in "qh" for t in range(1, 8)] + ["a%s%d" % (h, t) for h in "ab" for t in range(1, 9)]
-SEMAPHORES = "v s pe gp snd".split() + DMAS + ARRIVE
-CY, PCY, LAT, SC = 0.00083, 0.00042, 0.18, 1.2
-AHEAD, URGENT, ROUNDS, FLY = 0.7, 3.0, 2, 3.0
+ARRIVE = ["one"] + ["a%s%d" % (h, t) for h in "ab" for t in range(1, 9)]
+SEMAPHORES = "v s pe gp snd all".split() + DMAS + ARRIVE
+CY, PCY, LAT, SC = 0.00083, 0.00042, 0.27, 1.3
+AHEAD, URGENT, ROUNDS, FLY, STORE, GATHER = 0.4, 2.0, 2, 3.5, 5.0, 1.5
 
 
 def ap(name, c0, c1, step=1, p=128, ind=None):
     return (name, c0, c1, step, p, ind, None, (c0, c1))
 
 
-def a3(name, m0, m1, ms, c0, c1, part=(0, 4)):
-    return (name, c0, c1, 1, 128, None, (m0, m1, ms), part)
+def a3(name, m0, m1, ms, c0, c1, part=(0, 4), p=128):
+    return (name, c0, c1, 1, p, None, (m0, m1, ms), part)
 
 
 def toks(a):
@@ -55,8 +60,11 @@ def meet(a, b):
 
 
 def res(T, a):
-    if a[6]: return T[a[0]][0:128, a[6][0]:a[6][1]:a[6][2], a[1]:a[2]]
-    v = T[a[0]][0:a[4], a[1]:a[2]] if a[3] == 1 else T[a[0]][0:a[4], a[1]:a[2]:a[3]]
+    p0, p1 = a[4] if isinstance(a[4], tuple) else (0, a[4])
+    if len(SCRATCH.get(a[0], (0, ()))[1]) == 4: return T[a[0]][p0:p1, a[6][0]:a[6][1]:a[6][2], a[1]:a[2], 0]
+    if a[6] and a[6][1] - a[6][0] == 1: return T[a[0]][p0:p1, a[6][0], a[1]:a[2]]
+    if a[6]: return T[a[0]][p0:p1, a[6][0]:a[6][1]:a[6][2], a[1]:a[2]]
+    v = T[a[0]][p0:p1, a[1]:a[2]] if a[3] == 1 else T[a[0]][p0:p1, a[1]:a[2]:a[3]]
     return v.indirect(res(T, a[5])) if a[5] else v
 
 
@@ -69,12 +77,16 @@ def two(*aps):
     return all(SCRATCH[a[0]][2] in (H, Q, U) for a in aps)
 
 
+def shared(T, topo):
+    return [e for e in topo.engines(T.cores[0], T.cores[1]) if all(e in topo.engines(a, b) for a in T.cores for b in T.cores if a != b)]
+
+
 def build():
-    ops = []; tag = [None]
+    ops = []; tag = [None, None]
 
     def add(eng, emit, rd, wr, cost, n=1, done=None, after=(), lag=0.0):
         o = {"eng": eng, "emit": emit, "rd": [t for a in rd for t in toks(a)], "wr": [toks(a)[0] for a in wr], "cost": cost * (SC if n else 1),
-             "n": n, "done": done, "after": list(after), "lag": lag, "i": len(ops), "tag": tag[0]}
+             "n": n, "done": done, "after": list(after), "lag": lag, "i": len(ops), "tag": tag[0], "t": tag[1]}
         for a in wr: o["rd"] += toks(a)[1:]
         ops.append(o)
         return o["i"]
@@ -82,7 +94,7 @@ def build():
     def vc(out, ins, per=1.0):
         n = ln(out)
         if out[5]: return 0.06 + n * 3.8 * CY
-        if any(a[5] for a in ins): return 0.06 + n * 1.5 * CY
+        if any(a[5] for a in ins): return 0.06 + n * GATHER * CY
         return 0.02 + max(64, n * per) * CY
 
     def tt(out, a, b, op):
@@ -105,19 +117,23 @@ def build():
     def turn(out, a):
         return add("V", lambda g, T: g.vector.transpose(res(T, out), res(T, a)), (a,), (out,), vc(out, (), 0.5 if two(out, a) else 1))
 
+    def size(out, a):
+        emit = lambda g, T: g.vector.tensor_reduce(res(T, out), T[a[0]][0:128, a[6][0]:a[6][1], :, :], AxisListType.X, OP.max, apply_absolute_value=True)
+        return add("V", emit, (a,), (out,), vc(out, ()))
+
     def ms(out, x):
         return add("V", lambda g, T: g.vector.memset(res(T, out), x), (), (out,), vc(out, (), 0.5 if two(out) else 1))
 
     def act(out, a, func, scale=None, after=()):
         def emit(g, T):
-            if scale: return g.scalar.activation(res(T, out), res(T, a), func, scale=res(T, scale))
+            if scale: return g.scalar.activation(res(T, out), res(T, a), func, scale=scale)
             return g.scalar.activation(res(T, out), res(T, a), func)
-        return add("S", emit, (a, scale) if scale else (a,), (out,), 0.08 + ln(out) * (1.5 if a[5] else 1.0) * CY, after=after)
+        return add("S", emit, (a,), (out,), 0.08 + ln(out) * (GATHER if a[5] else 1.0) * CY, after=after)
 
     def mm(ml, f32=False, after=()):
         def emit(g, T):
             return [g.tensor.matmul(res(T, o), res(T, l), res(T, r), st, sp) for (o, l, r, st, sp) in ml]
-        c = sum(max(min(64, ln(m[1])), ln(m[2])) for m in ml) * (4 if f32 else 1) * PCY + 0.01
+        c = sum(max(min(64, ln(m[1])), ln(m[2])) for m in ml) * (4 if f32 else 1) * PCY + 0.01 + EACH * len(ml)
         return add("P", emit, [m[k] for m in ml for k in (1, 2)], [m[0] for m in ml], c, n=len(ml), after=after)
 
     def iota(out, pat, base, cmul):
@@ -129,8 +145,8 @@ def build():
     def aff(a, pat, base):
         return add("G", lambda g, T: g.affine_select(res(T, a), res(T, a), pat, OP.is_equal, 0.0, base, 1), (a,), (a,), 0.2 + 2 * ln(a) * CY)
 
-    def gcp(out, a):
-        return add("G", lambda g, T: g.affine_select(res(T, out), res(T, a), [[0, ln(a)]], OP.is_equal, 0.0, 0, 0), (a,), (out,), 0.17 + 2 * ln(a) * CY)
+    def gcp(out, a, after=()):
+        return add("G", lambda g, T: g.affine_select(res(T, out), res(T, a), [[0, ln(a)]], OP.is_equal, 0.0, 0, 0), (a,), (out,), 0.17 + 2 * ln(a) * CY, after=after)
 
     def dma(out, a, sem, lag):
         add("Y", lambda g, T: g.sync.dma_start(res(T, out), res(T, a)), [x for x in (a,) if x[0] in SCRATCH],
@@ -169,12 +185,11 @@ def build():
     aff(a64("exn", 0, 1024), [[-1, 16], [-16, 4], [0, 16]], 0)
     iota(s68("jrow"), [[0, 4], [1, 17]], -1, 0)
     iota(ap("gi", 0, 128), [[1, 8], [0, 16]], 0, 0)
-    iota(ap("iot", 144, NW), [[1, NW - 144]], 144, 0)
-    iota(ap("pr", 0, 128), [[0, 4], [1, 8], [0, 4]], 0, 0)
-    iota(c4("dump"), [[16, 4]], NW, 0)
-    iota(ap("bnd", 0, 576), [[0, 9], [1, 64]], int(TH + OFF), 0)
-    iota(ap("mt", 0, 512), [[128, 8], [4, 32], [-2, 2]], NB + 2, 0)
-    iota(ap("nn", 0, 512), [[128, 8], [2, 64]], NB + 1, 0)
+    numbers = [iota(ap("iot", c0, c1), [[1, c1 - c0]], c0, 0) for c0, c1 in ((144, 1280), (1280, NB), (NB, NW))]
+    iota(ap("dback", 0, 16), [[0, 4], [16, 4]], -64, 0)
+    numbers += [iota(ap("bnd", 0, 288), [[0, 9], [2, 32]], int(TH + OFF), 0),
+                iota(ap("mt", 0, 512), [[128, 8], [4, 32], [-2, 2]], NB + 2, 0)]
+    ms(ap("half", 0, 128), 0.5)
     ts(ci(1), ci(0), 15, None, OP.bitwise_and)
     ts(ci(2), ci(0), 4, None, OP.logical_shift_right)
     ts(ci(3), ci(1), 1, None, OP.logical_shift_right)
@@ -183,9 +198,14 @@ def build():
     ts(EV, OD, -1.0, 1.0, OP.mult, OP.add)
     ts(WC, GC, 16.0, 15.0, OP.mult, OP.add)
     ts(ap("Wy", 0, 144), ap("iot", 0, 144), WC, None, OP.is_equal)
-    ts(ap("Wz", 0, 144), ap("iot", 0, 144), WC, -2.0, OP.is_equal, OP.mult)
-    ts(a64("n64", 0, 64), a64("eye", 0, 64), -1.0, None, OP.mult)
-    for k in range(4): ts(ap("dm", 128 * k, 128 * k + 128), eye, (EV, OD)[k // 2], (1.0, -1.0)[k % 2], OP.mult, OP.mult)
+    act(ap("Wz", 0, 144), ap("Wy", 0, 144), AF.Copy, -2.0)
+    act(a64("n64", 0, 64), a64("eye", 0, 64), AF.Copy, -1.0)
+    if K32:
+        ts(X1, X, 1.0, None, OP.add)
+        ts(ap("pr", 0, 17), ap("iot", 0, 17), X1, None, OP.is_equal); ts(ap("pr", 32, 49), ap("iot", 0, 17), X, None, OP.is_equal)
+        tt(ap("dm", 0, 17), ap("pr", 0, 17), ap("pr", 32, 49), OP.subtract)
+    else:
+        for k in range(4): ts(ap("dm", 128 * k, 128 * k + 128), eye, (EV, OD)[k // 2], (1.0, -1.0)[k % 2], OP.mult, OP.mult)
     ms(ap("ones", 0, 128), 1.0); ms(f64("zero"), 0.0)
     cp(ap("onq", 0, 128), ap("ones", 0, 128))
     ms(s68("c4k"), 0.0); ms(ap("c4k", 0, 68, 17), -MID); ms(end("c4k"), MID); cp(s68("mrow"), s68("c4k"))
@@ -194,34 +214,35 @@ def build():
     ms(s68("dj"), -1.0); ms(ap("dj", 0, 68, 17), 0.0); ms(end("dj"), 15.0)
     ms(ap("d0", 0, 272), 0.0)
     for h in "ab":
-        for k in "01": ms(a3("pd" + k + h, 0, 30, 1, 0, 1), 0.0)
-        for k in (0, 33): cp(a3("tx" + h, 0, 4, 1, k, k + 1), c4("zero"))
-        ms(ap("mi" + h, 128, 256), 0.0)
+        for k in "012": ms(a3("pd" + k + h, 0, 30, 1, 0, 1), 0.0)
+        ms(a3("pd2" + h, 22, 30, 1, 1, 17, (4, 5)), 0.0)
+        for k in () if K32 else (0, 33): cp(a3("tx" + h, 0, 4, 1, k, k + 1), c4("zero"))
     ms(ap("tc", 0, 1), TH + OFF)
     ms(ap("PS", 0, 256), 0.0)
     ts(ap("boB", 0, 128), ap("gi", 0, 128), GC, 2.0 ** 64, OP.is_equal, OP.mult)
-    ts(X2, X, 2.0, None, OP.mult); ts(X1, X, -1.0, None, OP.add)
+    act(X2, X, AF.Copy, 2.0); ts(X1, X, -1.0, None, OP.add)
     ts(ap("dg", 0, 32), ap("iot", 0, 32), X2, -3.0, OP.is_equal, OP.mult)
     ts(ap("tb", 0, 16), ap("iot", 0, 16), X, None, OP.is_ge)
-    ts(ap("tb", 16, 32), ap("iot", 0, 16), X, None, OP.is_equal)
-    ts(ap("tb", 32, 48), ap("iot", 0, 16), X1, None, OP.is_equal)
+    ts(ap("tb", 16, 32), ap("iot", 0, 16), X1, None, OP.is_equal)
+    iota(ap("tz", 0, 160), [[0, 160]], 0, 0)
+    ts(ap("tz", 64, 80), ap("iot", 0, 16), X, None, OP.is_lt)
+    ts(ap("tz", 144, 160), ap("iot", 0, 16), X, None, OP.is_equal)
     ms(ap("seg", 0, 128), 0.0); ms(ap("seg", 0, 128, 32), 1.0)
-    ts(c4("dump"), c4("dump"), X, None, OP.add)
+    ts(c4("dump"), ap("iot", 0, 64, 16), X, None, OP.add)
+    ts(ap("dback", 0, 16), ap("dback", 0, 16), X, None, OP.add)
     ms(f64("quart"), 0.25)
     scan(f64("pow4"), f64("quart"), f64("zero"), OP.mult, OP.add, float(4.0 ** 32))
-    ts(ap("thm", 0, 128, 2), f64("pow4"), -1.0, None, OP.mult)
-    ts(ap("thm", 1, 128, 2), f64("pow4"), 2.0, None, OP.mult)
+    act(ap("thm", 0, 128, 2), f64("pow4"), AF.Copy, -1.0)
+    act(ap("thm", 1, 128, 2), f64("pow4"), AF.Copy, 2.0)
+    iota(ap("pr", 0, 128), [[0, 4], [1, 8], [0, 4]], 0, 0)
     ts(ap("pr", 0, 128), ap("pr", 0, 128), RH, 1e29, OP.not_equal, OP.mult)
     tt(ap("thm", 0, 128), ap("thm", 0, 128), ap("pr", 0, 128), OP.add)
-    for b in range(4):
-        ts(ci(4), ci(1), b, None, OP.logical_shift_right)
-        ts(ci(5), ci(4), 1, None, OP.bitwise_and)
-        ts(col(12 + b), ci(5), float(4.0 ** -(2 ** b) - 1.0), 1.0, OP.mult, OP.add)
-    tt(col(16), col(12), col(13), OP.mult); tt(col(17), col(14), col(15), OP.mult); tt(WM, col(16), col(17), OP.mult)
-    ts(c4("w4"), ap("pow4", 0, 64, 16), WM, None, OP.mult)
+    tt(ap("an", 0, 16), ap("tz", 144, 160), ap("pow4", 0, 16), OP.mult)
+    add("V", lambda g, T: g.vector.tensor_reduce(T.cols[:, 8:9], T.an[:, 0:16], AxisListType.X, OP.add), (ap("an", 0, 16),), (WM,), 0.08)
+    ts(c4("w4"), ap("pow4", 0, 64, 16), WM, 4.0 ** -31, OP.mult, OP.mult)
     ms(s68("dw"), 0.0)
-    ts(ap("dw", 0, 68, 17), c4("w4"), -1.0, None, OP.mult); cp(ap("dw", 15, 68, 17), c4("w4"))
-    cp(ap("HS", 0, 64), ap("hv32", 0, 64))
+    act(ap("dw", 0, 68, 17), c4("w4"), AF.Copy, -1.0); act(ap("dw", 15, 68, 17), c4("w4"), AF.Copy)
+    cp(ap("HS", 0, 64), ap("hv32", 0, 64)); ms(ap("HS", 72, 128), 0)
     for hi in range(2):
         for c in range(4): cp(ap("QP", 64 * hi + c, 64 * hi + 64, 4), ap("QS", 64 * hi + 16 * c, 64 * hi + 16 * c + 16))
         o = c4("sc" + "ab"[hi])
@@ -232,30 +253,44 @@ def build():
     ms(ap("Kp", 0, 1), 0.0)
     PT = {}
 
-    def step(t, s, h, P):
+    LAST = {"a": [], "b": []}
+
+    def step(t, s, h, P, turn_):
+        LAST[h] = []
         hi = "ab".index(h); win = NB + 128 * t; qr = YW * (2 * (t % 2) + hi)
-        L = c4("l" + h, 4 * s - 4) if s else c4("HS", t * 80 + hi * 4)
-        kids = ap("C" if t else "chi", 0, win if s else NB, ind=L); S = s68("sc" + h); D = s68("mi" + h); W = 68 * s
+        L = c4("l" + h, 4 * s - 4) if s else c4("HS", t * 136 + hi * 4)
+        kids = ap("C", 64, 64 + (win if s else NB), ind=L) if t else ap("chi", 0, NB, ind=L)
+        S = s68("sc" + h); D = s68("sc" + h, 68); W = (0, 68, 272)[s]
         cp(f64("ct" + h), kids)
         kv = KV[h][s]
-        cp(ap("kg" + h, 0, 16 * kv), ap("Ks", 0, win, ind=ap("ct" + h, 0, kv)))
-        act(ap("kg" + h, 16 * kv, 1024), ap("Ks", 0, win, ind=ap("ct" + h, kv, 64)), AF.Copy, after=[PT[h]] if s and PFIRST else [])
+        for k0, k1 in ((0, KW), (KW, kv)) if s and KW else ((0, kv),):
+            cp(ap("kg" + h, 16 * k0, 16 * k1), ap("Ks", 0, win, ind=ap("ct" + h, k0, k1)))
+        k1 = kv + (KS if s else 0)
+        if k1 > kv: act(ap("kg" + h, 16 * kv, 16 * k1), ap("Ks", 0, win, ind=ap("ct" + h, kv, k1)), AF.Copy, after=turn_)
+        act(ap("kg" + h, 16 * k1, 1024), ap("Ks", 0, win, ind=ap("ct" + h, k1, 64)), AF.Copy, after=turn_ + ([PT[h]] if s and PFIRST else []))
         ts(a3("cx" + h, 0, 4, 1, 0, 16, (0, 1)), f64("ct" + h), MID, EV, OP.subtract, OP.mult)
         ts(a3("cx" + h, 0, 4, 1, 16, 32, (1, 2)), f64("ct" + h), MID, OD, OP.subtract, OP.mult)
+        if K32:
+            turned = [(ap("sc" + h, 68 + 17 * c, 85 + 17 * c, p=q), a3("cx" + h, c, c + 1, 1, 0, 32, p=q), ap("dm", 0, 17, p=q),
+                       False, c == 3) for q in ((0, 32), (32, 64), (64, 96), (96, 128)) for c in range(4)]
+        else:
+            turn(a3("tx" + h, 0, 4, 1, 1, 33), a3("cx" + h, 0, 4, 1, 0, 32))
+            turned = [(D, ap("dm", 128 * k, 128 * k + 128), a3("tx" + h, 0, 4, 1, o, o + 17), False, k == 3) for k, o in enumerate((0, 1, 16, 17))]
         if h == "a" and s:
-            if t: act(f64("cf", 64 * s - 64), kids, AF.Copy)
+            if t and CF == "S": act(f64("cf", 64 * s - 64), kids, AF.Copy)
             else: cp(f64("cf", 64 * s - 64), f64("ct" + h))
-        turn(a3("tx" + h, 0, 4, 1, 1, 33), a3("cx" + h, 0, 4, 1, 0, 32))
-        mm([(D, ap("onq", 0, 128, p=1), ap("mrow", 0, 68, p=1), True, False)]
-           + [(D, ap("dm", 128 * k, 128 * k + 128), a3("tx" + h, 0, 4, 1, o, o + 17), False, k == 3) for k, o in enumerate((0, 1, 16, 17))])
-        mm([(S, ap("ones", 0, 128, p=2), ap("jrow", 0, 68, p=2), True, False)])
+        dd = mm([(D, ap("onq", 0, 128, p=1), ap("mrow", 0, 68, p=1), True, False)]
+                + turned)
+        mm([(S, ap("ones", 0, 128, p=2), ap("jrow", 0, 68, p=2), True, False)], after=[dd])
         for c, (m0, m1) in enumerate(CHUNKS):
-            c0, c1 = 68 * m0, 68 * m1; pd = "pd%d" % (c % 2) + h; n = 4 * (m1 - m0); d = a3(pd, 0, n, 1, 0, 17)
+            c0, c1 = 68 * m0, 68 * m1; pd = "pd%d" % c + h; n = 4 * (m1 - m0); d = a3(pd, 0, n, 1, 0, 17)
             dk = a3(pd, 0, n, 1, 1, 17); ex = a64("exn", 64 * m0, 64 * m1)
-            if s: mm([(dk, P, ex, True, False)])
-            mm([(a3(pd, b, n, 4, 1, 17), eye, ap("kg" + h, 256 * b + 16 * m0, 256 * b + 16 * m1), s == 0 and b == 0, s > 0 and b == 3) for b in range(4)])
-            if not s: mm([(dk, P, ex, False, True)])
-            act(ap("y" + h, c0, c1), d, AF.Abs)
+            pf = s > 0 and c >= PMM
+            if pf: mm([(dk, P, ex, True, False)])
+            mm([(a3(pd, b, n, 4, 1, 17), eye, ap("kg" + h, 256 * b + 16 * m0, 256 * b + 16 * m1), not pf and b == 0, pf and b == 3) for b in range(4)])
+            if not pf: mm([(dk, P, ex, False, True)])
+            y = size(ap("y" + h, c0, c1), d) if c == 2 and s in VABS else act(ap("y" + h, c0, c1), d, AF.Abs)
+            if c == ALT[h][s]: LAST[h] = [y]
             mm([(S, ap("Wy", 15 - m, 143 - m), s68("y" + h, 68 * m), False, False) for m in range(m0, m1)])
             scan(ap("z" + h, c0, c1), ap("qr", qr + c0, qr + c1), ap("y" + h, c0, c1), OP.max, OP.min)
             mm([(S, ap("Wz", 15 - m, 143 - m), s68("z" + h, 68 * m), False, m == 15) for m in range(m0, m1)])
@@ -263,27 +298,28 @@ def build():
         scan(s68("f" + h), s68("d0", 136 * (t % 2) + 68 * hi), S, OP.max, OP.min)
         tt(ne, S, s68("f" + h), OP.not_equal)
         scan(s68("w" + h, W), ne, D, OP.mult, OP.add)
-        Ln = c4("l" + h, 4 * s)
-        cp(Ln, end("w" + h, W))
+        cp(c4("l" + h, 4 * s), end("w" + h, W))
+        if h == "a" and s < 2: act(ap("nbr", s, 128, 2), ap("iot", 0, win, ind=c4("la", 4 * s)), AF.Copy)
+        if h == "a" and s:
+            scan(s68("wa", 68 + 68 * s), ne, s68("dj"), OP.mult, OP.add)
+            cp(c4("ju" if s == 1 else "ku"), end("wa", 68 + 68 * s))
+        if h == "a" and s == 1: scan(s68("uw"), ne, s68("dw"), OP.mult, OP.add)
+
+    def move(t, s, h, P, turn_):
+        hi = "ab".index(h); win = NB + 128 * t; kk = ap("Kp", 0, win, ind=c4("l" + h, 4 * s))
         kq = ap("Ks", win + s, win + 128, 2) if h == "a" and s < 2 else f64("kq" + h)
+        get = lambda: cp(kq, kk) if KQ[s] == "V" else act(kq, kk, AF.Copy, after=turn_)
         if t == NV - 1 and s == 2:
-            o = ap("mi" + h, 128, 192); Pn = f64("kq" + h, 64)
-            mm([(o, P, a64("n64", 0, 64), True, False)])
-            act(kq, ap("Kp", 0, win, ind=Ln), AF.Copy)
+            o = a3("pd2" + h, 22, 26, 1, 1, 17, (4, 5)); Pn = f64("kq" + h, 64)
+            mm([(o, P, a64("n64", 0, 64), True, False)]); get()
             mm([(o, eye, kq, False, True)])
         else:
-            o = a64("mi" + h, 128, 256); b = t * 256 + hi * 128
+            o = a3("pd2" + h, 22, 30, 1, 1, 17, (4, 5), 64); b = t * 256 + hi * 128
             Pn = a64("pt" + h, 128 * s, 128 * s + 128) if s < 2 else a64("PO", b, b + 128)
-            mm([(o, a64("n64", 0, 64), P, True, False)])
-            act(kq, ap("Kp", 0, win, ind=Ln), AF.Copy)
+            mm([(o, a64("n64", 0, 64), P, True, False)]); get()
             mm([(o, kq, eye, False, True)])
-        if Pn[0] == "PO": act(ap(*Pn[:3]), ap(*o[:3]), AF.Abs)
-        else: PT[h] = act(Pn, o, AF.Abs)
-        if h == "a" and s < 2: act(ap("nbr", s, 128, 2), ap("iot", 0, win, ind=Ln), AF.Copy)
-        if h == "a" and s:
-            scan(s68("uj"), ne, s68("dj"), OP.mult, OP.add)
-            cp(c4("ju" if s == 1 else "ku"), end("uj"))
-        if h == "a" and s == 1: scan(s68("uw"), ne, s68("dw"), OP.mult, OP.add)
+        if Pn[0] == "PO": act(ap(*Pn[:3]), a3("pd2" + h, 22, 30, 1, 1, 17, (4, 5)), AF.Abs)
+        else: PT[h] = act(Pn, o, AF.Abs, after=turn_)
         return Pn
 
     def slice_early(t):
@@ -294,60 +330,69 @@ def build():
             for w in range(2):
                 o = 128 * (c + 4 * w); n = 68 * w + 17 * c + 16
                 ts(ap("emat", o + 32 * c, o + 128), ap("nbr", 32 * c, 128), ap("wa", n, n + 1), None, OP.is_equal)
-        for w in range(2): tt(c4("nd", 4 * w), end("wa", 68 * w), c4("dump"), OP.subtract)
         tt(f64("an"), ap("tb", 0, 16, ind=c4("ju")), ra, OP.mult)
-        tt(f64("oj1"), ap("tb", 32, 48, ind=c4("ju")), f64("mt", 64 * t), OP.mult)
+        tt(f64("oj1"), ap("tb", 16, 32, ind=c4("ju")), f64("mt", 64 * t), OP.mult)
         tt(f64("val"), f64("an"), f64("oj1"), OP.add)
-        tt(f64("au"), ra, f64("an"), OP.subtract)
-        tt(f64("oj"), ap("tb", 16, 32, ind=c4("ju")), f64("nn", 64 * t), OP.mult)
-        tt(f64("mn"), f64("au"), f64("oj"), OP.add)
         if t < NV - 1: gcp(ap("Kp", win, win + 128), ap("Ks", win, win + 128))
 
     def slice_late(t):
-        win = NB + 128 * t; rb = f64("cf", 64)
+        win = 64 + NB + 128 * t; ra = f64("cf"); rb = f64("cf", 64)
+        tt(ap("nd", 0, 16), ap("wa", 16, 272, 17), ap("dback", 0, 16), OP.subtract)
         for c in range(4):
-            w = ap("wtf", c * 128, c * 128 + 128); n = 136 + 17 * c + 16; o = ap("sca", 128 + 32 * c, 256)
+            w = ap("wtf", c * 128, c * 128 + 128); n = 272 + 17 * c + 16; o = a3("pd0a", 2 * c, 8, 1, 1, 17)
             ts(w, ap("boB", 0, 128), ap("wa", n, n + 1), ap("wc", c, c + 1), OP.mult, OP.min)
-            mm([(o, w, ap("emat", 160 * c, 128 * c + 128), c == 0, False), (ap("sca", 128 + 32 * c, 160 + 32 * c), w, ap("dg", 0, 32), False, False),
+            mm([(o, w, ap("emat", 160 * c, 128 * c + 128), c == 0, False), (a3("pd0a", 2 * c, 2 * c + 2, 1, 1, 17), w, ap("dg", 0, 32), False, False),
                 (o, w, ap("emat", 512 + 160 * c, 512 + 128 * c + 128), False, c == 3)])
-        tt(ap("good", 0, 128), ap("sca", 128, 256), ap("thm", 0, 128), OP.is_lt)
+        tt(ap("good", 0, 128), a3("pd0a", 0, 8, 1, 1, 17), ap("thm", 0, 128), OP.is_lt)
         scan(ap("gd", 0, 128), ap("seg", 0, 128), ap("good", 0, 128), OP.max, OP.min)
-        for c in range(4): ts(ap("tlu", c, 8, 4), ap("nd", c, 8, 4), ap("gd", 32 * c + 31, 32 * c + 32), ap("dump", c, c + 1), OP.mult, OP.add)
+        for c in range(4):
+            ts(ap("tlu", c, 16, 4), ap("nd", c, 16, 4), ap("gd", 32 * c + 31, 32 * c + 32), ap("dump", c, c + 1), OP.mult, OP.add)
         tt(f64("val", 64), ap("tb", 0, 16, ind=c4("ku")), rb, OP.mult)
-        for w in range(2): cp(ap("C", 0, NW + 64, ind=c4("tlu", 4 * w)), f64("val", 64 * w))
-        tt(f64("mn", 64), rb, f64("val", 64), OP.subtract)
-        cp(c4("gu"), ap("gd", 31, 128, 32))
-        for w in range(2): tt(ap("C", win + w, win + 128, 2), ap("iot", 0, 8, ind=c4("gu")), f64("mn", 64 * w), OP.mult)
+        if t == NV - 1: cp(ap("C", 64, 65), C0)
+        for w in range(2): cp(ap("C", 0, win, ind=c4("tlu", 4 * w)), f64("val", 64 * w))
+        tt(f64("au"), ap("tz", 0, 80, ind=c4("tlu", 8)), ra, OP.mult)
+        tt(f64("oj"), ap("tz", 80, 160, ind=c4("tlu", 8)), ap("iot", win - 63, win + 64, 2), OP.mult)
+        tt(ap("C", win, win + 128, 2), f64("au"), f64("oj"), OP.add)
+        tt(ap("C", win + 1, win + 128, 2), ap("tz", 0, 80, ind=c4("tlu", 12)), rb, OP.mult)
         if t < NV - 1:
             act(c4("gh"), ap("gd", 31, 128, 32), AF.Copy)
-            mm([(ap("sca", 256, 257), ap("ones", 0, 128), ap("gh", c, c + 1), c == 0, c == 3) for c in range(4)])
+            mm([(ap("sca", 256, 257), ap("half", 0, 128), ap("gh", c, c + 1), c == 0, c == 3) for c in range(4)])
             cp(ap("zu", 0, 1), ap("sca", 256, 257))
-            act(ap("tc", 0, 16), ap("bnd", 0, 576, ind=ap("zu", 0, 1)), AF.Copy)
+            act(ap("tc", 0, 16), ap("bnd", 0, 288, ind=ap("zu", 0, 1)), AF.Copy)
 
-    sent = []
+    def deal(t0, t1, sem, lag, after):
+        def emit(g, T, core, topo):
+            to = [T.cores[(T.rank_of(core) + t) % N] for t in range(t0, t1)]
+            ids = [DstId(rid=topo.addr(c)[0], pnc=topo.addr(c)[1]) for c in to]
+            e = shared(T, topo) if len(to) > 1 else topo.engines(core, to[0]); k = len(e) // 2
+            g.remote_dma_fused([RemoteDMATransfer(dst_ids=ids, dma_engine_mask=sum(1 << x for x in e[w * k:w * k + k]), remote_sem=T.sem[sem], src=T[n][:, 0:128],
+                                                  dsts=[T[n][:, 128 * t:128 * t + 128] for t in range(t0, t1)]) for w, n in enumerate(("QP", "HS"))], local_sem=T.sem["snd"])
+        o = add("G", emit, (ap("QP", 0, 128), ap("HS", 0, 128), ap("Ks", 8, 16)), (), 2.0, n=0, done=("snd", 8), after=after)
+        ops[o]["many"] = t1 - t0 > 1
+        add("R", None, (), (ap("QP", 128 * t0, 128 * t1), ap("HS", 128 * t0, 128 * t1)), 0.0, n=0, done=(sem, t1 - t0), after=[o], lag=lag)
+        return o
+    numbers.append(deal(2, NV, "all", 20.0, [deal(1, 2, "one", 7.0, [])] + numbers[:2]))
+    sent = []; before = numbers
     for t in range(NV):
-        qn = ap("QP", (t + 1) * 128, (t + 2) * 128); hn = ap("HS", (t + 1) * 72, (t + 2) * 72)
-        if t < NV - 1:
-            qsent = send(qn, ap("QP", t * 128, t * 128 + 128), "aq%d" % (t + 1), sent)
-            hsent = send(hn, ap("HS", t * 72, t * 72 + 72), "ah%d" % (t + 1), sent)
-        P = {}
+        P = {}; tag[1] = t
         qr = 2 * YW * (t % 2)
         for hi in range(2):
             b = t * 256 + hi * 128; P["ab"[hi]] = a64("PS", b, b + 128)
-            if t == 0:
-                for j in range(17): cp(ap("qr", hi * YW + j, hi * YW + YW, 17), f64("QP", hi * 64))
-        if t:
-            for j in range(1 if t > 1 else 0, 17): gcp(ap("qr", qr + j, qr + 2 * YW, 17), ap("QP", t * 128, t * 128 + 128))
+        for j in range(1 if t > 1 else 0, 17):
+            o = ap("qr", qr + j, qr + 2 * YW, 17); q = ap("QP", t * 128, t * 128 + 128)
+            if t: gcp(o, q, before)
+            else: act(o, q, AF.Copy)
+        if t: before = sent
         d0 = 136 * (t % 2)
-        ts(ap("d0", d0 + 1, d0 + 136, 17), ap("HS", t * 72 + 64, t * 72 + 72), -1.0, ap("tc", 0, 1), OP.mult, OP.add)
-        if t < NV - 1:
-            recv(qn, "aq%d" % (t + 1), qsent); recv(hn, "ah%d" % (t + 1), hsent)
-        for s in range(3):
-            for h in "ab":
-                tag[0] = h; P[h] = step(t, s, h, P[h]); tag[0] = None
-            if s == 1: slice_early(t)
+        ts(ap("d0", d0 + 1, d0 + 136, 17), ap("HS", t * 128 + 64, t * 128 + 72), -1.0, ap("tc", 0, 1), OP.mult, OP.add)
+        for h, s in TURNS:
+            tag[0] = s; turn_ = LAST["ba"["ab".index(h)]]
+            if s: P[h] = move(t, s - 1, h, P[h], turn_)
+            step(t, s, h, P[h], turn_); tag[0] = None
+        slice_early(t)
+        for h in "ab": P[h] = move(t, 2, h, P[h], [])
         if t == 0:
-            for i in range(8): cp(ap("C", i * 320, (i + 1) * 320), ap("chi", i * 320, (i + 1) * 320))
+            for i in range(8): cp(ap("C", 64 + i * 320, 384 + i * 320), ap("chi", i * 320, 320 + i * 320))
         on = []
         for hi in range(2):
             b = t * 256 + hi * 128; sem = "a%s%d" % ("ab"[hi], t + 1)
@@ -356,8 +401,7 @@ def build():
         sent = [send(o, a, sem) for o, sem, a in on]
         slice_late(t)
         for k in range(2): recv(on[k][0], on[k][1], sent[k])
-    cp(ap("C", 0, 1), C0)
-    for i in range(4): dma(ap("yc", i * 896, (i + 1) * 896), ap("C", i * 896, (i + 1) * 896), "st%d" % i, 5)
+    for i, (c0, c1) in enumerate(((0, 1152), (1152, 2304), (2304, 3456), (3456, NW))): dma(ap("yc", c0, c1), ap("C", 64 + c0, 64 + c1), "st%d" % i, STORE if i < 3 else 2.5)
     for hi in range(2): dma(f64("yp", 64 * hi), f64("PF", 64 * hi), "sp" + "ab"[hi], 2)
     return ops
 
@@ -392,7 +436,7 @@ def plan(ops):
     for o in ops:
         for q in o["dep"]: succ[q].append(o["i"])
     for o in reversed(ops): pri[o["i"]] = o["cost"] + o["lag"] + LAT + max([pri[x] for x in succ[o["i"]]] or [0.0])
-    for o in ops: pri[o["i"]] += BIAS[o["tag"]]
+    for o in ops: pri[o["i"]] += BIAS.get((o["eng"], (o["wr"] + o["rd"])[0][0], o["tag"]), 0.0)
     order = {e: [] for e in "VSPGYR"}; free = {e: 0.0 for e in order}
     ready = {i for i in range(m) if left[i] == 0}; est = [0.0] * m; fin = [0.0] * m
     while ready:
@@ -471,14 +515,14 @@ def rank_program(g, core, T, topo):
         MEMO["o"] = build(); MEMO["p"] = plan(MEMO["o"])
     ops = MEMO["o"]; order, waits, cnt, _ = MEMO["p"]
     queue = {"V": g.vector, "S": g.scalar, "P": g.tensor, "G": g, "Y": g.sync}
-    sent = 0; r = T.rank_of(core)
-    into = len(topo.engines(T.cores[(r - 1) % N], core)); out = len(topo.engines(core, T.cores[(r + 1) % N]))
+    sent = 0; me = T.rank_of(core); every = len(shared(T, topo))
+    into = len(topo.engines(T.cores[(me - 1) % N], core)); out = len(topo.engines(core, T.cores[(me + 1) % N]))
     for e in "YVSPG":
         for i in order[e]:
             o = ops[i]
-            for s, v in waits[i]: queue[e].wait_ge(T.sem[s], into if s in ARRIVE else v)
+            for s, v in waits[i]: queue[e].wait_ge(T.sem[s], into if s in ARRIVE else v * every if s == "all" else v)
             if o["done"] == ("snd", 8):
-                o["emit"](g, T, core, topo); sent += out
+                o["emit"](g, T, core, topo); sent += every if o.get("many") else out
             elif o["done"]: o["emit"](g, T).then_inc(T.sem[o["done"][0]], 16)
             else:
                 r = o["emit"](g, T)

from concourse.bass import DstId, RemoteDMATransfer
from concourse.mybir import dt, AluOpType, AxisListType, ActivationFunctionType

OP = AluOpType
AF = ActivationFunctionType
N, NB, NV = 8, 2560, 8
NW = NB + 128 * NV
FAR, OFF, TH = 1024.0, 4096.0, 1235.0
BIAS = {("Y", "QS", None): 10.0, ("Y", "hv32", None): 9.0, ("V", "QP", None): 4.0, ("S", "qr", None): 3.0}
CHUNKS = ((0, 5), (5, 11), (11, 16))
KV = {"a": (32, 34, 32), "b": (32, 34, 32)}
CF, EACH, VABS = "V", 0.0, ()
TURNS = (("a", 0), ("b", 0), ("a", 1), ("b", 1), ("a", 2), ("b", 2))
K32 = False
PFIRST, KS, KQ, PMM, KW = True, 12, "SSS", 0, 10
ALT = {"a": (3, 1, 1), "b": (1, 1, 3)}
NOWAIT = ("bank", "ord")
LOADS = 4
YW = 64 * 17
F, H, Q, I, U = "float32", "bfloat16", "float16", "int32", "uint16"
MID = 1792.0
SCRATCH = {}
for _t, _n, _names in (
        (I, NB, "chi"), (F, NW + 64, "C"), (H, NW, "Ks Kp"), (H, 1024, "QP emat"), (U, 1024, "HS"), (H, 2048, "PS PO"),
        (I, 64, "hv32"), (H, 128, "QS PF eye ones half boB good seg kqa kqb"), (F, 128, "gd"), (H, 4, "gh"), (H, 144, "Wy Wz"), (H, 256, "pta ptb"),
        (H, 68, "c4k jrow dj dw nea neb uw"), (F, 68, "fa fb"), (F, 340, "wa wb"), (F, 512, "mt"), (Q, 512, "dm"), (Q, 128, "onq"), (Q, 68, "mrow"), (H, 512, "wtf"),
        (H, 64, "n64"), (H, 32, "dg"), (F, 64, "pow4 quart zero oj oj1 au an"), (F, 32, "tb"),
        (F, 128, "gi thm pr nbr val cf"), (F, 32, "cols"), (I, 16, "coli"), (U, 64, "cta ctb"),
        (F, NW, "iot"), (F, 16, "nd dback"), (F, 4, "dump w4 ca wc"), (U, 4, "ju ku"), (U, 16, "tlu"), (F, 160, "tz"),
        (F, 16, "tc"), (U, 2, "zu"), (F, 288, "bnd"), (F, 272, "d0"), (H, YW, "exn ya yb za zb"), (H, 4 * YW, "qr"), (U, 12, "la lb")):
    for _b in _names.split(): SCRATCH[_b] = ("sbuf", [128, _n], _t)
for _h in "ab":
    SCRATCH["kg" + _h] = ("sbuf", [128, 1024], H)
    SCRATCH["cx" + _h] = ("sbuf", [128, 4, 32], Q)
    SCRATCH["tx" + _h] = ("sbuf", [128, 4, 34], Q)
    SCRATCH["sc" + _h] = ("psum", [128, 512], F)
    for _b in ("pd0", "pd1", "pd2"): SCRATCH[_b + _h] = ("psum", [128, 30, 17], F)
PSUM = {k for k, v in SCRATCH.items() if v[0] == "psum"}
DMAS = ["ld%d" % i for i in range(LOADS)] + "ldk ldp ldq ldh st0 st1 st2 st3 spa spb".split()
ARRIVE = ["one"] + ["a%s%d" % (h, t) for h in "ab" for t in range(1, 9)]
SEMAPHORES = "v s pe gp snd all".split() + DMAS + ARRIVE
CY, PCY, LAT, SC = 0.00083, 0.00042, 0.27, 1.3
AHEAD, URGENT, ROUNDS, FLY, STORE, GATHER = 0.4, 2.0, 2, 3.5, 5.0, 1.5


def ap(name, c0, c1, step=1, p=128, ind=None):
    return (name, c0, c1, step, p, ind, None, (c0, c1))


def a3(name, m0, m1, ms, c0, c1, part=(0, 4), p=128):
    return (name, c0, c1, 1, p, None, (m0, m1, ms), part)


def toks(a):
    return [(a[0],) + a[7] + (a[3],)] + (toks(a[5]) if a[5] else [])


def meet(a, b):
    return a[0] < b[1] and b[0] < a[1] and (a[2] != b[2] or (a[0] - b[0]) % a[2] == 0)


def res(T, a):
    p0, p1 = a[4] if isinstance(a[4], tuple) else (0, a[4])
    if len(SCRATCH.get(a[0], (0, ()))[1]) == 4: return T[a[0]][p0:p1, a[6][0]:a[6][1]:a[6][2], a[1]:a[2], 0]
    if a[6] and a[6][1] - a[6][0] == 1: return T[a[0]][p0:p1, a[6][0], a[1]:a[2]]
    if a[6]: return T[a[0]][p0:p1, a[6][0]:a[6][1]:a[6][2], a[1]:a[2]]
    v = T[a[0]][p0:p1, a[1]:a[2]] if a[3] == 1 else T[a[0]][p0:p1, a[1]:a[2]:a[3]]
    return v.indirect(res(T, a[5])) if a[5] else v


def ln(a):
    if a[6]: return -(-(a[6][1] - a[6][0]) // a[6][2]) * (a[2] - a[1])
    return 16 * (a[5][2] - a[5][1]) if a[5] else -(-(a[2] - a[1]) // a[3])


def two(*aps):
    return all(SCRATCH[a[0]][2] in (H, Q, U) for a in aps)


def shared(T, topo):
    return [e for e in topo.engines(T.cores[0], T.cores[1]) if all(e in topo.engines(a, b) for a in T.cores for b in T.cores if a != b)]


def build():
    ops = []; tag = [None, None]

    def add(eng, emit, rd, wr, cost, n=1, done=None, after=(), lag=0.0):
        o = {"eng": eng, "emit": emit, "rd": [t for a in rd for t in toks(a)], "wr": [toks(a)[0] for a in wr], "cost": cost * (SC if n else 1),
             "n": n, "done": done, "after": list(after), "lag": lag, "i": len(ops), "tag": tag[0], "t": tag[1]}
        for a in wr: o["rd"] += toks(a)[1:]
        ops.append(o)
        return o["i"]

    def vc(out, ins, per=1.0):
        n = ln(out)
        if out[5]: return 0.06 + n * 3.8 * CY
        if any(a[5] for a in ins): return 0.06 + n * GATHER * CY
        return 0.02 + max(64, n * per) * CY

    def tt(out, a, b, op):
        per = 1 if a[0] in PSUM or b[0] in PSUM else 2
        return add("V", lambda g, T: g.vector.tensor_tensor(res(T, out), res(T, a), res(T, b), op), (a, b), (out,), vc(out, (a,), per))

    def ts(out, a, s1, s2, o1, o2=None):
        sc = lambda T, s: res(T, s) if isinstance(s, tuple) else s
        def emit(g, T):
            if o2 is None: return g.vector.tensor_scalar(res(T, out), res(T, a), sc(T, s1), None, o1)
            return g.vector.tensor_scalar(res(T, out), res(T, a), sc(T, s1), sc(T, s2), o1, o2)
        return add("V", emit, [a] + [s for s in (s1, s2) if isinstance(s, tuple)], (out,), vc(out, (), 0.5 if two(out, a) else 1))

    def cp(out, a):
        return add("V", lambda g, T: g.vector.tensor_copy(res(T, out), res(T, a)), (a,), (out,), vc(out, (a,), 0.5 if two(out, a) else 1))

    def scan(out, d0, d1, o1, o2, init=0.0):
        return add("V", lambda g, T: g.vector.tensor_tensor_scan(res(T, out), res(T, d0), res(T, d1), init, o1, o2), (d0, d1), (out,), vc(out, (), 0.5 if two(out, d0, d1) else 1))

    def turn(out, a):
        return add("V", lambda g, T: g.vector.transpose(res(T, out), res(T, a)), (a,), (out,), vc(out, (), 0.5 if two(out, a) else 1))

    def size(out, a):
        emit = lambda g, T: g.vector.tensor_reduce(res(T, out), T[a[0]][0:128, a[6][0]:a[6][1], :, :], AxisListType.X, OP.max, apply_absolute_value=True)
        return add("V", emit, (a,), (out,), vc(out, ()))

    def ms(out, x):
        return add("V", lambda g, T: g.vector.memset(res(T, out), x), (), (out,), vc(out, (), 0.5 if two(out) else 1))

    def act(out, a, func, scale=None, after=()):
        def emit(g, T):
            if scale: return g.scalar.activation(res(T, out), res(T, a), func, scale=scale)
            return g.scalar.activation(res(T, out), res(T, a), func)
        return add("S", emit, (a,), (out,), 0.08 + ln(out) * (GATHER if a[5] else 1.0) * CY, after=after)

    def mm(ml, f32=False, after=()):
        def emit(g, T):
            return [g.tensor.matmul(res(T, o), res(T, l), res(T, r), st, sp) for (o, l, r, st, sp) in ml]
        c = sum(max(min(64, ln(m[1])), ln(m[2])) for m in ml) * (4 if f32 else 1) * PCY + 0.01 + EACH * len(ml)
        return add("P", emit, [m[k] for m in ml for k in (1, 2)], [m[0] for m in ml], c, n=len(ml), after=after)

    def iota(out, pat, base, cmul):
        def emit(g, T):
            if SCRATCH[out[0]][2] == I: return g.iota(res(T, out), pat, base, cmul)
            return g.iota(res(T, out), pat, base, cmul, allow_small_or_imprecise_dtypes=True)
        return add("G", emit, (), (out,), 0.15 + 2 * ln(out) * CY)

    def aff(a, pat, base):
        return add("G", lambda g, T: g.affine_select(res(T, a), res(T, a), pat, OP.is_equal, 0.0, base, 1), (a,), (a,), 0.2 + 2 * ln(a) * CY)

    def gcp(out, a, after=()):
        return add("G", lambda g, T: g.affine_select(res(T, out), res(T, a), [[0, ln(a)]], OP.is_equal, 0.0, 0, 0), (a,), (out,), 0.17 + 2 * ln(a) * CY, after=after)

    def dma(out, a, sem, lag):
        add("Y", lambda g, T: g.sync.dma_start(res(T, out), res(T, a)), [x for x in (a,) if x[0] in SCRATCH],
            [x for x in (out,) if x[0] in SCRATCH], 0.1, done=(sem, 16), lag=lag)

    def send(out, a, sem, after=()):
        def emit(g, T, core, topo):
            dst = T.cores[(T.rank_of(core) + 1) % N]
            rid, pid, _ = topo.addr(dst)
            g.remote_dma(res(T, out), res(T, a), T.sem[sem], T.sem["snd"], pid, rid, topo.mask(core, dst))
        return add("G", emit, (a,), (), 0.8, n=0, done=("snd", 8), after=after)

    def recv(out, sem, sender):
        return add("R", None, (), (out,), 0.0, n=0, done=(sem, 8), after=[sender], lag=FLY)

    W4 = NB // LOADS
    dma(ap("hv32", 0, 64), ap("hv", 0, 64), "ldh", 2.2)
    dma(ap("QS", 0, 128), ap("qs", 0, 128), "ldq", 2.3)
    for i in range(LOADS): dma(ap("chi", i * W4, (i + 1) * W4), ap("ch", i * W4, (i + 1) * W4), "ld%d" % i, 3.0 + 0.8 * i)
    dma(ap("Ks", 0, NB), ap("kb", 0, NB), "ldk", 6.5)
    dma(ap("Kp", 0, NB), ap("kb", 0, NB), "ldp", 7.5)
    col = lambda k: ap("cols", k, k + 1)
    ci = lambda k: ap("coli", k, k + 1)
    a64 = lambda n, c0=0, c1=128: ap(n, c0, c1, 1, 64)
    s68 = lambda n, o=0: ap(n, o, o + 68)
    end = lambda n, o=0: ap(n, o + 16, o + 68, 17)
    f64 = lambda n, o=0: ap(n, o, o + 64)
    c4 = lambda n, o=0: ap(n, o, o + 4)
    eye = ap("eye", 0, 128)
    X, GC, RH, EV, OD, WC, X2, X1, WM, C0 = [col(k) for k in range(10)]
    iota(ci(0), [[0, 1]], 0, 1)
    iota(ap("iot", 0, 144), [[1, 144]], 0, 0)
    ms(eye, 1.0)
    aff(eye, [[-1, 128]], 0)
    ms(a64("exn", 0, 1024), -1.0)
    aff(a64("exn", 0, 1024), [[-1, 16], [-16, 4], [0, 16]], 0)
    iota(s68("jrow"), [[0, 4], [1, 17]], -1, 0)
    iota(ap("gi", 0, 128), [[1, 8], [0, 16]], 0, 0)
    numbers = [iota(ap("iot", c0, c1), [[1, c1 - c0]], c0, 0) for c0, c1 in ((144, 1280), (1280, NB), (NB, NW))]
    iota(ap("dback", 0, 16), [[0, 4], [16, 4]], -64, 0)
    numbers += [iota(ap("bnd", 0, 288), [[0, 9], [2, 32]], int(TH + OFF), 0),
                iota(ap("mt", 0, 512), [[128, 8], [4, 32], [-2, 2]], NB + 2, 0)]
    ms(ap("half", 0, 128), 0.5)
    ts(ci(1), ci(0), 15, None, OP.bitwise_and)
    ts(ci(2), ci(0), 4, None, OP.logical_shift_right)
    ts(ci(3), ci(1), 1, None, OP.logical_shift_right)
    ts(ci(6), ci(2), 1, None, OP.bitwise_and)
    cp(X, ci(1)); cp(GC, ci(2)); cp(RH, ci(3)); cp(OD, ci(6))
    ts(EV, OD, -1.0, 1.0, OP.mult, OP.add)
    ts(WC, GC, 16.0, 15.0, OP.mult, OP.add)
    ts(ap("Wy", 0, 144), ap("iot", 0, 144), WC, None, OP.is_equal)
    act(ap("Wz", 0, 144), ap("Wy", 0, 144), AF.Copy, -2.0)
    act(a64("n64", 0, 64), a64("eye", 0, 64), AF.Copy, -1.0)
    if K32:
        ts(X1, X, 1.0, None, OP.add)
        ts(ap("pr", 0, 17), ap("iot", 0, 17), X1, None, OP.is_equal); ts(ap("pr", 32, 49), ap("iot", 0, 17), X, None, OP.is_equal)
        tt(ap("dm", 0, 17), ap("pr", 0, 17), ap("pr", 32, 49), OP.subtract)
    else:
        for k in range(4): ts(ap("dm", 128 * k, 128 * k + 128), eye, (EV, OD)[k // 2], (1.0, -1.0)[k % 2], OP.mult, OP.mult)
    ms(ap("ones", 0, 128), 1.0); ms(f64("zero"), 0.0)
    cp(ap("onq", 0, 128), ap("ones", 0, 128))
    ms(s68("c4k"), 0.0); ms(ap("c4k", 0, 68, 17), -MID); ms(end("c4k"), MID); cp(s68("mrow"), s68("c4k"))
    ts(s68("jrow"), s68("jrow"), 1 / 16, -31 / 32, OP.mult, OP.add)
    ms(ap("jrow", 0, 68, p=1), OFF); ms(ap("jrow", 0, 68, 17), 0.0)
    ms(s68("dj"), -1.0); ms(ap("dj", 0, 68, 17), 0.0); ms(end("dj"), 15.0)
    ms(ap("d0", 0, 272), 0.0)
    for h in "ab":
        for k in "012": ms(a3("pd" + k + h, 0, 30, 1, 0, 1), 0.0)
        ms(a3("pd2" + h, 22, 30, 1, 1, 17, (4, 5)), 0.0)
        for k in () if K32 else (0, 33): cp(a3("tx" + h, 0, 4, 1, k, k + 1), c4("zero"))
    ms(ap("tc", 0, 1), TH + OFF)
    ms(ap("PS", 0, 256), 0.0)
    ts(ap("boB", 0, 128), ap("gi", 0, 128), GC, 2.0 ** 64, OP.is_equal, OP.mult)
    act(X2, X, AF.Copy, 2.0); ts(X1, X, -1.0, None, OP.add)
    ts(ap("dg", 0, 32), ap("iot", 0, 32), X2, -3.0, OP.is_equal, OP.mult)
    ts(ap("tb", 0, 16), ap("iot", 0, 16), X, None, OP.is_ge)
    ts(ap("tb", 16, 32), ap("iot", 0, 16), X1, None, OP.is_equal)
    iota(ap("tz", 0, 160), [[0, 160]], 0, 0)
    ts(ap("tz", 64, 80), ap("iot", 0, 16), X, None, OP.is_lt)
    ts(ap("tz", 144, 160), ap("iot", 0, 16), X, None, OP.is_equal)
    ms(ap("seg", 0, 128), 0.0); ms(ap("seg", 0, 128, 32), 1.0)
    ts(c4("dump"), ap("iot", 0, 64, 16), X, None, OP.add)
    ts(ap("dback", 0, 16), ap("dback", 0, 16), X, None, OP.add)
    ms(f64("quart"), 0.25)
    scan(f64("pow4"), f64("quart"), f64("zero"), OP.mult, OP.add, float(4.0 ** 32))
    act(ap("thm", 0, 128, 2), f64("pow4"), AF.Copy, -1.0)
    act(ap("thm", 1, 128, 2), f64("pow4"), AF.Copy, 2.0)
    iota(ap("pr", 0, 128), [[0, 4], [1, 8], [0, 4]], 0, 0)
    ts(ap("pr", 0, 128), ap("pr", 0, 128), RH, 1e29, OP.not_equal, OP.mult)
    tt(ap("thm", 0, 128), ap("thm", 0, 128), ap("pr", 0, 128), OP.add)
    tt(ap("an", 0, 16), ap("tz", 144, 160), ap("pow4", 0, 16), OP.mult)
    add("V", lambda g, T: g.vector.tensor_reduce(T.cols[:, 8:9], T.an[:, 0:16], AxisListType.X, OP.add), (ap("an", 0, 16),), (WM,), 0.08)
    ts(c4("w4"), ap("pow4", 0, 64, 16), WM, 4.0 ** -31, OP.mult, OP.mult)
    ms(s68("dw"), 0.0)
    act(ap("dw", 0, 68, 17), c4("w4"), AF.Copy, -1.0); act(ap("dw", 15, 68, 17), c4("w4"), AF.Copy)
    cp(ap("HS", 0, 64), ap("hv32", 0, 64)); ms(ap("HS", 72, 128), 0)
    for hi in range(2):
        for c in range(4): cp(ap("QP", 64 * hi + c, 64 * hi + 64, 4), ap("QS", 64 * hi + 16 * c, 64 * hi + 16 * c + 16))
        o = c4("sc" + "ab"[hi])
        mm([(o, ap("Wy", 15 - m, 143 - m), c4("QP", 64 * hi + 4 * m), m == 0, m == 15) for m in range(16)])
        cp(c4("HS", 64 + 4 * hi), o)
    cp(C0, ap("chi", 0, 1)); ms(ap("chi", 0, 1), 0)
    ms(ap("Ks", 0, 1), FAR)
    ms(ap("Kp", 0, 1), 0.0)
    PT = {}

    LAST = {"a": [], "b": []}

    def step(t, s, h, P, turn_):
        LAST[h] = []
        hi = "ab".index(h); win = NB + 128 * t; qr = YW * (2 * (t % 2) + hi)
        L = c4("l" + h, 4 * s - 4) if s else c4("HS", t * 136 + hi * 4)
        kids = ap("C", 64, 64 + (win if s else NB), ind=L) if t else ap("chi", 0, NB, ind=L)
        S = s68("sc" + h); D = s68("sc" + h, 68); W = (0, 68, 272)[s]
        cp(f64("ct" + h), kids)
        kv = KV[h][s]
        for k0, k1 in ((0, KW), (KW, kv)) if s and KW else ((0, kv),):
            cp(ap("kg" + h, 16 * k0, 16 * k1), ap("Ks", 0, win, ind=ap("ct" + h, k0, k1)))
        k1 = kv + (KS if s else 0)
        if k1 > kv: act(ap("kg" + h, 16 * kv, 16 * k1), ap("Ks", 0, win, ind=ap("ct" + h, kv, k1)), AF.Copy, after=turn_)
        act(ap("kg" + h, 16 * k1, 1024), ap("Ks", 0, win, ind=ap("ct" + h, k1, 64)), AF.Copy, after=turn_ + ([PT[h]] if s and PFIRST else []))
        ts(a3("cx" + h, 0, 4, 1, 0, 16, (0, 1)), f64("ct" + h), MID, EV, OP.subtract, OP.mult)
        ts(a3("cx" + h, 0, 4, 1, 16, 32, (1, 2)), f64("ct" + h), MID, OD, OP.subtract, OP.mult)
        if K32:
            turned = [(ap("sc" + h, 68 + 17 * c, 85 + 17 * c, p=q), a3("cx" + h, c, c + 1, 1, 0, 32, p=q), ap("dm", 0, 17, p=q),
                       False, c == 3) for q in ((0, 32), (32, 64), (64, 96), (96, 128)) for c in range(4)]
        else:
            turn(a3("tx" + h, 0, 4, 1, 1, 33), a3("cx" + h, 0, 4, 1, 0, 32))
            turned = [(D, ap("dm", 128 * k, 128 * k + 128), a3("tx" + h, 0, 4, 1, o, o + 17), False, k == 3) for k, o in enumerate((0, 1, 16, 17))]
        if h == "a" and s:
            if t and CF == "S": act(f64("cf", 64 * s - 64), kids, AF.Copy)
            else: cp(f64("cf", 64 * s - 64), f64("ct" + h))
        dd = mm([(D, ap("onq", 0, 128, p=1), ap("mrow", 0, 68, p=1), True, False)]
                + turned)
        mm([(S, ap("ones", 0, 128, p=2), ap("jrow", 0, 68, p=2), True, False)], after=[dd])
        for c, (m0, m1) in enumerate(CHUNKS):
            c0, c1 = 68 * m0, 68 * m1; pd = "pd%d" % c + h; n = 4 * (m1 - m0); d = a3(pd, 0, n, 1, 0, 17)
            dk = a3(pd, 0, n, 1, 1, 17); ex = a64("exn", 64 * m0, 64 * m1)
            pf = s > 0 and c >= PMM
            if pf: mm([(dk, P, ex, True, False)])
            mm([(a3(pd, b, n, 4, 1, 17), eye, ap("kg" + h, 256 * b + 16 * m0, 256 * b + 16 * m1), not pf and b == 0, pf and b == 3) for b in range(4)])
            if not pf: mm([(dk, P, ex, False, True)])
            y = size(ap("y" + h, c0, c1), d) if c == 2 and s in VABS else act(ap("y" + h, c0, c1), d, AF.Abs)
            if c == ALT[h][s]: LAST[h] = [y]
            mm([(S, ap("Wy", 15 - m, 143 - m), s68("y" + h, 68 * m), False, False) for m in range(m0, m1)])
            scan(ap("z" + h, c0, c1), ap("qr", qr + c0, qr + c1), ap("y" + h, c0, c1), OP.max, OP.min)
            mm([(S, ap("Wz", 15 - m, 143 - m), s68("z" + h, 68 * m), False, m == 15) for m in range(m0, m1)])
        ne = s68("ne" + h)
        scan(s68("f" + h), s68("d0", 136 * (t % 2) + 68 * hi), S, OP.max, OP.min)
        tt(ne, S, s68("f" + h), OP.not_equal)
        scan(s68("w" + h, W), ne, D, OP.mult, OP.add)
        cp(c4("l" + h, 4 * s), end("w" + h, W))
        if h == "a" and s < 2: act(ap("nbr", s, 128, 2), ap("iot", 0, win, ind=c4("la", 4 * s)), AF.Copy)
        if h == "a" and s:
            scan(s68("wa", 68 + 68 * s), ne, s68("dj"), OP.mult, OP.add)
            cp(c4("ju" if s == 1 else "ku"), end("wa", 68 + 68 * s))
        if h == "a" and s == 1: scan(s68("uw"), ne, s68("dw"), OP.mult, OP.add)

    def move(t, s, h, P, turn_):
        hi = "ab".index(h); win = NB + 128 * t; kk = ap("Kp", 0, win, ind=c4("l" + h, 4 * s))
        kq = ap("Ks", win + s, win + 128, 2) if h == "a" and s < 2 else f64("kq" + h)
        get = lambda: cp(kq, kk) if KQ[s] == "V" else act(kq, kk, AF.Copy, after=turn_)
        if t == NV - 1 and s == 2:
            o = a3("pd2" + h, 22, 26, 1, 1, 17, (4, 5)); Pn = f64("kq" + h, 64)
            mm([(o, P, a64("n64", 0, 64), True, False)]); get()
            mm([(o, eye, kq, False, True)])
        else:
            o = a3("pd2" + h, 22, 30, 1, 1, 17, (4, 5), 64); b = t * 256 + hi * 128
            Pn = a64("pt" + h, 128 * s, 128 * s + 128) if s < 2 else a64("PO", b, b + 128)
            mm([(o, a64("n64", 0, 64), P, True, False)]); get()
            mm([(o, kq, eye, False, True)])
        if Pn[0] == "PO": act(ap(*Pn[:3]), a3("pd2" + h, 22, 30, 1, 1, 17, (4, 5)), AF.Abs)
        else: PT[h] = act(Pn, o, AF.Abs, after=turn_)
        return Pn

    def slice_early(t):
        win = NB + 128 * t; ra = f64("cf")
        tt(c4("ca"), end("wa"), end("wa", 68), OP.not_equal)
        tt(c4("wc"), c4("ca"), end("uw"), OP.mult)
        for c in range(4):
            for w in range(2):
                o = 128 * (c + 4 * w); n = 68 * w + 17 * c + 16
                ts(ap("emat", o + 32 * c, o + 128), ap("nbr", 32 * c, 128), ap("wa", n, n + 1), None, OP.is_equal)
        tt(f64("an"), ap("tb", 0, 16, ind=c4("ju")), ra, OP.mult)
        tt(f64("oj1"), ap("tb", 16, 32, ind=c4("ju")), f64("mt", 64 * t), OP.mult)
        tt(f64("val"), f64("an"), f64("oj1"), OP.add)
        if t < NV - 1: gcp(ap("Kp", win, win + 128), ap("Ks", win, win + 128))

    def slice_late(t):
        win = 64 + NB + 128 * t; ra = f64("cf"); rb = f64("cf", 64)
        tt(ap("nd", 0, 16), ap("wa", 16, 272, 17), ap("dback", 0, 16), OP.subtract)
        for c in range(4):
            w = ap("wtf", c * 128, c * 128 + 128); n = 272 + 17 * c + 16; o = a3("pd0a", 2 * c, 8, 1, 1, 17)
            ts(w, ap("boB", 0, 128), ap("wa", n, n + 1), ap("wc", c, c + 1), OP.mult, OP.min)
            mm([(o, w, ap("emat", 160 * c, 128 * c + 128), c == 0, False), (a3("pd0a", 2 * c, 2 * c + 2, 1, 1, 17), w, ap("dg", 0, 32), False, False),
                (o, w, ap("emat", 512 + 160 * c, 512 + 128 * c + 128), False, c == 3)])
        tt(ap("good", 0, 128), a3("pd0a", 0, 8, 1, 1, 17), ap("thm", 0, 128), OP.is_lt)
        scan(ap("gd", 0, 128), ap("seg", 0, 128), ap("good", 0, 128), OP.max, OP.min)
        for c in range(4):
            ts(ap("tlu", c, 16, 4), ap("nd", c, 16, 4), ap("gd", 32 * c + 31, 32 * c + 32), ap("dump", c, c + 1), OP.mult, OP.add)
        tt(f64("val", 64), ap("tb", 0, 16, ind=c4("ku")), rb, OP.mult)
        if t == NV - 1: cp(ap("C", 64, 65), C0)
        for w in range(2): cp(ap("C", 0, win, ind=c4("tlu", 4 * w)), f64("val", 64 * w))
        tt(f64("au"), ap("tz", 0, 80, ind=c4("tlu", 8)), ra, OP.mult)
        tt(f64("oj"), ap("tz", 80, 160, ind=c4("tlu", 8)), ap("iot", win - 63, win + 64, 2), OP.mult)
        tt(ap("C", win, win + 128, 2), f64("au"), f64("oj"), OP.add)
        tt(ap("C", win + 1, win + 128, 2), ap("tz", 0, 80, ind=c4("tlu", 12)), rb, OP.mult)
        if t < NV - 1:
            act(c4("gh"), ap("gd", 31, 128, 32), AF.Copy)
            mm([(ap("sca", 256, 257), ap("half", 0, 128), ap("gh", c, c + 1), c == 0, c == 3) for c in range(4)])
            cp(ap("zu", 0, 1), ap("sca", 256, 257))
            act(ap("tc", 0, 16), ap("bnd", 0, 288, ind=ap("zu", 0, 1)), AF.Copy)

    def deal(t0, t1, sem, lag, after):
        def emit(g, T, core, topo):
            to = [T.cores[(T.rank_of(core) + t) % N] for t in range(t0, t1)]
            ids = [DstId(rid=topo.addr(c)[0], pnc=topo.addr(c)[1]) for c in to]
            e = shared(T, topo) if len(to) > 1 else topo.engines(core, to[0]); k = len(e) // 2
            g.remote_dma_fused([RemoteDMATransfer(dst_ids=ids, dma_engine_mask=sum(1 << x for x in e[w * k:w * k + k]), remote_sem=T.sem[sem], src=T[n][:, 0:128],
                                                  dsts=[T[n][:, 128 * t:128 * t + 128] for t in range(t0, t1)]) for w, n in enumerate(("QP", "HS"))], local_sem=T.sem["snd"])
        o = add("G", emit, (ap("QP", 0, 128), ap("HS", 0, 128), ap("Ks", 8, 16)), (), 2.0, n=0, done=("snd", 8), after=after)
        ops[o]["many"] = t1 - t0 > 1
        add("R", None, (), (ap("QP", 128 * t0, 128 * t1), ap("HS", 128 * t0, 128 * t1)), 0.0, n=0, done=(sem, t1 - t0), after=[o], lag=lag)
        return o
    numbers.append(deal(2, NV, "all", 20.0, [deal(1, 2, "one", 7.0, [])] + numbers[:2]))
    sent = []; before = numbers
    for t in range(NV):
        P = {}; tag[1] = t
        qr = 2 * YW * (t % 2)
        for hi in range(2):
            b = t * 256 + hi * 128; P["ab"[hi]] = a64("PS", b, b + 128)
        for j in range(1 if t > 1 else 0, 17):
            o = ap("qr", qr + j, qr + 2 * YW, 17); q = ap("QP", t * 128, t * 128 + 128)
            if t: gcp(o, q, before)
            else: act(o, q, AF.Copy)
        if t: before = sent
        d0 = 136 * (t % 2)
        ts(ap("d0", d0 + 1, d0 + 136, 17), ap("HS", t * 128 + 64, t * 128 + 72), -1.0, ap("tc", 0, 1), OP.mult, OP.add)
        for h, s in TURNS:
            tag[0] = s; turn_ = LAST["ba"["ab".index(h)]]
            if s: P[h] = move(t, s - 1, h, P[h], turn_)
            step(t, s, h, P[h], turn_); tag[0] = None
        slice_early(t)
        for h in "ab": P[h] = move(t, 2, h, P[h], [])
        if t == 0:
            for i in range(8): cp(ap("C", 64 + i * 320, 384 + i * 320), ap("chi", i * 320, 320 + i * 320))
        on = []
        for hi in range(2):
            b = t * 256 + hi * 128; sem = "a%s%d" % ("ab"[hi], t + 1)
            if t < NV - 1: on.append((ap("PS", b + 256, b + 384), sem, ap("PO", b, b + 128)))
            else: on.append((f64("PF", 64 * hi), sem, P["ab"[hi]]))
        sent = [send(o, a, sem) for o, sem, a in on]
        slice_late(t)
        for k in range(2): recv(on[k][0], on[k][1], sent[k])
    for i, (c0, c1) in enumerate(((0, 1152), (1152, 2304), (2304, 3456), (3456, NW))): dma(ap("yc", c0, c1), ap("C", 64 + c0, 64 + c1), "st%d" % i, STORE if i < 3 else 2.5)
    for hi in range(2): dma(f64("yp", 64 * hi), f64("PF", 64 * hi), "sp" + "ab"[hi], 2)
    return ops


def plan(ops):
    hist = {}; runs = {}; m = len(ops)
    for o in ops:
        dep = {}
        for x in o["rd"]:
            for (q, w, y) in hist.get(x[0], ()):
                if w and meet(x[1:], y): dep[q] = "raw"
        for x in o["wr"]:
            for (q, w, y) in hist.get(x[0], ()):
                if meet(x[1:], y): dep.setdefault(q, "waw" if w else "war")
        for q in o["after"]: dep.setdefault(q, "ord")
        for n in {x[0] for x in o["rd"] + o["wr"]} & PSUM:
            r = runs.setdefault(n, [])
            if not r or r[-1][0] != o["eng"]: r.append((o["eng"], []))
            if len(r) > 1:
                for q in r[-2][1]: dep.setdefault(q, "bank")
            r[-1][1].append(o["i"])
        dep.pop(o["i"], None)
        o["dep"] = dep
        for (n, lo, hi, st) in o["wr"]:
            old = hist.setdefault(n, [])
            old[:] = [e for e in old if not (lo <= e[2][0] and e[2][1] <= hi and (st == 1 or e[2] == (lo, hi, st)))] + [(o["i"], True, (lo, hi, st))]
        for x in o["rd"]: hist.setdefault(x[0], []).append((o["i"], False, x[1:]))
    succ = [[] for _ in ops]; left = [len(o["dep"]) for o in ops]; pri = [0.0] * m
    def free_of_wait(p, o):
        kind = o["dep"][p["i"]]
        return p["eng"] == o["eng"] != "Y" and (kind in NOWAIT or (o["eng"] == "P" and kind == "waw"))
    for o in ops:
        for q in o["dep"]: succ[q].append(o["i"])
    for o in reversed(ops): pri[o["i"]] = o["cost"] + o["lag"] + LAT + max([pri[x] for x in succ[o["i"]]] or [0.0])
    for o in ops: pri[o["i"]] += BIAS.get((o["eng"], (o["wr"] + o["rd"])[0][0], o["tag"]), 0.0)
    order = {e: [] for e in "VSPGYR"}; free = {e: 0.0 for e in order}
    ready = {i for i in range(m) if left[i] == 0}; est = [0.0] * m; fin = [0.0] * m
    while ready:
        best = None
        for e in free:
            cand = [i for i in ready if e == ops[i]["eng"]]
            if not cand: continue
            now = [i for i in cand if est[i] <= free[e]]
            i = max(now, key=lambda x: (pri[x], -x)) if now else min(cand, key=lambda x: (est[x], -pri[x], x))
            t0 = max(free[e], est[i])
            soon = [x for x in cand if t0 < est[x] < t0 + AHEAD * ops[i]["cost"] and pri[x] - pri[i] > URGENT * (est[x] - t0 + ops[x]["cost"])]
            if soon: i = max(soon, key=lambda x: (pri[x], -x))
            st = max(free[e], est[i])
            if best is None or (st, -pri[i]) < best[0]: best = ((st, -pri[i]), st, e, i)
        _, st, e, i = best
        ready.discard(i); ops[i]["st"] = st; order[e].append(i)
        free[e] = st + ops[i]["cost"] if e != "R" else 0.0
        fin[i] = st + ops[i]["cost"] + ops[i]["lag"]
        for x in succ[i]:
            est[x] = max(est[x], fin[i] + (0.0 if free_of_wait(ops[i], ops[x]) else LAT)); left[x] -= 1
            if left[x] == 0: ready.add(x)
    gap = lambda q, x: ops[q]["lag"] + (0.0 if free_of_wait(ops[q], ops[x]) else LAT)
    back = [[(x, gap(o["i"], x)) for x in succ[o["i"]]] for o in ops]; fore = [[(q, gap(q, o["i"])) for q in o["dep"]] for o in ops]
    def pack(seq, before, head):
        end = [0.0] * m; busy = {e: [] for e in order}
        for i in seq:
            c = ops[i]["cost"]; t = max([end[q] + d for q, d in before[i]] + [head[i]]); b = busy[ops[i]["eng"]]
            if c:
                k = len(b)
                while k and b[k - 1][1] > t: k -= 1
                while k < len(b) and b[k][0] < t + c: t = max(t, b[k][1]); k += 1
                b.insert(k, (t, t + c))
            end[i] = t + c
        return end
    span = lambda end: max(end[i] + ops[i]["lag"] for i in range(m))
    end = [fin[i] - ops[i]["lag"] for i in range(m)]; top = end
    for _ in range(ROUNDS):
        r = pack(sorted(range(m), key=lambda i: (-end[i] - ops[i]["lag"], -i)), back, [o["lag"] for o in ops])
        end = pack(sorted(range(m), key=lambda i: (-r[i], i)), fore, [0.0] * m)
        if span(end) < span(top): top = end
    for o in ops: o["st"] = top[o["i"]] - o["cost"]; fin[o["i"]] = top[o["i"]] + o["lag"]
    for e in order: order[e].sort(key=lambda i: (ops[i]["st"], i))
    cnt = {e: 0 for e in order}
    for e in order:
        for i in order[e]:
            if ops[i]["done"] is None:
                cnt[e] += ops[i]["n"]; ops[i]["tgt"] = (NAME[e], cnt[e])
            else: ops[i]["tgt"] = ops[i]["done"]
    known = {e: {} for e in order}; at = {}; ptr = {e: 0 for e in order}; waits = {}
    while len(at) < m:
        for e in order:
            while ptr[e] < len(order[e]):
                i = order[e][ptr[e]]; o = ops[i]
                if any(q not in at for q in o["dep"]): break
                w = []
                for q in sorted(o["dep"], key=lambda q: -fin[q]):
                    p = ops[q]
                    if e == "R" or p["done"] == ("snd", 8) or free_of_wait(p, o): continue
                    s, v = p["tgt"]
                    if known[e].get(s, 0) >= v: continue
                    w.append((s, v))
                    for s2, v2 in list(at[q].items()) + [(s, v)]:
                        if known[e].get(s2, 0) < v2: known[e][s2] = v2
                waits[i] = [x for x in w if not any(y[0] == x[0] and y[1] > x[1] for y in w)]
                at[i] = dict(known[e]); ptr[e] += 1
    return order, waits, cnt, max(fin)


NAME = {"V": "v", "S": "s", "P": "pe", "G": "gp"}
MEMO = {}


def rank_program(g, core, T, topo):
    if T.rank_of(core) is None: return
    if "p" not in MEMO:
        MEMO["o"] = build(); MEMO["p"] = plan(MEMO["o"])
    ops = MEMO["o"]; order, waits, cnt, _ = MEMO["p"]
    queue = {"V": g.vector, "S": g.scalar, "P": g.tensor, "G": g, "Y": g.sync}
    sent = 0; me = T.rank_of(core); every = len(shared(T, topo))
    into = len(topo.engines(T.cores[(me - 1) % N], core)); out = len(topo.engines(core, T.cores[(me + 1) % N]))
    for e in "YVSPG":
        for i in order[e]:
            o = ops[i]
            for s, v in waits[i]: queue[e].wait_ge(T.sem[s], into if s in ARRIVE else v * every if s == "all" else v)
            if o["done"] == ("snd", 8):
                o["emit"](g, T, core, topo); sent += every if o.get("many") else out
            elif o["done"]: o["emit"](g, T).then_inc(T.sem[o["done"][0]], 16)
            else:
                r = o["emit"](g, T)
                for x in (r if isinstance(r, list) else [r]): x.then_inc(T.sem[NAME[e]], 1)
    for e in "VSPG": g.wait_ge(T.sem[NAME[e]], cnt[e])
    for s in DMAS: g.wait_ge(T.sem[s], 16)
    g.wait_ge(T.sem["snd"], sent)
